import numpy as np
import ml_dtypes


def mxq(x, axis, fmt="e4m3"):
    dtype, down = {"e4m3": (ml_dtypes.float8_e4m3fn, 7), "e5m2": (ml_dtypes.float8_e5m2, 14)}[fmt]
    v = np.moveaxis(np.asarray(x, np.float32).astype(ml_dtypes.bfloat16).astype(np.float64), axis, -1)
    blocks = v.reshape(v.shape[:-1] + (-1, 32))
    amax = np.abs(blocks).max(-1, keepdims=True)
    byte = np.maximum(np.where(amax > 0, np.frexp(amax)[1] - 1 + 127, 0) - down, 1)
    scale = np.exp2(byte - 127.0)
    codes = (blocks / scale).astype(np.float32).astype(dtype).astype(np.float64)
    return np.moveaxis((codes * scale).reshape(v.shape), -1, axis)


WIDE = False


def mx_kscale(k):
    if not WIDE:
        return np.ones(k)
    levels = np.array([10, -10, 5, -5, 0])
    if k % 512:
        return np.exp2(np.random.permutation(np.resize(levels, k // 32))).repeat(32)
    a = np.empty((k // 512, 16))
    for p in range(k // 512):
        a[p, :8] = np.random.permutation(np.resize(levels, 8))
        for g in range(8):
            far = levels[np.abs(levels - a[p, g]) >= 10]
            a[p, g + 8] = far[np.random.randint(len(far))]
    return np.exp2(a.ravel()).repeat(32)


def f64(x):
    return np.asarray(x).astype(np.float64)


def striped(idx):
    return np.tile(idx.reshape(-1, 16).T, (8, 1)).astype(np.uint16)


def unstriped(offs):
    return offs[:16].T.reshape(-1).astype(np.int64)


E2M1 = np.array([0.0, 0.5, 1.0, 1.5, 2.0, 3.0, 4.0, 6.0, -0.0, -0.5, -1.0, -1.5, -2.0, -3.0, -4.0, -6.0])


def pack_weight(w, fmt):
    k, n = w.shape
    w = f64(np.asarray(w, np.float32).astype(ml_dtypes.bfloat16)).reshape(k // 32, 32, n)
    amax = np.abs(w).max(1)
    if fmt == "e4m3":
        byte = np.frexp(amax)[1] - 1 + 127 - 7
    else:
        mant, ex = np.frexp(amax / 6.0)
        byte = np.where(mant > 0.5, ex, ex - 1) + 127
    byte = np.clip(np.where(amax > 0, byte, 1), 1, 254)
    scaled = (w * np.exp2(127.0 - byte)[:, None, :]).reshape(k, n).astype(np.float32)
    by_word = np.ascontiguousarray(scaled.reshape(k // 512, 128, 4, n).transpose(0, 1, 3, 2))
    if fmt == "e4m3":
        words = by_word.astype(ml_dtypes.float8_e4m3fn).view(np.uint8)
    else:
        c = by_word.astype(ml_dtypes.float4_e2m1fn).view(np.uint8) & 0xF
        words = (c[..., 0::2] | (c[..., 1::2] << 4)).reshape(k // 512, 128, 2 * n)
    return np.ascontiguousarray(words), np.ascontiguousarray(byte.astype(np.uint8).reshape(k // 512, 16, n))


def unpack_weight(words, scales, fmt):
    g, _, n = scales.shape
    words = np.ascontiguousarray(words).reshape(g, 128, n, -1)
    if fmt == "e4m3":
        vals = words.view(ml_dtypes.float8_e4m3fn).astype(np.float64)
    else:
        nib = np.empty((g, 128, n, 4), np.uint8)
        nib[..., 0::2] = words & 0xF
        nib[..., 1::2] = words >> 4
        vals = E2M1[nib]
    vals = vals * np.repeat(np.exp2(scales.astype(np.float64) - 127.0), 8, axis=1)[..., None]
    return vals.transpose(0, 1, 3, 2).reshape(g * 512, n)


def gelu(v):
    return 0.5 * v * (1.0 + np.tanh(np.sqrt(2.0 / np.pi) * (v + 0.044715 * v**3)))


K, H, T, S, P = 1536, 1024, 4096, 1024, 512

def setup_inputs():
    n = np.random.standard_normal
    s = mx_kscale(K)[:, None]
    u = mx_kscale(H)[:, None]
    tab_words, tab_scales = pack_weight(n((K, T)) * s, "e4m3")
    w1 = n((K, H)) / np.sqrt(K) / s
    w2_words, w2_scales = pack_weight(0.6 * n((H, H)) / np.sqrt(H) / u, "e2m1")
    gain = np.exp(0.3 * n(H)) * u[:, 0]
    return {
        "tab_words": tab_words, "tab_scales": tab_scales,
        "offs": striped(np.random.permutation(T)[:S]),
        "w1": w1.astype(np.float32),
        "pos1": striped(np.random.permutation(S)[:P]),
        "pos2": striped(np.random.permutation(S)[:P]),
        "gain": gain.astype(np.float32),
        "w2_words": w2_words, "w2_scales": w2_scales,
    }

def reference(tab_words, tab_scales, offs, w1, pos1, pos2, gain, w2_words, w2_scales):
    v = unpack_weight(tab_words, tab_scales, "e4m3")[:, unstriped(offs)]
    h = mxq(f64(w1), 0, "e4m3").T @ v
    x = h[:, unstriped(pos1)]
    a = x * (1.0 / (1.0 + np.exp(-x)))
    z = np.square(a) * f64(gain)[:, None]
    w2 = unpack_weight(w2_words, w2_scales, "e2m1")
    y = w2.T @ mxq(z, 0, "e4m3")
    return h[:, unstriped(pos2)] * (1.0 + y)

@@ -1,0 +1,186 @@
+from contextlib import ExitStack
+
+import concourse.mybir as mybir
+
+K, H, T, S, M = 1536, 1024, 4096, 1024, 512
+FLOPS = 2 * K * H * S + 2 * H * H * M
+
+F32 = mybir.dt.float32
+BF16 = mybir.dt.bfloat16
+I32 = mybir.dt.int32
+U32 = mybir.dt.uint32
+U16 = mybir.dt.uint16
+U8 = mybir.dt.uint8
+FP8X4 = mybir.dt.float8_e4m3fn_x4
+FP4X4 = mybir.dt.float4_e2m1fn_x4
+ACT = mybir.ActivationFunctionType
+ALU = mybir.AluOpType
+
+P = 128
+PACK = 4
+K_PASS = P * PACK
+BANK = 512
+PASSES1 = K // K_PASS
+PASSES2 = H // K_PASS
+V_SHARE = 84
+
+
+def tile_list_ant_trail_residual_kernel(tc, tab_words, tab_scales, offs, w1, pos1, pos2, gain, w2_words, w2_scales, out):
+    nc = tc.nc
+    with ExitStack() as ctx:
+        keep = ctx.enter_context(tc.tile_pool(name="keep", bufs=1))
+        raws = ctx.enter_context(tc.tile_pool(name="raws", bufs=4))
+        ring = ctx.enter_context(tc.tile_pool(name="ring", bufs=3))
+        psum = ctx.enter_context(tc.psum_pool(name="psum", bufs=1))
+
+        offs_t = keep.tile([P, S // 16], U16, name="offs_t")
+        pos1_t = keep.tile([P, M // 16], U16, name="pos1_t")
+        pos2_t = keep.tile([P, M // 16], U16, name="pos2_t")
+        tab = [keep.tile([P, T], U32, name="tab%d" % a, align_bytes=64) for a in range(PASSES1)]
+        tab_sc = keep.tile([P, T], U8, name="tab_sc", align_bytes=64)
+        w2_raw = keep.tile([P, PASSES2, H // 2], I32, name="w2_raw", align_bytes=64)
+        w2_sc_raw = keep.tile([P, PASSES2, H], U8, name="w2_sc_raw", align_bytes=64)
+        gain_t = keep.tile([P, PASSES2, PACK], F32, name="gain_t")
+
+        nc.vector.memset(tab_sc[:].bitcast(I32), 0)
+        nc.vector.memset(w2_sc_raw[:].bitcast(I32), 0)
+        warm = keep.tile([P, 8], F32, name="warm")
+        nc.vector.memset(warm[:], 0.0)
+        nc.scalar.activation(out=warm[:], in_=warm[:], func=ACT.Silu)
+
+        raw = {}
+
+        def load_tab(a):
+            nc.sync.dma_start(out=tab[a][:].bitcast(I32), in_=tab_words[a].rearrange("p t i -> p (t i)").bitcast(I32))
+
+        def load_w1(b, a):
+            raw[b, a] = raws.tile([P, PACK, K_PASS], F32, name="raw")
+            nc.sync.dma_start(out=raw[b, a][:], in_=w1[a * K_PASS : (a + 1) * K_PASS, b * K_PASS : (b + 1) * K_PASS].rearrange("(p j) c -> p j c", j=PACK))
+
+        load_tab(0)
+        nc.sync.dma_start(offs_t[:], offs)
+        for q in range(4):
+            nc.sync.dma_start(out=tab_sc[32 * q : 32 * q + 4 * PASSES1, :].bitcast(I32), in_=tab_scales[:, 4 * q : 4 * q + 4, :].bitcast(I32))
+        load_w1(0, 0)
+        load_tab(1)
+        for q in range(4):
+            nc.sync.dma_start(out=w2_sc_raw[32 * q : 32 * q + 4, :, :].bitcast(I32), in_=w2_scales[:, 4 * q : 4 * q + 4, :].rearrange("a r n -> r a n").bitcast(I32))
+        load_w1(0, 1)
+        load_tab(2)
+        nc.sync.dma_start(pos1_t[:], pos1)
+        nc.sync.dma_start(pos2_t[:], pos2)
+        nc.sync.dma_start(out=gain_t[:], in_=gain.rearrange("(b p t) -> p b t", p=P, t=PACK))
+        load_w1(0, 2)
+        nc.sync.dma_start(out=w2_raw[:], in_=w2_words.rearrange("a p n -> p a n").bitcast(I32))
+
+        v_words = [keep.tile([P, S], U32, name="v_words%d" % a, align_bytes=64) for a in range(PASSES1)]
+        v_sc = keep.tile([P, S], U8, name="v_sc", align_bytes=64)
+        w2_w = keep.tile([P, PASSES2, 2 * H], U8, name="w2_w", align_bytes=64)
+        w2_sc = keep.tile([P, PASSES2, H], U8, name="w2_sc", align_bytes=64)
+
+        w_codes, w_sc, banks, h, z_codes, z_sc, picked2 = {}, {}, {}, {}, {}, {}, {}
+
+        def quantise_w1(b, a, split):
+            rounded = ring.tile([P, PACK * K_PASS], BF16, name="rounded", align_bytes=64)
+            src = raw[b, a][:].rearrange("p j (m t) -> p m j t", t=PACK)
+            dst = rounded[:].rearrange("p (t m j) -> p m j t", t=PACK, j=PACK)
+            w_codes[b, a] = keep.tile([P, K_PASS], U32, name="w_codes%d%d" % (b, a), align_bytes=64)
+            w_sc[b, a] = keep.tile([P, K_PASS], U8, name="w_sc%d%d" % (b, a), align_bytes=64)
+            if split:
+                nc.vector.tensor_copy(out=dst[:, :V_SHARE], in_=src[:, :V_SHARE])
+                nc.scalar.copy(out=dst[:, V_SHARE:], in_=src[:, V_SHARE:])
+                for t in range(PACK):
+                    nc.vector.quantize_mx(out=w_codes[b, a][:, t * P : (t + 1) * P].bitcast(FP8X4), scales=w_sc[b, a][:, t * P : (t + 1) * P], in_=rounded[:, t * K_PASS : (t + 1) * K_PASS])
+            else:
+                nc.scalar.copy(out=dst, in_=src)
+                nc.vector.quantize_mx(out=w_codes[b, a][:].bitcast(FP8X4), scales=w_sc[b, a][:], in_=rounded[:])
+
+        def first_passes(b, a):
+            for t in range(PACK):
+                for half in range(2):
+                    if a == 0:
+                        banks[b, t, half] = psum.tile([P, BANK], F32, name="bank%d" % (2 * t + half))
+                    cols = slice(half * BANK, (half + 1) * BANK)
+                    nc.tensor.matmul_mx(
+                        out=banks[b, t, half][:],
+                        lhsT=w_codes[b, a][:, t * P : (t + 1) * P].bitcast(FP8X4),
+                        lhsT_scale=w_sc[b, a][:, t * P : (t + 1) * P],
+                        rhs=v_words[a][:, cols].bitcast(FP8X4),
+                        rhs_scale=v_sc[4 * a : P, cols],
+                        start=(a == 0),
+                        stop=(a == PASSES1 - 1),
+                    )
+
+        def make_z(b):
+            x = keep.tile([P, PACK, M], F32, name="x%d" % b)
+            for t in range(PACK):
+                h[b, t] = keep.tile([P, S], F32, name="h%d%d" % (b, t))
+                for half in range(2):
+                    nc.scalar.copy(out=h[b, t][:, half * BANK : (half + 1) * BANK], in_=banks[b, t, half][:])
+                nc.vector.tensor_copy(out=x[:, t, :], in_=h[b, t][:].indirect(pos1_t[:]))
+            return x
+
+        def finish_z(b, x):
+            for t in range(PACK):
+                nc.scalar.activation(out=x[:, t, :], in_=x[:, t, :], func=ACT.Silu)
+                nc.scalar.activation(out=x[:, t, :], in_=x[:, t, :], func=ACT.Square)
+            z = ring.tile([P, PACK * M], BF16, name="rounded", align_bytes=64)
+            nc.vector.tensor_tensor(
+                out=z[:].rearrange("p (c i t) -> p c t i", i=4, t=PACK),
+                in0=x[:].rearrange("p t (c i) -> p c t i", i=4),
+                in1=gain_t[:, b, :].unsqueeze(1).unsqueeze(3).to_broadcast([P, M // 4, PACK, 4]),
+                op=ALU.mult,
+            )
+            z_codes[b] = keep.tile([P, M], U32, name="z_codes%d" % b, align_bytes=64)
+            z_sc[b] = keep.tile([P, M], U8, name="z_sc%d" % b, align_bytes=64)
+            nc.vector.quantize_mx(out=z_codes[b][:].bitcast(FP8X4), scales=z_sc[b][:], in_=z[:])
+
+        def pick2(b):
+            for t in range(PACK):
+                picked2[b, t] = keep.tile([P, M], F32, name="picked%d%d" % (b, t))
+                nc.vector.tensor_copy(out=picked2[b, t][:], in_=h[b, t][:].indirect(pos2_t[:]))
+
+        nc.vector.tensor_copy(out=w2_sc[:].rearrange("p a (b t m) -> p (a b) m t", t=PACK, m=P), in_=w2_sc_raw[:].rearrange("p a (b m t) -> p (a b) m t", t=PACK, m=P))
+        nc.vector.tensor_copy(out=v_sc[:], in_=tab_sc[:].indirect(offs_t[:]))
+        for a in range(PASSES1):
+            nc.vector.tensor_copy(out=v_words[a][:], in_=tab[a][:].indirect(offs_t[:]))
+            quantise_w1(0, a, a == PASSES1 - 1)
+            first_passes(0, a)
+        nc.vector.tensor_copy(
+            out=w2_w[:].bitcast(U16).rearrange("p a (b t m) -> p (a b) m t", t=PACK, m=P),
+            in_=w2_raw[:].bitcast(U16).rearrange("p a (b m t) -> p (a b) m t", t=PACK, m=P),
+        )
+        for a in range(PASSES1):
+            load_w1(1, a)
+        x0 = make_z(0)
+        for a in range(PASSES1):
+            quantise_w1(1, a, False)
+            first_passes(1, a)
+        x1 = make_z(1)
+        finish_z(0, x0)
+        finish_z(1, x1)
+        pick2(0)
+        pick2(1)
+
+        out_rows = out.rearrange("(b p t) m -> b t p m", p=P, t=PACK)
+        y = {}
+        for a in range(PASSES2):
+            for b in range(PASSES2):
+                for t in range(PACK):
+                    if a == 0:
+                        y[b, t] = psum.tile([P, BANK], F32, name="bank%d" % (PACK * b + t))
+                    c0 = b * K_PASS + t * P
+                    nc.tensor.matmul_mx(
+                        out=y[b, t][:],
+                        lhsT=w2_w[:, a, 2 * c0 : 2 * (c0 + P)].bitcast(FP4X4),
+                        lhsT_scale=w2_sc[:, a, c0 : c0 + P],
+                        rhs=z_codes[a][:].bitcast(FP8X4),
+                        rhs_scale=z_sc[a][:],
+                        start=(a == 0),
+                        stop=(a == PASSES2 - 1),
+                    )
+        for b in range(PASSES2):
+            for t in range(PACK):
+                result = ring.tile([P, M], F32, name="result")
+                nc.vector.scalar_tensor_tensor(out=result[:], in0=y[b, t][:], scalar=1.0, in1=picked2[b, t][:], op0=ALU.add, op1=ALU.mult)
+                nc.sync.dma_start(out=out_rows[b, t], in_=result[:])

@@ -30,7 +30,6 @@ def tile_list_ant_trail_residual_kernel(tc, tab_words, tab_scales, offs, w1, pos
     with ExitStack() as ctx:
         keep = ctx.enter_context(tc.tile_pool(name="keep", bufs=1))
         raws = ctx.enter_context(tc.tile_pool(name="raws", bufs=4))
-        ring = ctx.enter_context(tc.tile_pool(name="ring", bufs=3))
         psum = ctx.enter_context(tc.psum_pool(name="psum", bufs=1))
 
         offs_t = keep.tile([P, S // 16], U16, name="offs_t")
@@ -80,23 +79,27 @@ def tile_list_ant_trail_residual_kernel(tc, tab_words, tab_scales, offs, w1, pos
 
         w_codes, w_sc, banks, h, z_codes, z_sc, picked2 = {}, {}, {}, {}, {}, {}, {}
 
-        def quantise_w1(b, a, split):
-            rounded = ring.tile([P, PACK * K_PASS], BF16, name="rounded", align_bytes=64)
+        def quantise_w1(b, a, how):
+            rounded = keep.tile([P, PACK * K_PASS], BF16, name="rounded", tag="stage%d" % a, align_bytes=64)
             src = raw[b, a][:].rearrange("p j (m t) -> p m j t", t=PACK)
             dst = rounded[:].rearrange("p (t m j) -> p m j t", t=PACK, j=PACK)
             w_codes[b, a] = keep.tile([P, K_PASS], U32, name="w_codes%d%d" % (b, a), align_bytes=64)
             w_sc[b, a] = keep.tile([P, K_PASS], U8, name="w_sc%d%d" % (b, a), align_bytes=64)
-            if split:
+            if how == "split":
                 nc.vector.tensor_copy(out=dst[:, :V_SHARE], in_=src[:, :V_SHARE])
                 nc.scalar.copy(out=dst[:, V_SHARE:], in_=src[:, V_SHARE:])
                 for t in range(PACK):
                     nc.vector.quantize_mx(out=w_codes[b, a][:, t * P : (t + 1) * P].bitcast(FP8X4), scales=w_sc[b, a][:, t * P : (t + 1) * P], in_=rounded[:, t * K_PASS : (t + 1) * K_PASS])
             else:
-                nc.scalar.copy(out=dst, in_=src)
+                if how == "vector":
+                    nc.vector.tensor_copy(out=dst, in_=src)
+                else:
+                    nc.scalar.copy(out=dst, in_=src)
                 nc.vector.quantize_mx(out=w_codes[b, a][:].bitcast(FP8X4), scales=w_sc[b, a][:], in_=rounded[:])
 
-        def first_passes(b, a):
+        def first_passes(b):
             for t in range(PACK):
+              for a in range(PASSES1):
                 for half in range(2):
                     if a == 0:
                         banks[b, t, half] = psum.tile([P, BANK], F32, name="bank%d" % (2 * t + half))
@@ -112,7 +115,7 @@ def tile_list_ant_trail_residual_kernel(tc, tab_words, tab_scales, offs, w1, pos
                     )
 
         def make_z(b):
-            x = keep.tile([P, PACK, M], F32, name="x%d" % b)
+            x = keep.tile([P, PACK, M], F32, name="x", tag="x%d" % b, align_bytes=64)
             for t in range(PACK):
                 h[b, t] = keep.tile([P, S], F32, name="h%d%d" % (b, t))
                 for half in range(2):
@@ -123,44 +126,50 @@ def tile_list_ant_trail_residual_kernel(tc, tab_words, tab_scales, offs, w1, pos
         def finish_z(b, x):
             for t in range(PACK):
                 nc.scalar.activation(out=x[:, t, :], in_=x[:, t, :], func=ACT.Silu)
-                nc.scalar.activation(out=x[:, t, :], in_=x[:, t, :], func=ACT.Square)
-            z = ring.tile([P, PACK * M], BF16, name="rounded", align_bytes=64)
-            nc.vector.tensor_tensor(
-                out=z[:].rearrange("p (c i t) -> p c t i", i=4, t=PACK),
-                in0=x[:].rearrange("p t (c i) -> p c t i", i=4),
-                in1=gain_t[:, b, :].unsqueeze(1).unsqueeze(3).to_broadcast([P, M // 4, PACK, 4]),
-                op=ALU.mult,
-            )
+            squares = keep.tile([P, M, PACK], F32, name="squares", tag="squares%d" % b, align_bytes=64)
+            z = keep.tile([P, M, PACK], BF16, name="z", tag="z%d" % b, align_bytes=64)
+            for half in range(2):
+                cols = slice(half * M // 2, (half + 1) * M // 2)
+                nc.scalar.activation(
+                    out=squares[:, cols, :].rearrange("p (c i) t -> p c t i", i=4),
+                    in_=x[:, :, cols].rearrange("p t (c i) -> p c t i", i=4),
+                    func=ACT.Square,
+                )
+                nc.vector.tensor_tensor(out=z[:, cols, :], in0=squares[:, cols, :], in1=gain_t[:, b, :].unsqueeze(1).to_broadcast([P, M // 2, PACK]), op=ALU.mult)
             z_codes[b] = keep.tile([P, M], U32, name="z_codes%d" % b, align_bytes=64)
             z_sc[b] = keep.tile([P, M], U8, name="z_sc%d" % b, align_bytes=64)
-            nc.vector.quantize_mx(out=z_codes[b][:].bitcast(FP8X4), scales=z_sc[b][:], in_=z[:])
+            nc.vector.quantize_mx(out=z_codes[b][:].bitcast(FP8X4), scales=z_sc[b][:], in_=z[:].rearrange("p m t -> p (m t)"))
 
-        def pick2(b):
-            for t in range(PACK):
-                picked2[b, t] = keep.tile([P, M], F32, name="picked%d%d" % (b, t))
-                nc.vector.tensor_copy(out=picked2[b, t][:], in_=h[b, t][:].indirect(pos2_t[:]))
+        def pick2(tag, tiles, align):
+            group = keep.tile([P, len(tiles), M], F32, name="picked", tag=tag, align_bytes=align)
+            for i, (b, t) in enumerate(tiles):
+                picked2[b, t] = group[:, i, :]
+                nc.vector.tensor_copy(out=picked2[b, t], in_=h[b, t][:].indirect(pos2_t[:]))
 
         nc.vector.tensor_copy(out=w2_sc[:].rearrange("p a (b t m) -> p (a b) m t", t=PACK, m=P), in_=w2_sc_raw[:].rearrange("p a (b m t) -> p (a b) m t", t=PACK, m=P))
         nc.vector.tensor_copy(out=v_sc[:], in_=tab_sc[:].indirect(offs_t[:]))
         for a in range(PASSES1):
             nc.vector.tensor_copy(out=v_words[a][:], in_=tab[a][:].indirect(offs_t[:]))
-            quantise_w1(0, a, a == PASSES1 - 1)
-            first_passes(0, a)
+            quantise_w1(0, a, "split" if a == PASSES1 - 1 else "scalar")
+        first_passes(0)
         nc.vector.tensor_copy(
             out=w2_w[:].bitcast(U16).rearrange("p a (b t m) -> p (a b) m t", t=PACK, m=P),
             in_=w2_raw[:].bitcast(U16).rearrange("p a (b m t) -> p (a b) m t", t=PACK, m=P),
         )
         for a in range(PASSES1):
             load_w1(1, a)
-        x0 = make_z(0)
         for a in range(PASSES1):
-            quantise_w1(1, a, False)
-            first_passes(1, a)
+            quantise_w1(1, a, "scalar" if a == 1 else "split")
+        x0 = make_z(0)
+        first_passes(1)
         x1 = make_z(1)
         finish_z(0, x0)
         finish_z(1, x1)
-        pick2(0)
-        pick2(1)
+        pick2("stage1", [(0, 0), (0, 1)], 64)
+        pick2("stage2", [(0, 2), (0, 3)], 64)
+        pick2("squares0", [(1, 0), (1, 1)], 64)
+        pick2("z1", [(1, 2)], 64)
+        pick2("squares1", [(1, 3)], 64)
 
         out_rows = out.rearrange("(b p t) m -> b t p m", p=P, t=PACK)
         y = {}
@@ -181,6 +190,6 @@ def tile_list_ant_trail_residual_kernel(tc, tab_words, tab_scales, offs, w1, pos
                     )
         for b in range(PASSES2):
             for t in range(PACK):
-                result = ring.tile([P, M], F32, name="result")
-                nc.vector.scalar_tensor_tensor(out=result[:], in0=y[b, t][:], scalar=1.0, in1=picked2[b, t][:], op0=ALU.add, op1=ALU.mult)
+                result = keep.tile([P, M], F32, name="result%d%d" % (b, t))
+                nc.vector.scalar_tensor_tensor(out=result[:], in0=y[b, t][:], scalar=1.0, in1=picked2[b, t], op0=ALU.add, op1=ALU.mult)
                 nc.sync.dma_start(out=out_rows[b, t], in_=result[:])

@@ -22,7 +22,6 @@ K_PASS = P * PACK
 BANK = 512
 PASSES1 = K // K_PASS
 PASSES2 = H // K_PASS
-V_SHARE = 84
 
 
 def tile_list_ant_trail_residual_kernel(tc, tab_words, tab_scales, offs, w1, pos1, pos2, gain, w2_words, w2_scales, out):
@@ -43,6 +42,13 @@ def tile_list_ant_trail_residual_kernel(tc, tab_words, tab_scales, offs, w1, pos
 
         nc.vector.memset(tab_sc[:].bitcast(I32), 0)
         nc.vector.memset(w2_sc_raw[:].bitcast(I32), 0)
+        v_rows = keep.tile([P, S], U8, name="v_rows", align_bytes=64)
+        v_sc = [keep.tile([P, S], U8, name="v_sc%d" % a, align_bytes=64) for a in range(PASSES1)]
+        w2_rows = keep.tile([P, PASSES2, H], U8, name="w2_rows", align_bytes=64)
+        w2_sc = keep.tile([P, PASSES2, H], U8, name="w2_sc", align_bytes=64)
+        for a in range(PASSES1):
+            nc.vector.memset(v_sc[a][:].bitcast(I32), 0)
+        nc.vector.memset(w2_sc[:].bitcast(I32), 0)
         warm = keep.tile([P, 8], F32, name="warm")
         nc.vector.memset(warm[:], 0.0)
         nc.scalar.activation(out=warm[:], in_=warm[:], func=ACT.Silu)
@@ -56,26 +62,32 @@ def tile_list_ant_trail_residual_kernel(tc, tab_words, tab_scales, offs, w1, pos
             raw[b, a] = raws.tile([P, PACK, K_PASS], F32, name="raw")
             nc.sync.dma_start(out=raw[b, a][:], in_=w1[a * K_PASS : (a + 1) * K_PASS, b * K_PASS : (b + 1) * K_PASS].rearrange("(p j) c -> p j c", j=PACK))
 
+        row0 = (0, 16, 64)
+
+        def place_rows(a):
+            for q in range(4):
+                nc.sync.dma_start(out=v_sc[a][32 * q : 32 * q + 4, :].bitcast(I32), in_=v_rows[row0[a] + 4 * q : row0[a] + 4 * q + 4, :].bitcast(I32))
+
         load_tab(0)
         nc.sync.dma_start(offs_t[:], offs)
-        for q in range(4):
-            nc.sync.dma_start(out=tab_sc[32 * q : 32 * q + 4 * PASSES1, :].bitcast(I32), in_=tab_scales[:, 4 * q : 4 * q + 4, :].bitcast(I32))
+        nc.sync.dma_start(out=tab_sc[0:32, :].bitcast(I32), in_=tab_scales[0:2].rearrange("a q t -> (a q) t").bitcast(I32))
+        nc.sync.dma_start(out=tab_sc[64:80, :].bitcast(I32), in_=tab_scales[2].bitcast(I32))
+        nc.sync.dma_start(out=w2_sc_raw[96:112, :, :].bitcast(I32), in_=w2_scales.rearrange("a q n -> q a n").bitcast(I32))
+        nc.vector.tensor_copy(out=v_rows[:], in_=tab_sc[:].indirect(offs_t[:]))
         load_w1(0, 0)
         load_tab(1)
-        for q in range(4):
-            nc.sync.dma_start(out=w2_sc_raw[32 * q : 32 * q + 4, :, :].bitcast(I32), in_=w2_scales[:, 4 * q : 4 * q + 4, :].rearrange("a r n -> r a n").bitcast(I32))
-        load_w1(0, 1)
-        load_tab(2)
         nc.sync.dma_start(pos1_t[:], pos1)
         nc.sync.dma_start(pos2_t[:], pos2)
-        nc.sync.dma_start(out=gain_t[:], in_=gain.rearrange("(b p t) -> p b t", p=P, t=PACK))
+        place_rows(0)
+        load_w1(0, 1)
+        load_tab(2)
+        place_rows(1)
         load_w1(0, 2)
+        place_rows(2)
         nc.sync.dma_start(out=w2_raw[:], in_=w2_words.rearrange("a p n -> p a n").bitcast(I32))
 
         v_words = [keep.tile([P, S], U32, name="v_words%d" % a, align_bytes=64) for a in range(PASSES1)]
-        v_sc = keep.tile([P, S], U8, name="v_sc", align_bytes=64)
         w2_w = keep.tile([P, PASSES2, 2 * H], U8, name="w2_w", align_bytes=64)
-        w2_sc = keep.tile([P, PASSES2, H], U8, name="w2_sc", align_bytes=64)
 
         w_codes, w_sc, banks, h, z_codes, z_sc, picked2 = {}, {}, {}, {}, {}, {}, {}
 
@@ -85,9 +97,9 @@ def tile_list_ant_trail_residual_kernel(tc, tab_words, tab_scales, offs, w1, pos
             dst = rounded[:].rearrange("p (t m j) -> p m j t", t=PACK, j=PACK)
             w_codes[b, a] = keep.tile([P, K_PASS], U32, name="w_codes%d%d" % (b, a), align_bytes=64)
             w_sc[b, a] = keep.tile([P, K_PASS], U8, name="w_sc%d%d" % (b, a), align_bytes=64)
-            if how == "split":
-                nc.vector.tensor_copy(out=dst[:, :V_SHARE], in_=src[:, :V_SHARE])
-                nc.scalar.copy(out=dst[:, V_SHARE:], in_=src[:, V_SHARE:])
+            if isinstance(how, int):
+                nc.vector.tensor_copy(out=dst[:, :how], in_=src[:, :how])
+                nc.scalar.copy(out=dst[:, how:], in_=src[:, how:])
                 for t in range(PACK):
                     nc.vector.quantize_mx(out=w_codes[b, a][:, t * P : (t + 1) * P].bitcast(FP8X4), scales=w_sc[b, a][:, t * P : (t + 1) * P], in_=rounded[:, t * K_PASS : (t + 1) * K_PASS])
             else:
@@ -109,7 +121,7 @@ def tile_list_ant_trail_residual_kernel(tc, tab_words, tab_scales, offs, w1, pos
                         lhsT=w_codes[b, a][:, t * P : (t + 1) * P].bitcast(FP8X4),
                         lhsT_scale=w_sc[b, a][:, t * P : (t + 1) * P],
                         rhs=v_words[a][:, cols].bitcast(FP8X4),
-                        rhs_scale=v_sc[4 * a : P, cols],
+                        rhs_scale=v_sc[a][:, cols],
                         start=(a == 0),
                         stop=(a == PASSES1 - 1),
                     )
@@ -146,11 +158,10 @@ def tile_list_ant_trail_residual_kernel(tc, tab_words, tab_scales, offs, w1, pos
                 picked2[b, t] = group[:, i, :]
                 nc.vector.tensor_copy(out=picked2[b, t], in_=h[b, t][:].indirect(pos2_t[:]))
 
-        nc.vector.tensor_copy(out=w2_sc[:].rearrange("p a (b t m) -> p (a b) m t", t=PACK, m=P), in_=w2_sc_raw[:].rearrange("p a (b m t) -> p (a b) m t", t=PACK, m=P))
-        nc.vector.tensor_copy(out=v_sc[:], in_=tab_sc[:].indirect(offs_t[:]))
         for a in range(PASSES1):
             nc.vector.tensor_copy(out=v_words[a][:], in_=tab[a][:].indirect(offs_t[:]))
-            quantise_w1(0, a, "split" if a == PASSES1 - 1 else "scalar")
+            quantise_w1(0, a, 84 if a == PASSES1 - 1 else "scalar")
+        nc.vector.tensor_copy(out=w2_rows[:].rearrange("p a (b t m) -> p (a b) m t", t=PACK, m=P), in_=w2_sc_raw[:].rearrange("p a (b m t) -> p (a b) m t", t=PACK, m=P))
         first_passes(0)
         nc.vector.tensor_copy(
             out=w2_w[:].bitcast(U16).rearrange("p a (b t m) -> p (a b) m t", t=PACK, m=P),
@@ -158,18 +169,19 @@ def tile_list_ant_trail_residual_kernel(tc, tab_words, tab_scales, offs, w1, pos
         )
         for a in range(PASSES1):
             load_w1(1, a)
+        nc.sync.dma_start(out=gain_t[:], in_=gain.rearrange("(b p t) -> p b t", p=P, t=PACK))
+        for q in range(4):
+            nc.sync.dma_start(out=w2_sc[32 * q : 32 * q + 4, :, :].bitcast(I32), in_=w2_rows[96 + 4 * q : 96 + 4 * q + 4, :, :].bitcast(I32))
         for a in range(PASSES1):
-            quantise_w1(1, a, "scalar" if a == 1 else "split")
+            quantise_w1(1, a, (64, "scalar", 48)[a])
         x0 = make_z(0)
         first_passes(1)
         x1 = make_z(1)
         finish_z(0, x0)
         finish_z(1, x1)
-        pick2("stage1", [(0, 0), (0, 1)], 64)
-        pick2("stage2", [(0, 2), (0, 3)], 64)
-        pick2("squares0", [(1, 0), (1, 1)], 64)
-        pick2("z1", [(1, 2)], 64)
-        pick2("squares1", [(1, 3)], 64)
+        tags = ("stage0", "stage1", "stage2", "own", "squares0", "z0", "squares1", "z1")
+        for i, tag in enumerate(tags):
+            pick2(tag, [divmod(i, PACK)], 64)
 
         out_rows = out.rearrange("(b p t) m -> b t p m", p=P, t=PACK)
         y = {}

@@ -58,9 +58,14 @@ def tile_list_ant_trail_residual_kernel(tc, tab_words, tab_scales, offs, w1, pos
         def load_tab(a):
             nc.sync.dma_start(out=tab[a][:].bitcast(I32), in_=tab_words[a].rearrange("p t i -> p (t i)").bitcast(I32))
 
-        def load_w1(b, a):
-            raw[b, a] = raws.tile([P, PACK, K_PASS], F32, name="raw")
-            nc.sync.dma_start(out=raw[b, a][:], in_=w1[a * K_PASS : (a + 1) * K_PASS, b * K_PASS : (b + 1) * K_PASS].rearrange("(p j) c -> p j c", j=PACK))
+        def load_w1(b, a, parts=1):
+            width = K_PASS // parts
+            raw[b, a] = []
+            for part in range(parts):
+                piece = raws.tile([P, PACK, width], F32, name="raw")
+                c0 = b * K_PASS + part * width
+                nc.sync.dma_start(out=piece[:], in_=w1[a * K_PASS : (a + 1) * K_PASS, c0 : c0 + width].rearrange("(p j) c -> p j c", j=PACK))
+                raw[b, a].append(piece)
 
         row0 = (0, 16, 64)
 
@@ -69,9 +74,9 @@ def tile_list_ant_trail_residual_kernel(tc, tab_words, tab_scales, offs, w1, pos
                 nc.sync.dma_start(out=v_sc[a][32 * q : 32 * q + 4, :].bitcast(I32), in_=v_rows[row0[a] + 4 * q : row0[a] + 4 * q + 4, :].bitcast(I32))
 
         load_tab(0)
-        nc.sync.dma_start(offs_t[:], offs)
         nc.sync.dma_start(out=tab_sc[0:32, :].bitcast(I32), in_=tab_scales[0:2].rearrange("a q t -> (a q) t").bitcast(I32))
         nc.sync.dma_start(out=tab_sc[64:80, :].bitcast(I32), in_=tab_scales[2].bitcast(I32))
+        nc.sync.dma_start(offs_t[:], offs)
         nc.sync.dma_start(out=w2_sc_raw[96:112, :, :].bitcast(I32), in_=w2_scales.rearrange("a q n -> q a n").bitcast(I32))
         nc.vector.tensor_copy(out=v_rows[:], in_=tab_sc[:].indirect(offs_t[:]))
         load_w1(0, 0)
@@ -82,7 +87,7 @@ def tile_list_ant_trail_residual_kernel(tc, tab_words, tab_scales, offs, w1, pos
         load_w1(0, 1)
         load_tab(2)
         place_rows(1)
-        load_w1(0, 2)
+        load_w1(0, 2, 2)
         place_rows(2)
         nc.sync.dma_start(out=w2_raw[:], in_=w2_words.rearrange("a p n -> p a n").bitcast(I32))
 
@@ -91,23 +96,23 @@ def tile_list_ant_trail_residual_kernel(tc, tab_words, tab_scales, offs, w1, pos
 
         w_codes, w_sc, banks, h, z_codes, z_sc, picked2 = {}, {}, {}, {}, {}, {}, {}
 
-        def quantise_w1(b, a, how):
+        def quantise_w1(b, a, vector_share, by_tile):
             rounded = keep.tile([P, PACK * K_PASS], BF16, name="rounded", tag="stage%d" % a, align_bytes=64)
-            src = raw[b, a][:].rearrange("p j (m t) -> p m j t", t=PACK)
             dst = rounded[:].rearrange("p (t m j) -> p m j t", t=PACK, j=PACK)
+            m0 = 0
+            for piece in raw[b, a]:
+                src = piece[:].rearrange("p j (m t) -> p m j t", t=PACK)
+                count = src.shape[1]
+                share = vector_share if m0 + count == P else 0
+                if share:
+                    nc.vector.tensor_copy(out=dst[:, m0 : m0 + share], in_=src[:, :share])
+                nc.scalar.copy(out=dst[:, m0 + share : m0 + count], in_=src[:, share:])
+                m0 = m0 + count
             w_codes[b, a] = keep.tile([P, K_PASS], U32, name="w_codes%d%d" % (b, a), align_bytes=64)
             w_sc[b, a] = keep.tile([P, K_PASS], U8, name="w_sc%d%d" % (b, a), align_bytes=64)
-            if isinstance(how, int):
-                nc.vector.tensor_copy(out=dst[:, :how], in_=src[:, :how])
-                nc.scalar.copy(out=dst[:, how:], in_=src[:, how:])
-                for t in range(PACK):
-                    nc.vector.quantize_mx(out=w_codes[b, a][:, t * P : (t + 1) * P].bitcast(FP8X4), scales=w_sc[b, a][:, t * P : (t + 1) * P], in_=rounded[:, t * K_PASS : (t + 1) * K_PASS])
-            else:
-                if how == "vector":
-                    nc.vector.tensor_copy(out=dst, in_=src)
-                else:
-                    nc.scalar.copy(out=dst, in_=src)
-                nc.vector.quantize_mx(out=w_codes[b, a][:].bitcast(FP8X4), scales=w_sc[b, a][:], in_=rounded[:])
+            step = P if by_tile else K_PASS
+            for c0 in range(0, K_PASS, step):
+                nc.vector.quantize_mx(out=w_codes[b, a][:, c0 : c0 + step].bitcast(FP8X4), scales=w_sc[b, a][:, c0 : c0 + step], in_=rounded[:, PACK * c0 : PACK * (c0 + step)])
 
         def first_passes(b):
             for t in range(PACK):
@@ -160,7 +165,7 @@ def tile_list_ant_trail_residual_kernel(tc, tab_words, tab_scales, offs, w1, pos
 
         for a in range(PASSES1):
             nc.vector.tensor_copy(out=v_words[a][:], in_=tab[a][:].indirect(offs_t[:]))
-            quantise_w1(0, a, 84 if a == PASSES1 - 1 else "scalar")
+            quantise_w1(0, a, (0, 0, 42)[a], a == PASSES1 - 1)
         nc.vector.tensor_copy(out=w2_rows[:].rearrange("p a (b t m) -> p (a b) m t", t=PACK, m=P), in_=w2_sc_raw[:].rearrange("p a (b m t) -> p (a b) m t", t=PACK, m=P))
         first_passes(0)
         nc.vector.tensor_copy(
@@ -173,13 +178,13 @@ def tile_list_ant_trail_residual_kernel(tc, tab_words, tab_scales, offs, w1, pos
         for q in range(4):
             nc.sync.dma_start(out=w2_sc[32 * q : 32 * q + 4, :, :].bitcast(I32), in_=w2_rows[96 + 4 * q : 96 + 4 * q + 4, :, :].bitcast(I32))
         for a in range(PASSES1):
-            quantise_w1(1, a, (64, "scalar", 48)[a])
+            quantise_w1(1, a, (64, 0, 48)[a], a == PASSES1 - 1)
         x0 = make_z(0)
         first_passes(1)
         x1 = make_z(1)
         finish_z(0, x0)
         finish_z(1, x1)
-        tags = ("stage0", "stage1", "stage2", "own", "squares0", "z0", "squares1", "z1")
+        tags = ("stage0", "stage1", "stage2", "own", "squares0", "squares1")
         for i, tag in enumerate(tags):
             pick2(tag, [divmod(i, PACK)], 64)
 
@@ -203,5 +208,10 @@ def tile_list_ant_trail_residual_kernel(tc, tab_words, tab_scales, offs, w1, pos
         for b in range(PASSES2):
             for t in range(PACK):
                 result = keep.tile([P, M], F32, name="result%d%d" % (b, t))
-                nc.vector.scalar_tensor_tensor(out=result[:], in0=y[b, t][:], scalar=1.0, in1=picked2[b, t], op0=ALU.add, op1=ALU.mult)
+                if (b, t) in picked2:
+                    nc.vector.scalar_tensor_tensor(out=result[:], in0=y[b, t][:], scalar=1.0, in1=picked2[b, t], op0=ALU.add, op1=ALU.mult)
+                else:
+                    factor = keep.tile([P, M], F32, name="factor", tag="x%d" % (t % 2), align_bytes=64)
+                    nc.scalar.activation(out=factor[:], in_=y[b, t][:], func=ACT.Identity, bias=1.0)
+                    nc.vector.tensor_tensor(out=result[:], in0=h[b, t][:].indirect(pos2_t[:]), in1=factor[:], op=ALU.mult)
                 nc.sync.dma_start(out=out_rows[b, t], in_=result[:])

@@ -22,6 +22,7 @@ K_PASS = P * PACK
 BANK = 512
 PASSES1 = K // K_PASS
 PASSES2 = H // K_PASS
+ON_GPSIMD = []
 
 
 def tile_list_ant_trail_residual_kernel(tc, tab_words, tab_scales, offs, w1, pos1, pos2, gain, w2_words, w2_scales, out):
@@ -54,6 +55,8 @@ def tile_list_ant_trail_residual_kernel(tc, tab_words, tab_scales, offs, w1, pos
         nc.scalar.activation(out=warm[:], in_=warm[:], func=ACT.Silu)
 
         raw = {}
+        squares, z = {}, {}
+        h_on = {}
 
         def load_tab(a):
             nc.sync.dma_start(out=tab[a][:].bitcast(I32), in_=tab_words[a].rearrange("p t i -> p (t i)").bitcast(I32))
@@ -62,22 +65,27 @@ def tile_list_ant_trail_residual_kernel(tc, tab_words, tab_scales, offs, w1, pos
             width = K_PASS // parts
             raw[b, a] = []
             for part in range(parts):
-                piece = raws.tile([P, PACK, width], F32, name="raw")
+                if (b, a) == (1, PASSES1 - 1):
+                    piece = keep.tile([P, PACK, width], F32, name="raw_last", align_bytes=64)
+                else:
+                    piece = raws.tile([P, PACK, width], F32, name="raw")
                 c0 = b * K_PASS + part * width
                 nc.sync.dma_start(out=piece[:], in_=w1[a * K_PASS : (a + 1) * K_PASS, c0 : c0 + width].rearrange("(p j) c -> p j c", j=PACK))
                 raw[b, a].append(piece)
 
-        row0 = (0, 16, 64)
+        staged = ((0, 4), (64, 4), (2, 8))
 
         def place_rows(a):
+            first, step = staged[a]
             for q in range(4):
-                nc.sync.dma_start(out=v_sc[a][32 * q : 32 * q + 4, :].bitcast(I32), in_=v_rows[row0[a] + 4 * q : row0[a] + 4 * q + 4, :].bitcast(I32))
+                row = first + 4 * q * step
+                nc.sync.dma_start(out=v_sc[a][32 * q + 4 * a : 32 * q + 4 * a + 4, :].bitcast(I32), in_=v_rows[row : row + 3 * step + 1 : step, :].bitcast(I32))
 
         load_tab(0)
-        nc.sync.dma_start(out=tab_sc[0:32, :].bitcast(I32), in_=tab_scales[0:2].rearrange("a q t -> (a q) t").bitcast(I32))
-        nc.sync.dma_start(out=tab_sc[64:80, :].bitcast(I32), in_=tab_scales[2].bitcast(I32))
+        nc.sync.dma_start(out=tab_sc[0:128:4, :].bitcast(I32), in_=tab_scales[0:2].rearrange("a q t -> (a q) t").bitcast(I32))
+        nc.sync.dma_start(out=tab_sc[2:128:8, :].bitcast(I32), in_=tab_scales[2].bitcast(I32))
         nc.sync.dma_start(offs_t[:], offs)
-        nc.sync.dma_start(out=w2_sc_raw[96:112, :, :].bitcast(I32), in_=w2_scales.rearrange("a q n -> q a n").bitcast(I32))
+        nc.sync.dma_start(out=w2_sc_raw[1:128:8, :, :].bitcast(I32), in_=w2_scales.rearrange("a q n -> q a n").bitcast(I32))
         nc.vector.tensor_copy(out=v_rows[:], in_=tab_sc[:].indirect(offs_t[:]))
         load_w1(0, 0)
         load_tab(1)
@@ -104,9 +112,12 @@ def tile_list_ant_trail_residual_kernel(tc, tab_words, tab_scales, offs, w1, pos
                 src = piece[:].rearrange("p j (m t) -> p m j t", t=PACK)
                 count = src.shape[1]
                 share = vector_share if m0 + count == P else 0
-                if share:
+                if share and (b, a) not in ON_GPSIMD:
                     nc.vector.tensor_copy(out=dst[:, m0 : m0 + share], in_=src[:, :share])
-                nc.scalar.copy(out=dst[:, m0 + share : m0 + count], in_=src[:, share:])
+                if share and (b, a) in ON_GPSIMD:
+                    nc.gpsimd.tensor_scalar(out=dst[:, m0 : m0 + share].rearrange("p m j t -> p m t j"), in0=src[:, :share].rearrange("p m j t -> p m t j"), scalar1=1.0, scalar2=0.0, op0=ALU.mult, op1=ALU.add)
+                if share < count:
+                    nc.scalar.copy(out=dst[:, m0 + share : m0 + count], in_=src[:, share:])
                 m0 = m0 + count
             w_codes[b, a] = keep.tile([P, K_PASS], U32, name="w_codes%d%d" % (b, a), align_bytes=64)
             w_sc[b, a] = keep.tile([P, K_PASS], U8, name="w_sc%d%d" % (b, a), align_bytes=64)
@@ -126,42 +137,52 @@ def tile_list_ant_trail_residual_kernel(tc, tab_words, tab_scales, offs, w1, pos
                         lhsT=w_codes[b, a][:, t * P : (t + 1) * P].bitcast(FP8X4),
                         lhsT_scale=w_sc[b, a][:, t * P : (t + 1) * P],
                         rhs=v_words[a][:, cols].bitcast(FP8X4),
-                        rhs_scale=v_sc[a][:, cols],
+                        rhs_scale=v_sc[a][4 * a :, cols],
                         start=(a == 0),
                         stop=(a == PASSES1 - 1),
                     )
 
         def make_z(b):
             x = keep.tile([P, PACK, M], F32, name="x", tag="x%d" % b, align_bytes=64)
+            if b == 1:
+                joined = keep.tile([P, PACK * S], F32, name="h1")
             for t in range(PACK):
-                h[b, t] = keep.tile([P, S], F32, name="h%d%d" % (b, t))
+                if b == 0:
+                    h[b, t] = keep.tile([P, S], F32, name="h0%d" % t)
+                    h_on[b, t] = h[b, t][:]
+                else:
+                    h[b, t] = joined[:, t * S : (t + 1) * S]
+                    h_on[b, t] = joined[:, t * S :]
                 for half in range(2):
                     nc.scalar.copy(out=h[b, t][:, half * BANK : (half + 1) * BANK], in_=banks[b, t, half][:])
-                nc.vector.tensor_copy(out=x[:, t, :], in_=h[b, t][:].indirect(pos1_t[:]))
+                nc.vector.tensor_copy(out=x[:, t, :], in_=h[b, t][:, :].indirect(pos1_t[:]))
             return x
 
-        def finish_z(b, x):
+        def silu(picked1, x):
             for t in range(PACK):
-                nc.scalar.activation(out=x[:, t, :], in_=x[:, t, :], func=ACT.Silu)
-            squares = keep.tile([P, M, PACK], F32, name="squares", tag="squares%d" % b, align_bytes=64)
-            z = keep.tile([P, M, PACK], BF16, name="z", tag="z%d" % b, align_bytes=64)
-            for half in range(2):
-                cols = slice(half * M // 2, (half + 1) * M // 2)
-                nc.scalar.activation(
-                    out=squares[:, cols, :].rearrange("p (c i) t -> p c t i", i=4),
-                    in_=x[:, :, cols].rearrange("p t (c i) -> p c t i", i=4),
-                    func=ACT.Square,
-                )
-                nc.vector.tensor_tensor(out=z[:, cols, :], in0=squares[:, cols, :], in1=gain_t[:, b, :].unsqueeze(1).to_broadcast([P, M // 2, PACK]), op=ALU.mult)
-            z_codes[b] = keep.tile([P, M], U32, name="z_codes%d" % b, align_bytes=64)
-            z_sc[b] = keep.tile([P, M], U8, name="z_sc%d" % b, align_bytes=64)
-            nc.vector.quantize_mx(out=z_codes[b][:].bitcast(FP8X4), scales=z_sc[b][:], in_=z[:].rearrange("p m t -> p (m t)"))
+                nc.scalar.activation(out=x[:, t, :], in_=picked1[:, t, :], func=ACT.Silu)
 
-        def pick2(tag, tiles, align):
-            group = keep.tile([P, len(tiles), M], F32, name="picked", tag=tag, align_bytes=align)
+        def z_half(b, x, half):
+            if half == 0:
+                squares[b] = keep.tile([P, M, PACK], F32, name="squares", tag="squares%d" % b, align_bytes=64)
+                z[b] = keep.tile([P, M, PACK], BF16, name="z", tag="z", align_bytes=64)
+            cols = slice(half * M // 2, (half + 1) * M // 2)
+            nc.scalar.activation(
+                out=squares[b][:, cols, :].rearrange("p (c i) t -> p c t i", i=4),
+                in_=x[:, :, cols].rearrange("p t (c i) -> p c t i", i=4),
+                func=ACT.Square,
+            )
+            (nc.gpsimd if b == 0 else nc.vector).tensor_tensor(out=z[b][:, cols, :], in0=squares[b][:, cols, :], in1=gain_t[:, b, :].unsqueeze(1).to_broadcast([P, M // 2, PACK]), op=ALU.mult)
+            if half == 1:
+                z_codes[b] = keep.tile([P, M], U32, name="z_codes%d" % b, align_bytes=64)
+                z_sc[b] = keep.tile([P, M], U8, name="z_sc%d" % b, align_bytes=64)
+                nc.vector.quantize_mx(out=z_codes[b][:].bitcast(FP8X4), scales=z_sc[b][:], in_=z[b][:].rearrange("p m t -> p (m t)"))
+
+        def pick2(tag, tiles, wide):
+            group = keep.tile([P, len(tiles), M], F32, name="picked", tag=tag, align_bytes=64)
             for i, (b, t) in enumerate(tiles):
                 picked2[b, t] = group[:, i, :]
-                nc.vector.tensor_copy(out=picked2[b, t], in_=h[b, t][:].indirect(pos2_t[:]))
+                nc.vector.tensor_copy(out=picked2[b, t], in_=h_on[b, t].indirect(pos2_t[:]))
 
         for a in range(PASSES1):
             nc.vector.tensor_copy(out=v_words[a][:], in_=tab[a][:].indirect(offs_t[:]))
@@ -176,42 +197,50 @@ def tile_list_ant_trail_residual_kernel(tc, tab_words, tab_scales, offs, w1, pos
             load_w1(1, a)
         nc.sync.dma_start(out=gain_t[:], in_=gain.rearrange("(b p t) -> p b t", p=P, t=PACK))
         for q in range(4):
-            nc.sync.dma_start(out=w2_sc[32 * q : 32 * q + 4, :, :].bitcast(I32), in_=w2_rows[96 + 4 * q : 96 + 4 * q + 4, :, :].bitcast(I32))
+            nc.sync.dma_start(out=w2_sc[32 * q : 32 * q + 4, :, :].bitcast(I32), in_=w2_rows[1 + 32 * q : 32 * q + 32 : 8, :, :].bitcast(I32))
         for a in range(PASSES1):
             quantise_w1(1, a, (64, 0, 48)[a], a == PASSES1 - 1)
         x0 = make_z(0)
         first_passes(1)
+        silu0 = keep.tile([P, PACK, M], F32, name="silu0", tag="raw_last", align_bytes=64)
+        for half in range(2):
+            cols = slice(half * M // 2, (half + 1) * M // 2)
+            nc.scalar.activation(out=silu0[:, :, cols], in_=x0[:, :, cols], func=ACT.Silu)
+        z_half(0, silu0, 0)
         x1 = make_z(1)
-        finish_z(0, x0)
-        finish_z(1, x1)
-        tags = ("stage0", "stage1", "stage2", "own", "squares0", "squares1")
-        for i, tag in enumerate(tags):
-            pick2(tag, [divmod(i, PACK)], 64)
+        pick2("wide", [(1, 1), (1, 2)], True)
+        z_half(0, silu0, 1)
+        silu(x1, x1)
+        for half in range(2):
+            z_half(1, x1, half)
+        pick2("stage0", [(0, 0)], False)
+        pick2("stage2", [(0, 1), (0, 2), (0, 3)], False)
+        pick2("squares1", [(1, 3)], False)
 
+        results = keep.tile([P, PASSES2 * PACK, M], F32, name="results", tag="tab0", align_bytes=64)
         out_rows = out.rearrange("(b p t) m -> b t p m", p=P, t=PACK)
         y = {}
+        tiles = list(picked2) + [(b, t) for b in range(PASSES2) for t in range(PACK) if (b, t) not in picked2]
         for a in range(PASSES2):
-            for b in range(PASSES2):
-                for t in range(PACK):
-                    if a == 0:
-                        y[b, t] = psum.tile([P, BANK], F32, name="bank%d" % (PACK * b + t))
-                    c0 = b * K_PASS + t * P
-                    nc.tensor.matmul_mx(
-                        out=y[b, t][:],
-                        lhsT=w2_w[:, a, 2 * c0 : 2 * (c0 + P)].bitcast(FP4X4),
-                        lhsT_scale=w2_sc[:, a, c0 : c0 + P],
-                        rhs=z_codes[a][:].bitcast(FP8X4),
-                        rhs_scale=z_sc[a][:],
-                        start=(a == 0),
-                        stop=(a == PASSES2 - 1),
-                    )
-        for b in range(PASSES2):
-            for t in range(PACK):
-                result = keep.tile([P, M], F32, name="result%d%d" % (b, t))
-                if (b, t) in picked2:
-                    nc.vector.scalar_tensor_tensor(out=result[:], in0=y[b, t][:], scalar=1.0, in1=picked2[b, t], op0=ALU.add, op1=ALU.mult)
-                else:
-                    factor = keep.tile([P, M], F32, name="factor", tag="x%d" % (t % 2), align_bytes=64)
-                    nc.scalar.activation(out=factor[:], in_=y[b, t][:], func=ACT.Identity, bias=1.0)
-                    nc.vector.tensor_tensor(out=result[:], in0=h[b, t][:].indirect(pos2_t[:]), in1=factor[:], op=ALU.mult)
-                nc.sync.dma_start(out=out_rows[b, t], in_=result[:])
+            for b, t in tiles:
+                if a == 0:
+                    y[b, t] = psum.tile([P, BANK], F32, name="bank%d" % (PACK * b + t))
+                c0 = b * K_PASS + t * P
+                nc.tensor.matmul_mx(
+                    out=y[b, t][:],
+                    lhsT=w2_w[:, a, 2 * c0 : 2 * (c0 + P)].bitcast(FP4X4),
+                    lhsT_scale=w2_sc[:, a, c0 : c0 + P],
+                    rhs=z_codes[a][:].bitcast(FP8X4),
+                    rhs_scale=z_sc[a][:],
+                    start=(a == 0),
+                    stop=(a == PASSES2 - 1),
+                )
+        for b, t in tiles:
+            result = results[:, PACK * b + t, :]
+            if (b, t) in picked2:
+                nc.vector.scalar_tensor_tensor(out=result, in0=y[b, t][:], scalar=1.0, in1=picked2[b, t], op0=ALU.add, op1=ALU.mult)
+            else:
+                factor = keep.tile([P, M], F32, name="factor%d%d" % (b, t), align_bytes=64)
+                nc.scalar.activation(out=factor[:], in_=y[b, t][:], func=ACT.Identity, bias=1.0)
+                nc.vector.tensor_tensor(out=result, in0=h_on[b, t].indirect(pos2_t[:]), in1=factor[:], op=ALU.mult)
+            nc.sync.dma_start(out=out_rows[b, t], in_=result)

@@ -22,7 +22,7 @@ K_PASS = P * PACK
 BANK = 512
 PASSES1 = K // K_PASS
 PASSES2 = H // K_PASS
-ON_GPSIMD = []
+ON_GPSIMD = [(1, 0)]
 
 
 def tile_list_ant_trail_residual_kernel(tc, tab_words, tab_scales, offs, w1, pos1, pos2, gain, w2_words, w2_scales, out):
@@ -120,16 +120,17 @@ def tile_list_ant_trail_residual_kernel(tc, tab_words, tab_scales, offs, w1, pos
                     nc.scalar.copy(out=dst[:, m0 + share : m0 + count], in_=src[:, share:])
                 m0 = m0 + count
             w_codes[b, a] = keep.tile([P, K_PASS], U32, name="w_codes%d%d" % (b, a), align_bytes=64)
-            w_sc[b, a] = keep.tile([P, K_PASS], U8, name="w_sc%d%d" % (b, a), align_bytes=64)
+            w_sc[b, a] = keep.tile([P, K_PASS], U8, name="w_sc%d%d" % (b, a), tag={(1, 0): "stage1", (1, 2): "stage0"}.get((b, a), "w_sc%d%d" % (b, a)), align_bytes=64)
             step = P if by_tile else K_PASS
             for c0 in range(0, K_PASS, step):
                 nc.vector.quantize_mx(out=w_codes[b, a][:, c0 : c0 + step].bitcast(FP8X4), scales=w_sc[b, a][:, c0 : c0 + step], in_=rounded[:, PACK * c0 : PACK * (c0 + step)])
 
         def first_passes(b):
             for t in range(PACK):
-              for a in range(PASSES1):
+              order = ((0, 1, 2), (1, 0, 2))[b]
+              for a in order:
                 for half in range(2):
-                    if a == 0:
+                    if a == order[0]:
                         banks[b, t, half] = psum.tile([P, BANK], F32, name="bank%d" % (2 * t + half))
                     cols = slice(half * BANK, (half + 1) * BANK)
                     nc.tensor.matmul_mx(
@@ -138,7 +139,7 @@ def tile_list_ant_trail_residual_kernel(tc, tab_words, tab_scales, offs, w1, pos
                         lhsT_scale=w_sc[b, a][:, t * P : (t + 1) * P],
                         rhs=v_words[a][:, cols].bitcast(FP8X4),
                         rhs_scale=v_sc[a][4 * a :, cols],
-                        start=(a == 0),
+                        start=(a == order[0]),
                         stop=(a == PASSES1 - 1),
                     )
 
@@ -174,8 +175,12 @@ def tile_list_ant_trail_residual_kernel(tc, tab_words, tab_scales, offs, w1, pos
             )
             (nc.gpsimd if b == 0 else nc.vector).tensor_tensor(out=z[b][:, cols, :], in0=squares[b][:, cols, :], in1=gain_t[:, b, :].unsqueeze(1).to_broadcast([P, M // 2, PACK]), op=ALU.mult)
             if half == 1:
+                quantise_z(b)
+
+        def quantise_z(b):
+            if True:
                 z_codes[b] = keep.tile([P, M], U32, name="z_codes%d" % b, align_bytes=64)
-                z_sc[b] = keep.tile([P, M], U8, name="z_sc%d" % b, align_bytes=64)
+                z_sc[b] = keep.tile([P, M], U8, name="z_sc%d" % b, tag=("x1", "z_sc1")[b], align_bytes=64)
                 nc.vector.quantize_mx(out=z_codes[b][:].bitcast(FP8X4), scales=z_sc[b][:], in_=z[b][:].rearrange("p m t -> p (m t)"))
 
         def pick2(tag, tiles, wide):
@@ -198,23 +203,30 @@ def tile_list_ant_trail_residual_kernel(tc, tab_words, tab_scales, offs, w1, pos
         nc.sync.dma_start(out=gain_t[:], in_=gain.rearrange("(b p t) -> p b t", p=P, t=PACK))
         for q in range(4):
             nc.sync.dma_start(out=w2_sc[32 * q : 32 * q + 4, :, :].bitcast(I32), in_=w2_rows[1 + 32 * q : 32 * q + 32 : 8, :, :].bitcast(I32))
-        for a in range(PASSES1):
-            quantise_w1(1, a, (64, 0, 48)[a], a == PASSES1 - 1)
+        for a in (1, 0, 2):
+            quantise_w1(1, a, (128, 0, 48)[a], a == PASSES1 - 1)
         x0 = make_z(0)
         first_passes(1)
-        silu0 = keep.tile([P, PACK, M], F32, name="silu0", tag="raw_last", align_bytes=64)
+        silu0 = keep.tile([P, M, PACK], F32, name="silu0", tag="raw_last", align_bytes=64)
+        scaled0 = keep.tile([P, M, PACK], F32, name="scaled0", tag="squares0", align_bytes=64)
+        z[0] = keep.tile([P, M, PACK], BF16, name="z", tag="z", align_bytes=64)
         for half in range(2):
             cols = slice(half * M // 2, (half + 1) * M // 2)
-            nc.scalar.activation(out=silu0[:, :, cols], in_=x0[:, :, cols], func=ACT.Silu)
-        z_half(0, silu0, 0)
+            nc.scalar.activation(
+                out=silu0[:, cols, :].rearrange("p (c i) t -> p c t i", i=4),
+                in_=x0[:, :, cols].rearrange("p t (c i) -> p c t i", i=4),
+                func=ACT.Silu,
+            )
+            nc.gpsimd.tensor_tensor(out=scaled0[:, cols, :], in0=silu0[:, cols, :], in1=gain_t[:, 0, :].unsqueeze(1).to_broadcast([P, M // 2, PACK]), op=ALU.mult)
+            nc.gpsimd.tensor_tensor(out=z[0][:, cols, :], in0=scaled0[:, cols, :], in1=silu0[:, cols, :], op=ALU.mult)
         x1 = make_z(1)
         pick2("wide", [(1, 1), (1, 2)], True)
-        z_half(0, silu0, 1)
-        silu(x1, x1)
+        silu1 = keep.tile([P, PACK, M], F32, name="silu1", tag="x0", align_bytes=64)
+        silu(x1, silu1)
+        quantise_z(0)
         for half in range(2):
-            z_half(1, x1, half)
-        pick2("stage0", [(0, 0)], False)
-        pick2("stage2", [(0, 1), (0, 2), (0, 3)], False)
+            z_half(1, silu1, half)
+        pick2("stage2", [(0, 0), (0, 1), (0, 2)], False)
         pick2("squares1", [(1, 3)], False)
 
         results = keep.tile([P, PASSES2 * PACK, M], F32, name="results", tag="tab0", align_bytes=64)

@@ -22,7 +22,8 @@ K_PASS = P * PACK
 BANK = 512
 PASSES1 = K // K_PASS
 PASSES2 = H // K_PASS
-ON_GPSIMD = [(1, 0)]
+HALF = M // 2
+VECTOR_SHARE = (42, 48)
 
 
 def tile_list_ant_trail_residual_kernel(tc, tab_words, tab_scales, offs, w1, pos1, pos2, gain, w2_words, w2_scales, out):
@@ -40,23 +41,20 @@ def tile_list_ant_trail_residual_kernel(tc, tab_words, tab_scales, offs, w1, pos
         w2_raw = keep.tile([P, PASSES2, H // 2], I32, name="w2_raw", align_bytes=64)
         w2_sc_raw = keep.tile([P, PASSES2, H], U8, name="w2_sc_raw", align_bytes=64)
         gain_t = keep.tile([P, PASSES2, PACK], F32, name="gain_t")
-
-        nc.vector.memset(tab_sc[:].bitcast(I32), 0)
-        nc.vector.memset(w2_sc_raw[:].bitcast(I32), 0)
         v_rows = keep.tile([P, S], U8, name="v_rows", align_bytes=64)
         v_sc = [keep.tile([P, S], U8, name="v_sc%d" % a, align_bytes=64) for a in range(PASSES1)]
         w2_rows = keep.tile([P, PASSES2, H], U8, name="w2_rows", align_bytes=64)
         w2_sc = keep.tile([P, PASSES2, H], U8, name="w2_sc", align_bytes=64)
-        for a in range(PASSES1):
-            nc.vector.memset(v_sc[a][:].bitcast(I32), 0)
-        nc.vector.memset(w2_sc[:].bitcast(I32), 0)
+        v_words = [keep.tile([P, S], U32, name="v_words%d" % a, align_bytes=64) for a in range(PASSES1)]
+        w2_w = keep.tile([P, PASSES2, 2 * H], U8, name="w2_w", align_bytes=64)
+
+        for plane in [tab_sc, w2_sc_raw] + v_sc + [w2_sc]:
+            nc.vector.memset(plane[:].bitcast(I32), 0)
         warm = keep.tile([P, 8], F32, name="warm")
         nc.vector.memset(warm[:], 0.0)
         nc.scalar.activation(out=warm[:], in_=warm[:], func=ACT.Silu)
 
-        raw = {}
-        squares, z = {}, {}
-        h_on = {}
+        raw, w_codes, w_sc, banks, h, h_on, z_codes, z_sc, picked, y = {}, {}, {}, {}, {}, {}, {}, {}, {}, {}
 
         def load_tab(a):
             nc.sync.dma_start(out=tab[a][:].bitcast(I32), in_=tab_words[a].rearrange("p t i -> p (t i)").bitcast(I32))
@@ -99,101 +97,82 @@ def tile_list_ant_trail_residual_kernel(tc, tab_words, tab_scales, offs, w1, pos
         place_rows(2)
         nc.sync.dma_start(out=w2_raw[:], in_=w2_words.rearrange("a p n -> p a n").bitcast(I32))
 
-        v_words = [keep.tile([P, S], U32, name="v_words%d" % a, align_bytes=64) for a in range(PASSES1)]
-        w2_w = keep.tile([P, PASSES2, 2 * H], U8, name="w2_w", align_bytes=64)
-
-        w_codes, w_sc, banks, h, z_codes, z_sc, picked2 = {}, {}, {}, {}, {}, {}, {}
-
-        def quantise_w1(b, a, vector_share, by_tile):
+        def quantise_w1(b, a, scale_tag):
             rounded = keep.tile([P, PACK * K_PASS], BF16, name="rounded", tag="stage%d" % a, align_bytes=64)
             dst = rounded[:].rearrange("p (t m j) -> p m j t", t=PACK, j=PACK)
+            last = a == PASSES1 - 1
             m0 = 0
             for piece in raw[b, a]:
                 src = piece[:].rearrange("p j (m t) -> p m j t", t=PACK)
                 count = src.shape[1]
-                share = vector_share if m0 + count == P else 0
-                if share and (b, a) not in ON_GPSIMD:
-                    nc.vector.tensor_copy(out=dst[:, m0 : m0 + share], in_=src[:, :share])
-                if share and (b, a) in ON_GPSIMD:
-                    nc.gpsimd.tensor_scalar(out=dst[:, m0 : m0 + share].rearrange("p m j t -> p m t j"), in0=src[:, :share].rearrange("p m j t -> p m t j"), scalar1=1.0, scalar2=0.0, op0=ALU.mult, op1=ALU.add)
-                if share < count:
+                if (b, a) == (1, 0):
+                    nc.gpsimd.tensor_scalar(out=dst.rearrange("p m j t -> p m t j"), in0=src.rearrange("p m j t -> p m t j"), scalar1=1.0, scalar2=0.0, op0=ALU.mult, op1=ALU.add)
+                else:
+                    share = VECTOR_SHARE[b] if last and m0 + count == P else 0
+                    if share:
+                        nc.vector.tensor_copy(out=dst[:, m0 : m0 + share], in_=src[:, :share])
                     nc.scalar.copy(out=dst[:, m0 + share : m0 + count], in_=src[:, share:])
                 m0 = m0 + count
             w_codes[b, a] = keep.tile([P, K_PASS], U32, name="w_codes%d%d" % (b, a), align_bytes=64)
-            w_sc[b, a] = keep.tile([P, K_PASS], U8, name="w_sc%d%d" % (b, a), tag={(1, 0): "stage1", (1, 2): "stage0"}.get((b, a), "w_sc%d%d" % (b, a)), align_bytes=64)
-            step = P if by_tile else K_PASS
+            w_sc[b, a] = keep.tile([P, K_PASS], U8, name="w_sc%d%d" % (b, a), tag=scale_tag, align_bytes=64)
+            step = P if last else K_PASS
             for c0 in range(0, K_PASS, step):
                 nc.vector.quantize_mx(out=w_codes[b, a][:, c0 : c0 + step].bitcast(FP8X4), scales=w_sc[b, a][:, c0 : c0 + step], in_=rounded[:, PACK * c0 : PACK * (c0 + step)])
 
-        def first_passes(b):
+        def first_passes(b, order):
             for t in range(PACK):
-              order = ((0, 1, 2), (1, 0, 2))[b]
-              for a in order:
-                for half in range(2):
-                    if a == order[0]:
-                        banks[b, t, half] = psum.tile([P, BANK], F32, name="bank%d" % (2 * t + half))
-                    cols = slice(half * BANK, (half + 1) * BANK)
-                    nc.tensor.matmul_mx(
-                        out=banks[b, t, half][:],
-                        lhsT=w_codes[b, a][:, t * P : (t + 1) * P].bitcast(FP8X4),
-                        lhsT_scale=w_sc[b, a][:, t * P : (t + 1) * P],
-                        rhs=v_words[a][:, cols].bitcast(FP8X4),
-                        rhs_scale=v_sc[a][4 * a :, cols],
-                        start=(a == order[0]),
-                        stop=(a == PASSES1 - 1),
-                    )
+                for a in order:
+                    for half in range(2):
+                        if a == order[0]:
+                            banks[b, t, half] = psum.tile([P, BANK], F32, name="bank%d" % (2 * t + half))
+                        cols = slice(half * BANK, (half + 1) * BANK)
+                        nc.tensor.matmul_mx(
+                            out=banks[b, t, half][:],
+                            lhsT=w_codes[b, a][:, t * P : (t + 1) * P].bitcast(FP8X4),
+                            lhsT_scale=w_sc[b, a][:, t * P : (t + 1) * P],
+                            rhs=v_words[a][:, cols].bitcast(FP8X4),
+                            rhs_scale=v_sc[a][4 * a :, cols],
+                            start=(a == order[0]),
+                            stop=(a == order[-1]),
+                        )
 
-        def make_z(b):
-            x = keep.tile([P, PACK, M], F32, name="x", tag="x%d" % b, align_bytes=64)
-            if b == 1:
-                joined = keep.tile([P, PACK * S], F32, name="h1")
+        def pick1(b):
+            x = keep.tile([P, PACK, M], F32, name="x%d" % b, align_bytes=64)
             for t in range(PACK):
-                if b == 0:
-                    h[b, t] = keep.tile([P, S], F32, name="h0%d" % t)
-                    h_on[b, t] = h[b, t][:]
-                else:
-                    h[b, t] = joined[:, t * S : (t + 1) * S]
-                    h_on[b, t] = joined[:, t * S :]
                 for half in range(2):
                     nc.scalar.copy(out=h[b, t][:, half * BANK : (half + 1) * BANK], in_=banks[b, t, half][:])
-                nc.vector.tensor_copy(out=x[:, t, :], in_=h[b, t][:, :].indirect(pos1_t[:]))
+                nc.vector.tensor_copy(out=x[:, t, :], in_=h[b, t].indirect(pos1_t[:]))
             return x
 
-        def silu(picked1, x):
-            for t in range(PACK):
-                nc.scalar.activation(out=x[:, t, :], in_=picked1[:, t, :], func=ACT.Silu)
-
-        def z_half(b, x, half):
-            if half == 0:
-                squares[b] = keep.tile([P, M, PACK], F32, name="squares", tag="squares%d" % b, align_bytes=64)
-                z[b] = keep.tile([P, M, PACK], BF16, name="z", tag="z", align_bytes=64)
-            cols = slice(half * M // 2, (half + 1) * M // 2)
-            nc.scalar.activation(
-                out=squares[b][:, cols, :].rearrange("p (c i) t -> p c t i", i=4),
-                in_=x[:, :, cols].rearrange("p t (c i) -> p c t i", i=4),
-                func=ACT.Square,
-            )
-            (nc.gpsimd if b == 0 else nc.vector).tensor_tensor(out=z[b][:, cols, :], in0=squares[b][:, cols, :], in1=gain_t[:, b, :].unsqueeze(1).to_broadcast([P, M // 2, PACK]), op=ALU.mult)
-            if half == 1:
-                quantise_z(b)
-
-        def quantise_z(b):
-            if True:
-                z_codes[b] = keep.tile([P, M], U32, name="z_codes%d" % b, align_bytes=64)
-                z_sc[b] = keep.tile([P, M], U8, name="z_sc%d" % b, tag=("x1", "z_sc1")[b], align_bytes=64)
-                nc.vector.quantize_mx(out=z_codes[b][:].bitcast(FP8X4), scales=z_sc[b][:], in_=z[b][:].rearrange("p m t -> p (m t)"))
-
-        def pick2(tag, tiles, wide):
-            group = keep.tile([P, len(tiles), M], F32, name="picked", tag=tag, align_bytes=64)
+        def pick2(group, tiles):
             for i, (b, t) in enumerate(tiles):
-                picked2[b, t] = group[:, i, :]
-                nc.vector.tensor_copy(out=picked2[b, t], in_=h_on[b, t].indirect(pos2_t[:]))
+                picked[b, t] = group[:, i, :]
+                nc.vector.tensor_copy(out=picked[b, t], in_=h_on[b, t].indirect(pos2_t[:]))
+
+        def weave(dst, src, cols, func):
+            nc.scalar.activation(out=dst[:, cols, :].rearrange("p (c i) t -> p c t i", i=4), in_=src[:, :, cols].rearrange("p t (c i) -> p c t i", i=4), func=func)
+
+        def gains(b):
+            return gain_t[:, b, :].unsqueeze(1).to_broadcast([P, HALF, PACK])
+
+        def quantise_z(b, z, scale_tag):
+            z_codes[b] = keep.tile([P, M], U32, name="z_codes%d" % b, align_bytes=64)
+            z_sc[b] = keep.tile([P, M], U8, name="z_sc%d" % b, tag=scale_tag, align_bytes=64)
+            nc.vector.quantize_mx(out=z_codes[b][:].bitcast(FP8X4), scales=z_sc[b][:], in_=z[:].rearrange("p m t -> p (m t)"))
+
+        joined = keep.tile([P, PACK * S], F32, name="h1")
+        for t in range(PACK):
+            h[0, t] = keep.tile([P, S], F32, name="h0%d" % t)[:]
+            h_on[0, t] = h[0, t]
+            h[1, t] = joined[:, t * S : (t + 1) * S]
+            h_on[1, t] = joined[:, t * S :]
+        halves = [slice(u * HALF, (u + 1) * HALF) for u in range(2)]
 
         for a in range(PASSES1):
             nc.vector.tensor_copy(out=v_words[a][:], in_=tab[a][:].indirect(offs_t[:]))
-            quantise_w1(0, a, (0, 0, 42)[a], a == PASSES1 - 1)
+            quantise_w1(0, a, "w_sc0%d" % a)
         nc.vector.tensor_copy(out=w2_rows[:].rearrange("p a (b t m) -> p (a b) m t", t=PACK, m=P), in_=w2_sc_raw[:].rearrange("p a (b m t) -> p (a b) m t", t=PACK, m=P))
-        first_passes(0)
+        first_passes(0, (0, 1, 2))
         nc.vector.tensor_copy(
             out=w2_w[:].bitcast(U16).rearrange("p a (b t m) -> p (a b) m t", t=PACK, m=P),
             in_=w2_raw[:].bitcast(U16).rearrange("p a (b m t) -> p (a b) m t", t=PACK, m=P),
@@ -203,36 +182,40 @@ def tile_list_ant_trail_residual_kernel(tc, tab_words, tab_scales, offs, w1, pos
         nc.sync.dma_start(out=gain_t[:], in_=gain.rearrange("(b p t) -> p b t", p=P, t=PACK))
         for q in range(4):
             nc.sync.dma_start(out=w2_sc[32 * q : 32 * q + 4, :, :].bitcast(I32), in_=w2_rows[1 + 32 * q : 32 * q + 32 : 8, :, :].bitcast(I32))
-        for a in (1, 0, 2):
-            quantise_w1(1, a, (128, 0, 48)[a], a == PASSES1 - 1)
-        x0 = make_z(0)
-        first_passes(1)
+
+        quantise_w1(1, 1, "w_sc11")
+        quantise_w1(1, 0, "stage1")
+        quantise_w1(1, 2, "stage0")
+        x0 = pick1(0)
+        first_passes(1, (1, 0, 2))
+
         silu0 = keep.tile([P, M, PACK], F32, name="silu0", tag="raw_last", align_bytes=64)
-        scaled0 = keep.tile([P, M, PACK], F32, name="scaled0", tag="squares0", align_bytes=64)
-        z[0] = keep.tile([P, M, PACK], BF16, name="z", tag="z", align_bytes=64)
-        for half in range(2):
-            cols = slice(half * M // 2, (half + 1) * M // 2)
-            nc.scalar.activation(
-                out=silu0[:, cols, :].rearrange("p (c i) t -> p c t i", i=4),
-                in_=x0[:, :, cols].rearrange("p t (c i) -> p c t i", i=4),
-                func=ACT.Silu,
-            )
-            nc.gpsimd.tensor_tensor(out=scaled0[:, cols, :], in0=silu0[:, cols, :], in1=gain_t[:, 0, :].unsqueeze(1).to_broadcast([P, M // 2, PACK]), op=ALU.mult)
-            nc.gpsimd.tensor_tensor(out=z[0][:, cols, :], in0=scaled0[:, cols, :], in1=silu0[:, cols, :], op=ALU.mult)
-        x1 = make_z(1)
-        pick2("wide", [(1, 1), (1, 2)], True)
+        late = keep.tile([P, PACK + 3, M], F32, name="late", tag="stage2", align_bytes=64)
+        scaled0 = late[:, :PACK, :].rearrange("p a (c t) -> p (a c) t", t=PACK)
+        z0 = keep.tile([P, M, PACK], BF16, name="z0", tag="z", align_bytes=64)
+        for cols in halves:
+            weave(silu0, x0, cols, ACT.Silu)
+            nc.gpsimd.tensor_tensor(out=scaled0[:, cols, :], in0=silu0[:, cols, :], in1=gains(0), op=ALU.mult)
+            nc.gpsimd.tensor_tensor(out=z0[:, cols, :], in0=scaled0[:, cols, :], in1=silu0[:, cols, :], op=ALU.mult)
+        x1 = pick1(1)
+        pick2(keep.tile([P, 2, M], F32, name="picked_mid", align_bytes=64), [(1, 1), (1, 2)])
+
         silu1 = keep.tile([P, PACK, M], F32, name="silu1", tag="x0", align_bytes=64)
-        silu(x1, silu1)
-        quantise_z(0)
-        for half in range(2):
-            z_half(1, silu1, half)
-        pick2("stage2", [(0, 0), (0, 1), (0, 2)], False)
-        pick2("squares1", [(1, 3)], False)
+        for t in range(PACK):
+            nc.scalar.activation(out=silu1[:, t, :], in_=x1[:, t, :], func=ACT.Silu)
+        quantise_z(0, z0, "x1")
+        squares = keep.tile([P, M, PACK], F32, name="squares", align_bytes=64)
+        z1 = keep.tile([P, M, PACK], BF16, name="z1", tag="z", align_bytes=64)
+        for cols in halves:
+            weave(squares, silu1, cols, ACT.Square)
+            nc.vector.tensor_tensor(out=z1[:, cols, :], in0=squares[:, cols, :], in1=gains(1), op=ALU.mult)
+        quantise_z(1, z1, "z_sc1")
+        pick2(late[:, PACK:, :], [(0, 0), (0, 1), (0, 2)])
+        pick2(keep.tile([P, 1, M], F32, name="picked_last", tag="squares", align_bytes=64), [(1, 3)])
 
         results = keep.tile([P, PASSES2 * PACK, M], F32, name="results", tag="tab0", align_bytes=64)
         out_rows = out.rearrange("(b p t) m -> b t p m", p=P, t=PACK)
-        y = {}
-        tiles = list(picked2) + [(b, t) for b in range(PASSES2) for t in range(PACK) if (b, t) not in picked2]
+        tiles = list(picked) + [(b, t) for b in range(PASSES2) for t in range(PACK) if (b, t) not in picked]
         for a in range(PASSES2):
             for b, t in tiles:
                 if a == 0:
@@ -247,12 +230,18 @@ def tile_list_ant_trail_residual_kernel(tc, tab_words, tab_scales, offs, w1, pos
                     start=(a == 0),
                     stop=(a == PASSES2 - 1),
                 )
-        for b, t in tiles:
+        for i, (b, t) in enumerate(tiles):
             result = results[:, PACK * b + t, :]
-            if (b, t) in picked2:
-                nc.vector.scalar_tensor_tensor(out=result, in0=y[b, t][:], scalar=1.0, in1=picked2[b, t], op0=ALU.add, op1=ALU.mult)
-            else:
-                factor = keep.tile([P, M], F32, name="factor%d%d" % (b, t), align_bytes=64)
-                nc.scalar.activation(out=factor[:], in_=y[b, t][:], func=ACT.Identity, bias=1.0)
-                nc.vector.tensor_tensor(out=result, in0=h_on[b, t].indirect(pos2_t[:]), in1=factor[:], op=ALU.mult)
-            nc.sync.dma_start(out=out_rows[b, t], in_=result)
+            if (b, t) in picked and i >= 1:
+                nc.vector.scalar_tensor_tensor(out=result, in0=y[b, t][:], scalar=1.0, in1=picked[b, t], op0=ALU.add, op1=ALU.mult)
+                nc.sync.dma_start(out=out_rows[b, t], in_=result)
+                continue
+            factor = keep.tile([P, M], F32, name="factor%d%d" % (b, t), align_bytes=64)
+            nc.scalar.activation(out=factor[:], in_=y[b, t][:], func=ACT.Identity, bias=1.0)
+            if (b, t) in picked:
+                nc.gpsimd.tensor_tensor(out=result, in0=picked[b, t], in1=factor[:], op=ALU.mult)
+                nc.sync.dma_start(out=out_rows[b, t], in_=result)
+                continue
+            for cols in halves if i == len(tiles) - 1 else [slice(0, M)]:
+                nc.vector.tensor_tensor(out=result[:, cols], in0=h_on[b, t].indirect(pos2_t[:, cols.start // 16 : cols.stop // 16]), in1=factor[:, cols], op=ALU.mult)
+                nc.sync.dma_start(out=out_rows[b, t][:, cols], in_=result[:, cols])

@@ -24,6 +24,7 @@ PASSES1 = K // K_PASS
 PASSES2 = H // K_PASS
 HALF = M // 2
 VECTOR_SHARE = (42, 48)
+EARLY_PASSES = 5
 
 
 def tile_list_ant_trail_residual_kernel(tc, tab_words, tab_scales, offs, w1, pos1, pos2, gain, w2_words, w2_scales, out):
@@ -187,10 +188,11 @@ def tile_list_ant_trail_residual_kernel(tc, tab_words, tab_scales, offs, w1, pos
         quantise_w1(1, 0, "stage1")
         quantise_w1(1, 2, "stage0")
         x0 = pick1(0)
+        pick2(keep.tile([P, 1, M], F32, name="picked_first", align_bytes=64), [(0, 2)])
         first_passes(1, (1, 0, 2))
 
         silu0 = keep.tile([P, M, PACK], F32, name="silu0", tag="raw_last", align_bytes=64)
-        late = keep.tile([P, PACK + 3, M], F32, name="late", tag="stage2", align_bytes=64)
+        late = keep.tile([P, PACK + 2, M], F32, name="late", tag="stage2", align_bytes=64)
         scaled0 = late[:, :PACK, :].rearrange("p a (c t) -> p (a c) t", t=PACK)
         z0 = keep.tile([P, M, PACK], BF16, name="z0", tag="z", align_bytes=64)
         for cols in halves:
@@ -200,7 +202,7 @@ def tile_list_ant_trail_residual_kernel(tc, tab_words, tab_scales, offs, w1, pos
         x1 = pick1(1)
         pick2(keep.tile([P, 2, M], F32, name="picked_mid", align_bytes=64), [(1, 1), (1, 2)])
 
-        silu1 = keep.tile([P, PACK, M], F32, name="silu1", tag="x0", align_bytes=64)
+        silu1 = keep.tile([P, PACK, M], F32, name="silu1", tag="stage0", align_bytes=64)
         for t in range(PACK):
             nc.scalar.activation(out=silu1[:, t, :], in_=x1[:, t, :], func=ACT.Silu)
         quantise_z(0, z0, "x1")
@@ -210,26 +212,28 @@ def tile_list_ant_trail_residual_kernel(tc, tab_words, tab_scales, offs, w1, pos
             weave(squares, silu1, cols, ACT.Square)
             nc.vector.tensor_tensor(out=z1[:, cols, :], in0=squares[:, cols, :], in1=gains(1), op=ALU.mult)
         quantise_z(1, z1, "z_sc1")
-        pick2(late[:, PACK:, :], [(0, 0), (0, 1), (0, 2)])
+        pick2(late[:, PACK:, :], [(0, 0), (0, 1)])
         pick2(keep.tile([P, 1, M], F32, name="picked_last", tag="squares", align_bytes=64), [(1, 3)])
 
         results = keep.tile([P, PASSES2 * PACK, M], F32, name="results", tag="tab0", align_bytes=64)
         out_rows = out.rearrange("(b p t) m -> b t p m", p=P, t=PACK)
         tiles = list(picked) + [(b, t) for b in range(PASSES2) for t in range(PACK) if (b, t) not in picked]
-        for a in range(PASSES2):
-            for b, t in tiles:
-                if a == 0:
-                    y[b, t] = psum.tile([P, BANK], F32, name="bank%d" % (PACK * b + t))
-                c0 = b * K_PASS + t * P
-                nc.tensor.matmul_mx(
-                    out=y[b, t][:],
-                    lhsT=w2_w[:, a, 2 * c0 : 2 * (c0 + P)].bitcast(FP4X4),
-                    lhsT_scale=w2_sc[:, a, c0 : c0 + P],
-                    rhs=z_codes[a][:].bitcast(FP8X4),
-                    rhs_scale=z_sc[a][:],
-                    start=(a == 0),
-                    stop=(a == PASSES2 - 1),
-                )
+        passes = [(a, tile) for a in range(PASSES2) for tile in tiles[:EARLY_PASSES]]
+        passes = passes + [(a, tile) for tile in tiles[EARLY_PASSES:] for a in reversed(range(PASSES2))]
+        for a, (b, t) in passes:
+            first = (b, t) not in y
+            if first:
+                y[b, t] = psum.tile([P, BANK], F32, name="bank%d" % (PACK * b + t))
+            c0 = b * K_PASS + t * P
+            nc.tensor.matmul_mx(
+                out=y[b, t][:],
+                lhsT=w2_w[:, a, 2 * c0 : 2 * (c0 + P)].bitcast(FP4X4),
+                lhsT_scale=w2_sc[:, a, c0 : c0 + P],
+                rhs=z_codes[a][:].bitcast(FP8X4),
+                rhs_scale=z_sc[a][:],
+                start=first,
+                stop=not first,
+            )
         for i, (b, t) in enumerate(tiles):
             result = results[:, PACK * b + t, :]
             if (b, t) in picked and i >= 1:
@@ -240,7 +244,7 @@ def tile_list_ant_trail_residual_kernel(tc, tab_words, tab_scales, offs, w1, pos
             nc.scalar.activation(out=factor[:], in_=y[b, t][:], func=ACT.Identity, bias=1.0)
             if (b, t) in picked:
                 nc.gpsimd.tensor_tensor(out=result, in0=picked[b, t], in1=factor[:], op=ALU.mult)
-                nc.sync.dma_start(out=out_rows[b, t], in_=result)
+                nc.scalar.dma_start(out=out_rows[b, t], in_=result)
                 continue
             for cols in halves if i == len(tiles) - 1 else [slice(0, M)]:
                 nc.vector.tensor_tensor(out=result[:, cols], in0=h_on[b, t].indirect(pos2_t[:, cols.start // 16 : cols.stop // 16]), in1=factor[:, cols], op=ALU.mult)

@@ -89,7 +89,6 @@ def tile_list_ant_trail_residual_kernel(tc, tab_words, tab_scales, offs, w1, pos
         load_w1(0, 0)
         load_tab(1)
         nc.sync.dma_start(pos1_t[:], pos1)
-        nc.sync.dma_start(pos2_t[:], pos2)
         place_rows(0)
         load_w1(0, 1)
         load_tab(2)
@@ -151,7 +150,7 @@ def tile_list_ant_trail_residual_kernel(tc, tab_words, tab_scales, offs, w1, pos
                 nc.vector.tensor_copy(out=picked[b, t], in_=h_on[b, t].indirect(pos2_t[:]))
 
         def weave(dst, src, cols, func):
-            nc.scalar.activation(out=dst[:, cols, :].rearrange("p (c i) t -> p c t i", i=4), in_=src[:, :, cols].rearrange("p t (c i) -> p c t i", i=4), func=func)
+            nc.scalar.activation(out=dst[:, cols, :].rearrange("p (c i) t -> p c t i", i=2), in_=src[:, :, cols].rearrange("p t (c i) -> p c t i", i=2), func=func)
 
         def gains(b):
             return gain_t[:, b, :].unsqueeze(1).to_broadcast([P, HALF, PACK])
@@ -178,7 +177,9 @@ def tile_list_ant_trail_residual_kernel(tc, tab_words, tab_scales, offs, w1, pos
             out=w2_w[:].bitcast(U16).rearrange("p a (b t m) -> p (a b) m t", t=PACK, m=P),
             in_=w2_raw[:].bitcast(U16).rearrange("p a (b m t) -> p (a b) m t", t=PACK, m=P),
         )
-        for a in range(PASSES1):
+        load_w1(1, 0)
+        nc.sync.dma_start(pos2_t[:], pos2)
+        for a in range(1, PASSES1):
             load_w1(1, a)
         nc.sync.dma_start(out=gain_t[:], in_=gain.rearrange("(b p t) -> p b t", p=P, t=PACK))
         for q in range(4):

@@ -23,8 +23,8 @@ BANK = 512
 PASSES1 = K // K_PASS
 PASSES2 = H // K_PASS
 HALF = M // 2
-VECTOR_SHARE = (42, 48)
-EARLY_PASSES = 5
+VECTOR_SHARE = 42
+QUARTER = M // 4
 
 
 def tile_list_ant_trail_residual_kernel(tc, tab_words, tab_scales, offs, w1, pos1, pos2, gain, w2_words, w2_scales, out):
@@ -32,6 +32,7 @@ def tile_list_ant_trail_residual_kernel(tc, tab_words, tab_scales, offs, w1, pos
     with ExitStack() as ctx:
         keep = ctx.enter_context(tc.tile_pool(name="keep", bufs=1))
         raws = ctx.enter_context(tc.tile_pool(name="raws", bufs=4))
+        laid = ctx.enter_context(tc.tile_pool(name="laid", bufs=1))
         psum = ctx.enter_context(tc.psum_pool(name="psum", bufs=1))
 
         offs_t = keep.tile([P, S // 16], U16, name="offs_t")
@@ -55,7 +56,11 @@ def tile_list_ant_trail_residual_kernel(tc, tab_words, tab_scales, offs, w1, pos
         nc.vector.memset(warm[:], 0.0)
         nc.scalar.activation(out=warm[:], in_=warm[:], func=ACT.Silu)
 
-        raw, w_codes, w_sc, banks, h, h_on, z_codes, z_sc, picked, y = {}, {}, {}, {}, {}, {}, {}, {}, {}, {}
+        raw, w_codes, w_sc, banks, h, x, z_codes, z_sc, picked, y = {}, {}, {}, {}, {}, {}, {}, {}, {}, {}
+
+        for b in range(PASSES2):
+            for a in range(PASSES1):
+                w_codes[b, a] = keep.tile([P, K_PASS], U32, name="w_codes%d%d" % (b, a), align_bytes=64)
 
         def load_tab(a):
             nc.sync.dma_start(out=tab[a][:].bitcast(I32), in_=tab_words[a].rearrange("p t i -> p (t i)").bitcast(I32))
@@ -65,7 +70,7 @@ def tile_list_ant_trail_residual_kernel(tc, tab_words, tab_scales, offs, w1, pos
             raw[b, a] = []
             for part in range(parts):
                 if (b, a) == (1, PASSES1 - 1):
-                    piece = keep.tile([P, PACK, width], F32, name="raw_last", align_bytes=64)
+                    piece = keep.tile([P, PACK, width], F32, name="raw_last%d" % part, align_bytes=64)
                 else:
                     piece = raws.tile([P, PACK, width], F32, name="raw")
                 c0 = b * K_PASS + part * width
@@ -97,27 +102,38 @@ def tile_list_ant_trail_residual_kernel(tc, tab_words, tab_scales, offs, w1, pos
         place_rows(2)
         nc.sync.dma_start(out=w2_raw[:], in_=w2_words.rearrange("a p n -> p a n").bitcast(I32))
 
-        def quantise_w1(b, a, scale_tag):
-            rounded = keep.tile([P, PACK * K_PASS], BF16, name="rounded", tag="stage%d" % a, align_bytes=64)
-            dst = rounded[:].rearrange("p (t m j) -> p m j t", t=PACK, j=PACK)
+        def woven_w1(rounded, tiles):
+            return rounded[:, :].rearrange("p (t m j) -> p m j t", t=tiles, j=PACK)
+
+        def planar_w1(piece):
+            return piece[:].rearrange("p j (m t) -> p m j t", t=PACK)
+
+        def gpsimd_round(dst, src):
+            nc.gpsimd.tensor_scalar(out=dst.rearrange("p m j t -> p m t j"), in0=src.rearrange("p m j t -> p m t j"), scalar1=1.0, scalar2=0.0, op0=ALU.mult, op1=ALU.add)
+
+        def quantise(b, a, rounded, c0, width, step):
+            for c in range(0, width, step):
+                cols = slice(c0 + c, c0 + c + step)
+                nc.vector.quantize_mx(out=w_codes[b, a][:, cols].bitcast(FP8X4), scales=w_sc[b, a][:, cols], in_=rounded[:, PACK * c : PACK * (c + step)])
+
+        def quantise_first(a):
+            rounded = keep.tile([P, PACK * K_PASS], BF16, name="rounded%d" % a, align_bytes=64)
+            dst = woven_w1(rounded, PACK)
             last = a == PASSES1 - 1
             m0 = 0
-            for piece in raw[b, a]:
-                src = piece[:].rearrange("p j (m t) -> p m j t", t=PACK)
+            for piece in raw[0, a]:
+                src = planar_w1(piece)
                 count = src.shape[1]
-                if (b, a) == (1, 0):
-                    nc.gpsimd.tensor_scalar(out=dst.rearrange("p m j t -> p m t j"), in0=src.rearrange("p m j t -> p m t j"), scalar1=1.0, scalar2=0.0, op0=ALU.mult, op1=ALU.add)
-                else:
-                    share = VECTOR_SHARE[b] if last and m0 + count == P else 0
-                    if share:
-                        nc.vector.tensor_copy(out=dst[:, m0 : m0 + share], in_=src[:, :share])
-                    nc.scalar.copy(out=dst[:, m0 + share : m0 + count], in_=src[:, share:])
+                share = VECTOR_SHARE if last and m0 + count == P else 0
+                if share:
+                    nc.vector.tensor_copy(out=dst[:, m0 : m0 + share], in_=src[:, :share])
+                nc.scalar.copy(out=dst[:, m0 + share : m0 + count], in_=src[:, share:])
                 m0 = m0 + count
-            w_codes[b, a] = keep.tile([P, K_PASS], U32, name="w_codes%d%d" % (b, a), align_bytes=64)
-            w_sc[b, a] = keep.tile([P, K_PASS], U8, name="w_sc%d%d" % (b, a), tag=scale_tag, align_bytes=64)
-            step = P if last else K_PASS
-            for c0 in range(0, K_PASS, step):
-                nc.vector.quantize_mx(out=w_codes[b, a][:, c0 : c0 + step].bitcast(FP8X4), scales=w_sc[b, a][:, c0 : c0 + step], in_=rounded[:, PACK * c0 : PACK * (c0 + step)])
+            w_sc[0, a] = keep.tile([P, K_PASS], U8, name="w_sc0%d" % a, align_bytes=64)
+            quantise(0, a, rounded, 0, K_PASS, P if last else K_PASS)
+
+        def at(name, cols, dtype, offset):
+            return laid.tile([P, cols], dtype, name=name, offset=offset, align_bytes=64)
 
         def first_passes(b, order):
             for t in range(PACK):
@@ -136,41 +152,41 @@ def tile_list_ant_trail_residual_kernel(tc, tab_words, tab_scales, offs, w1, pos
                             stop=(a == order[-1]),
                         )
 
-        def pick1(b):
-            x = keep.tile([P, PACK, M], F32, name="x%d" % b, align_bytes=64)
-            for t in range(PACK):
-                for half in range(2):
-                    nc.scalar.copy(out=h[b, t][:, half * BANK : (half + 1) * BANK], in_=banks[b, t, half][:])
-                nc.vector.tensor_copy(out=x[:, t, :], in_=h[b, t].indirect(pos1_t[:]))
-            return x
+        def pick1(b, t, into=None):
+            h[b, t] = keep.tile([P, S], F32, name="h%d%d" % (b, t), align_bytes=64)
+            for half in range(2):
+                nc.scalar.copy(out=h[b, t][:, half * BANK : (half + 1) * BANK], in_=banks[b, t, half][:])
+            x[b, t] = into if into is not None else keep.tile([P, M], F32, name="x%d%d" % (b, t), align_bytes=64)[:]
+            nc.vector.tensor_copy(out=x[b, t], in_=h[b, t][:].indirect(pos1_t[:]))
 
         def pick2(group, tiles):
             for i, (b, t) in enumerate(tiles):
-                picked[b, t] = group[:, i, :]
-                nc.vector.tensor_copy(out=picked[b, t], in_=h_on[b, t].indirect(pos2_t[:]))
+                picked[b, t] = group[:, i * M : (i + 1) * M]
+                nc.vector.tensor_copy(out=picked[b, t], in_=h[b, t][:].indirect(pos2_t[:]))
 
-        def weave(dst, src, cols, func):
-            nc.scalar.activation(out=dst[:, cols, :].rearrange("p (c i) t -> p c t i", i=2), in_=src[:, :, cols].rearrange("p t (c i) -> p c t i", i=2), func=func)
+        def silu(b, tag):
+            s = keep.tile([P, PACK, M], F32, name="silu%d" % b, tag=tag, align_bytes=64)
+            for t in range(PACK):
+                nc.scalar.activation(out=s[:, t, :], in_=x[b, t], func=ACT.Silu)
+            return s
 
-        def gains(b):
-            return gain_t[:, b, :].unsqueeze(1).to_broadcast([P, HALF, PACK])
+        def planar(tile, cols, run):
+            return tile[:, :, cols].rearrange("p t (c i) -> p c t i", i=run)
 
-        def quantise_z(b, z, scale_tag):
+        def woven(tile, cols, run):
+            return tile[:, cols, :].rearrange("p (c i) t -> p c t i", i=run)
+
+        def quantise_z(b, z, scales):
             z_codes[b] = keep.tile([P, M], U32, name="z_codes%d" % b, align_bytes=64)
-            z_sc[b] = keep.tile([P, M], U8, name="z_sc%d" % b, tag=scale_tag, align_bytes=64)
-            nc.vector.quantize_mx(out=z_codes[b][:].bitcast(FP8X4), scales=z_sc[b][:], in_=z[:].rearrange("p m t -> p (m t)"))
+            z_sc[b] = scales
+            nc.vector.quantize_mx(out=z_codes[b][:].bitcast(FP8X4), scales=z_sc[b][:], in_=z)
 
-        joined = keep.tile([P, PACK * S], F32, name="h1")
-        for t in range(PACK):
-            h[0, t] = keep.tile([P, S], F32, name="h0%d" % t)[:]
-            h_on[0, t] = h[0, t]
-            h[1, t] = joined[:, t * S : (t + 1) * S]
-            h_on[1, t] = joined[:, t * S :]
         halves = [slice(u * HALF, (u + 1) * HALF) for u in range(2)]
+        quarters = [slice(u * QUARTER, (u + 1) * QUARTER) for u in range(4)]
 
         for a in range(PASSES1):
             nc.vector.tensor_copy(out=v_words[a][:], in_=tab[a][:].indirect(offs_t[:]))
-            quantise_w1(0, a, "w_sc0%d" % a)
+            quantise_first(a)
         nc.vector.tensor_copy(out=w2_rows[:].rearrange("p a (b t m) -> p (a b) m t", t=PACK, m=P), in_=w2_sc_raw[:].rearrange("p a (b m t) -> p (a b) m t", t=PACK, m=P))
         first_passes(0, (0, 1, 2))
         nc.vector.tensor_copy(
@@ -179,74 +195,97 @@ def tile_list_ant_trail_residual_kernel(tc, tab_words, tab_scales, offs, w1, pos
         )
         load_w1(1, 0)
         nc.sync.dma_start(pos2_t[:], pos2)
-        for a in range(1, PASSES1):
-            load_w1(1, a)
+        load_w1(1, 1)
+        load_w1(1, 2, 2)
         nc.sync.dma_start(out=gain_t[:], in_=gain.rearrange("(b p t) -> p b t", p=P, t=PACK))
         for q in range(4):
             nc.sync.dma_start(out=w2_sc[32 * q : 32 * q + 4, :, :].bitcast(I32), in_=w2_rows[1 + 32 * q : 32 * q + 32 : 8, :, :].bitcast(I32))
 
-        quantise_w1(1, 1, "w_sc11")
-        quantise_w1(1, 0, "stage1")
-        quantise_w1(1, 2, "stage0")
-        x0 = pick1(0)
-        pick2(keep.tile([P, 1, M], F32, name="picked_first", align_bytes=64), [(0, 2)])
-        first_passes(1, (1, 0, 2))
+        pick1(0, 0)
+        pick1(0, 1)
+        r10 = at("r10", 8 * K_PASS, BF16, 2048)[:, : PACK * K_PASS]
+        gpsimd_round(woven_w1(r10, PACK), planar_w1(raw[1, 0][0]))
+        w_sc[1, 0] = keep.tile([P, K_PASS], U8, name="w_sc10", align_bytes=64)
+        quantise(1, 0, r10, 0, K_PASS, K_PASS)
+        x23 = at("x23", 2 * M, F32, 0)
+        pick1(0, 2, x23[:, :M])
+        pick1(0, 3, x23[:, M:])
+        r11 = at("r11", PACK * K_PASS, BF16, 4096)
+        gpsimd_round(woven_w1(r11, PACK), planar_w1(raw[1, 1][0]))
+        pick2(at("picked_a", M, F32, 8192), [(0, 3)])
+        r12 = at("r12", 8 * K_PASS, BF16, 19456)[:, : PACK * K_PASS]
+        nc.scalar.copy(out=woven_w1(r12, PACK)[:, : P // 2], in_=planar_w1(raw[1, 2][0]))
+        gpsimd_round(woven_w1(r12, PACK)[:, P // 2 :], planar_w1(raw[1, 2][1]))
+        w_sc[1, 1] = keep.tile([P, K_PASS], U8, name="w_sc11", tag="raw_last1", align_bytes=64)
+        quantise(1, 1, r11, 0, K_PASS, K_PASS)
+        w_sc[1, 2] = keep.tile([P, K_PASS], U8, name="w_sc12", align_bytes=64)
+        quantise(1, 2, r12, 0, K_PASS, K_PASS)
+        pick2(at("picked_b", M, F32, 20480), [(0, 0)])
+        first_passes(1, (0, 1, 2))
 
-        silu0 = keep.tile([P, M, PACK], F32, name="silu0", tag="raw_last", align_bytes=64)
-        late = keep.tile([P, PACK + 2, M], F32, name="late", tag="stage2", align_bytes=64)
-        scaled0 = late[:, :PACK, :].rearrange("p a (c t) -> p (a c) t", t=PACK)
-        z0 = keep.tile([P, M, PACK], BF16, name="z0", tag="z", align_bytes=64)
-        for cols in halves:
-            weave(silu0, x0, cols, ACT.Silu)
-            nc.gpsimd.tensor_tensor(out=scaled0[:, cols, :], in0=silu0[:, cols, :], in1=gains(0), op=ALU.mult)
-            nc.gpsimd.tensor_tensor(out=z0[:, cols, :], in0=scaled0[:, cols, :], in1=silu0[:, cols, :], op=ALU.mult)
-        x1 = pick1(1)
-        pick2(keep.tile([P, 2, M], F32, name="picked_mid", align_bytes=64), [(1, 1), (1, 2)])
+        def squares(b, s, parts, tag):
+            sq = keep.tile([P, M, PACK], F32, name="squares%d" % b, tag=tag, align_bytes=64)
+            for cols in parts:
+                nc.scalar.activation(out=woven(sq, cols, 2), in_=planar(s, cols, 2), func=ACT.Square)
+            return sq
 
-        silu1 = keep.tile([P, PACK, M], F32, name="silu1", tag="stage0", align_bytes=64)
-        for t in range(PACK):
-            nc.scalar.activation(out=silu1[:, t, :], in_=x1[:, t, :], func=ACT.Silu)
-        quantise_z(0, z0, "x1")
-        squares = keep.tile([P, M, PACK], F32, name="squares", align_bytes=64)
-        z1 = keep.tile([P, M, PACK], BF16, name="z1", tag="z", align_bytes=64)
-        for cols in halves:
-            weave(squares, silu1, cols, ACT.Square)
-            nc.vector.tensor_tensor(out=z1[:, cols, :], in0=squares[:, cols, :], in1=gains(1), op=ALU.mult)
-        quantise_z(1, z1, "z_sc1")
-        pick2(late[:, PACK:, :], [(0, 0), (0, 1)])
-        pick2(keep.tile([P, 1, M], F32, name="picked_last", tag="squares", align_bytes=64), [(1, 3)])
+        def gain_product(engine, b, z, sq, parts):
+            for cols in parts:
+                gains = gain_t[:, b, :].unsqueeze(1).to_broadcast([P, cols.stop - cols.start, PACK])
+                engine.tensor_tensor(out=z[:, :].rearrange("p (m t) -> p m t", t=PACK)[:, cols, :], in0=sq[:, cols, :], in1=gains, op=ALU.mult)
+
+        z0 = at("z0", 2 * PACK * M, BF16, 12288)[:, : PACK * M]
+        gain_product(nc.gpsimd, 0, z0, squares(0, silu(0, "raw_last0"), halves, "tab2"), halves)
+        for u in range(2):
+            pair = at("x1%d" % u, 2 * M, F32, 22528 + 4096 * u)
+            pick1(1, 2 * u, pair[:, :M])
+            pick1(1, 2 * u + 1, pair[:, M:])
+
+        silu1 = silu(1, "w_codes12")
+        quantise_z(0, z0, at("z_sc0", M, U8, 22528))
+        pick2(at("picked_c", 3 * M, F32, 14336), [(0, 1), (0, 2), (1, 0)])
+        z1 = at("z1", PACK * M, BF16, 10240)
+        parts = [slice(0, 144), slice(144, 288), slice(288, 400), slice(400, 512)]
+        squares1 = squares(1, silu1, parts, "tab1")
+        gain_product(nc.gpsimd, 1, z1, squares1, parts[:2])
+        gain_product(nc.vector, 1, z1, squares1, parts[2:])
+        quantise_z(1, z1[:], keep.tile([P, M], U8, name="z_sc1", align_bytes=64))
+        pick2(keep.tile([P, M], F32, name="picked_last", tag="tab1", align_bytes=64), [(1, 1)])
 
         results = keep.tile([P, PASSES2 * PACK, M], F32, name="results", tag="tab0", align_bytes=64)
         out_rows = out.rearrange("(b p t) m -> b t p m", p=P, t=PACK)
-        tiles = list(picked) + [(b, t) for b in range(PASSES2) for t in range(PACK) if (b, t) not in picked]
-        passes = [(a, tile) for a in range(PASSES2) for tile in tiles[:EARLY_PASSES]]
-        passes = passes + [(a, tile) for tile in tiles[EARLY_PASSES:] for a in reversed(range(PASSES2))]
-        for a, (b, t) in passes:
-            first = (b, t) not in y
-            if first:
-                y[b, t] = psum.tile([P, BANK], F32, name="bank%d" % (PACK * b + t))
-            c0 = b * K_PASS + t * P
-            nc.tensor.matmul_mx(
-                out=y[b, t][:],
-                lhsT=w2_w[:, a, 2 * c0 : 2 * (c0 + P)].bitcast(FP4X4),
-                lhsT_scale=w2_sc[:, a, c0 : c0 + P],
-                rhs=z_codes[a][:].bitcast(FP8X4),
-                rhs_scale=z_sc[a][:],
-                start=first,
-                stop=not first,
-            )
-        for i, (b, t) in enumerate(tiles):
+        early = list(picked)
+        by_gpsimd, by_vector = early[:2], early[2:]
+        fused = [(1, t) for t in range(PACK) if (1, t) not in picked]
+        tiles = by_gpsimd + by_vector[:1] + fused + by_vector[1:]
+        for a in range(PASSES2):
+            for b, t in tiles:
+                if a == 0:
+                    y[b, t] = psum.tile([P, BANK], F32, name="bank%d" % (PACK * b + t))
+                c0 = b * K_PASS + t * P
+                nc.tensor.matmul_mx(
+                    out=y[b, t][:],
+                    lhsT=w2_w[:, a, 2 * c0 : 2 * (c0 + P)].bitcast(FP4X4),
+                    lhsT_scale=w2_sc[:, a, c0 : c0 + P],
+                    rhs=z_codes[a][:].bitcast(FP8X4),
+                    rhs_scale=z_sc[a][:],
+                    start=(a == 0),
+                    stop=(a == PASSES2 - 1),
+                )
+        factor = {}
+        for b, t in by_gpsimd + fused:
+            factor[b, t] = keep.tile([P, M], F32, name="factor%d%d" % (b, t), align_bytes=64)
+            nc.scalar.activation(out=factor[b, t][:], in_=y[b, t][:], func=ACT.Identity, bias=1.0)
+        for b, t in by_gpsimd:
             result = results[:, PACK * b + t, :]
-            if (b, t) in picked and i >= 1:
-                nc.vector.scalar_tensor_tensor(out=result, in0=y[b, t][:], scalar=1.0, in1=picked[b, t], op0=ALU.add, op1=ALU.mult)
-                nc.sync.dma_start(out=out_rows[b, t], in_=result)
-                continue
-            factor = keep.tile([P, M], F32, name="factor%d%d" % (b, t), align_bytes=64)
-            nc.scalar.activation(out=factor[:], in_=y[b, t][:], func=ACT.Identity, bias=1.0)
-            if (b, t) in picked:
-                nc.gpsimd.tensor_tensor(out=result, in0=picked[b, t], in1=factor[:], op=ALU.mult)
-                nc.scalar.dma_start(out=out_rows[b, t], in_=result)
-                continue
-            for cols in halves if i == len(tiles) - 1 else [slice(0, M)]:
-                nc.vector.tensor_tensor(out=result[:, cols], in0=h_on[b, t].indirect(pos2_t[:, cols.start // 16 : cols.stop // 16]), in1=factor[:, cols], op=ALU.mult)
+            nc.gpsimd.tensor_tensor(out=result, in0=picked[b, t], in1=factor[b, t][:], op=ALU.mult)
+            nc.scalar.dma_start(out=out_rows[b, t], in_=result)
+        for b, t in by_vector:
+            result = results[:, PACK * b + t, :]
+            nc.vector.scalar_tensor_tensor(out=result, in0=y[b, t][:], scalar=1.0, in1=picked[b, t], op0=ALU.add, op1=ALU.mult)
+            nc.sync.dma_start(out=out_rows[b, t], in_=result)
+        for b, t in fused:
+            result = results[:, PACK * b + t, :]
+            for cols in halves if (b, t) == fused[-1] else [slice(0, M)]:
+                nc.vector.tensor_tensor(out=result[:, cols], in0=h[b, t][:].indirect(pos2_t[:, cols.start // 16 : cols.stop // 16]), in1=factor[b, t][:, cols], op=ALU.mult)
                 nc.sync.dma_start(out=out_rows[b, t][:, cols], in_=result[:, cols])

@@ -70,7 +70,7 @@ def tile_list_ant_trail_residual_kernel(tc, tab_words, tab_scales, offs, w1, pos
             raw[b, a] = []
             for part in range(parts):
                 if (b, a) == (1, PASSES1 - 1):
-                    piece = keep.tile([P, PACK, width], F32, name="raw_last%d" % part, align_bytes=64)
+                    piece = laid.tile([P, PACK, width], F32, name="raw_last", offset=0, align_bytes=64)
                 else:
                     piece = raws.tile([P, PACK, width], F32, name="raw")
                 c0 = b * K_PASS + part * width
@@ -196,59 +196,63 @@ def tile_list_ant_trail_residual_kernel(tc, tab_words, tab_scales, offs, w1, pos
         load_w1(1, 0)
         nc.sync.dma_start(pos2_t[:], pos2)
         load_w1(1, 1)
-        load_w1(1, 2, 2)
+        load_w1(1, 2)
         nc.sync.dma_start(out=gain_t[:], in_=gain.rearrange("(b p t) -> p b t", p=P, t=PACK))
         for q in range(4):
             nc.sync.dma_start(out=w2_sc[32 * q : 32 * q + 4, :, :].bitcast(I32), in_=w2_rows[1 + 32 * q : 32 * q + 32 : 8, :, :].bitcast(I32))
 
-        pick1(0, 0)
-        pick1(0, 1)
-        r10 = at("r10", 8 * K_PASS, BF16, 2048)[:, : PACK * K_PASS]
+        x0 = keep.tile([P, PACK, M], F32, name="x0", align_bytes=64)
+        for t in range(PACK):
+            pick1(0, t, x0[:, t, :])
+        r10 = at("r10", 8 * K_PASS, BF16, 11264)[:, : PACK * K_PASS]
         gpsimd_round(woven_w1(r10, PACK), planar_w1(raw[1, 0][0]))
         w_sc[1, 0] = keep.tile([P, K_PASS], U8, name="w_sc10", align_bytes=64)
         quantise(1, 0, r10, 0, K_PASS, K_PASS)
-        x23 = at("x23", 2 * M, F32, 0)
-        pick1(0, 2, x23[:, :M])
-        pick1(0, 3, x23[:, M:])
-        r11 = at("r11", PACK * K_PASS, BF16, 4096)
-        gpsimd_round(woven_w1(r11, PACK), planar_w1(raw[1, 1][0]))
-        pick2(at("picked_a", M, F32, 8192), [(0, 3)])
-        r12 = at("r12", 8 * K_PASS, BF16, 19456)[:, : PACK * K_PASS]
-        nc.scalar.copy(out=woven_w1(r12, PACK)[:, : P // 2], in_=planar_w1(raw[1, 2][0]))
-        gpsimd_round(woven_w1(r12, PACK)[:, P // 2 :], planar_w1(raw[1, 2][1]))
-        w_sc[1, 1] = keep.tile([P, K_PASS], U8, name="w_sc11", tag="raw_last1", align_bytes=64)
+        pick2(at("picked_a", 2 * M, F32, 8704), [(0, 0), (0, 1)])
+        r11 = keep.tile([P, PACK * K_PASS], BF16, name="r11", tag="rounded0", align_bytes=64)
+        nc.scalar.copy(out=woven_w1(r11, PACK), in_=planar_w1(raw[1, 1][0]))
+        r12a = keep.tile([P, 2 * K_PASS], BF16, name="r12a", tag="rounded1", align_bytes=64)
+        nc.scalar.copy(out=woven_w1(r12a, 2), in_=planar_w1(raw[1, 2][0])[:, :, :, :2])
+        r12b = at("r12b", 12 * K_PASS, BF16, 18432)[:, : 2 * K_PASS]
+        gpsimd_round(woven_w1(r12b, 2), planar_w1(raw[1, 2][0])[:, :, :, 2:])
+        w_sc[1, 1] = at("w_sc11", K_PASS, U8, 0)
         quantise(1, 1, r11, 0, K_PASS, K_PASS)
         w_sc[1, 2] = keep.tile([P, K_PASS], U8, name="w_sc12", align_bytes=64)
-        quantise(1, 2, r12, 0, K_PASS, K_PASS)
-        pick2(at("picked_b", M, F32, 20480), [(0, 0)])
+        quantise(1, 2, r12a, 0, 2 * P, 2 * P)
+        quantise(1, 2, r12b, 2 * P, 2 * P, 2 * P)
+        pick2(at("picked_b", 2 * M, F32, 19456), [(0, 2), (0, 3)])
         first_passes(1, (0, 1, 2))
 
-        def squares(b, s, parts, tag):
-            sq = keep.tile([P, M, PACK], F32, name="squares%d" % b, tag=tag, align_bytes=64)
-            for cols in parts:
-                nc.scalar.activation(out=woven(sq, cols, 2), in_=planar(s, cols, 2), func=ACT.Square)
-            return sq
+        def product(engine, dst, src, other):
+            engine.tensor_tensor(out=dst, in0=src, in1=other, op=ALU.mult)
 
-        def gain_product(engine, b, z, sq, parts):
-            for cols in parts:
-                gains = gain_t[:, b, :].unsqueeze(1).to_broadcast([P, cols.stop - cols.start, PACK])
-                engine.tensor_tensor(out=z[:, :].rearrange("p (m t) -> p m t", t=PACK)[:, cols, :], in0=sq[:, cols, :], in1=gains, op=ALU.mult)
+        def gains(b, cols):
+            return gain_t[:, b, :].unsqueeze(1).to_broadcast([P, cols.stop - cols.start, PACK])
 
-        z0 = at("z0", 2 * PACK * M, BF16, 12288)[:, : PACK * M]
-        gain_product(nc.gpsimd, 0, z0, squares(0, silu(0, "raw_last0"), halves, "tab2"), halves)
-        for u in range(2):
-            pair = at("x1%d" % u, 2 * M, F32, 22528 + 4096 * u)
-            pick1(1, 2 * u, pair[:, :M])
-            pick1(1, 2 * u + 1, pair[:, M:])
+        silu0 = laid.tile([P, M, PACK], F32, name="silu0", offset=512, align_bytes=64)
+        for cols in halves:
+            nc.scalar.activation(out=woven(silu0, cols, 2), in_=planar(x0, cols, 2), func=ACT.Silu)
+        z0 = at("z0", PACK * M, BF16, 15360)
+        z0_w = z0[:].rearrange("p (m t) -> p m t", t=PACK)
+        part0 = at("part0", PACK * M, F32, 27648)[:].rearrange("p (m t) -> p m t", t=PACK)
+        both, squared = halves
+        nc.scalar.activation(out=part0[:, squared, :], in_=silu0[:, squared, :], func=ACT.Square)
+        product(nc.gpsimd, part0[:, both, :], silu0[:, both, :], gains(0, both))
+        product(nc.gpsimd, z0_w[:, both, :], part0[:, both, :], silu0[:, both, :])
+        product(nc.gpsimd, z0_w[:, squared, :], part0[:, squared, :], gains(0, squared))
+        pairs = [at("x1a", 2 * M, F32, 23552), keep.tile([P, 2 * M], F32, name="x1b", align_bytes=64)]
+        for t in range(PACK):
+            pick1(1, t, pairs[t // 2][:, (t % 2) * M : (t % 2 + 1) * M])
 
         silu1 = silu(1, "w_codes12")
-        quantise_z(0, z0, at("z_sc0", M, U8, 22528))
-        pick2(at("picked_c", 3 * M, F32, 14336), [(0, 1), (0, 2), (1, 0)])
-        z1 = at("z1", PACK * M, BF16, 10240)
-        parts = [slice(0, 144), slice(144, 288), slice(288, 400), slice(400, 512)]
-        squares1 = squares(1, silu1, parts, "tab1")
-        gain_product(nc.gpsimd, 1, z1, squares1, parts[:2])
-        gain_product(nc.vector, 1, z1, squares1, parts[2:])
+        quantise_z(0, z0[:], at("z_sc0", M, U8, 23552))
+        pick2(at("picked_c", M, F32, 17408), [(1, 0)])
+        z1 = at("z1", PACK * M, BF16, 13312)
+        z1_w = z1[:].rearrange("p (m t) -> p m t", t=PACK)
+        squares1 = keep.tile([P, M, PACK], F32, name="squares1", tag="tab1", align_bytes=64)
+        for cols in quarters:
+            nc.scalar.activation(out=woven(squares1, cols, 2), in_=planar(silu1, cols, 2), func=ACT.Square)
+            product(nc.vector, z1_w[:, cols, :], squares1[:, cols, :], gains(1, cols))
         quantise_z(1, z1[:], keep.tile([P, M], U8, name="z_sc1", align_bytes=64))
         pick2(keep.tile([P, M], F32, name="picked_last", tag="tab1", align_bytes=64), [(1, 1)])
 

@@ -24,11 +24,36 @@ PASSES1 = K // K_PASS
 PASSES2 = H // K_PASS
 HALF = M // 2
 VECTOR_SHARE = 42
+GPSIMD_SHARE = 40
 QUARTER = M // 4
+WIDTH = {F32: 4, BF16: 2, U8: 1}
+LAID = [
+    ("raw_mid", 8192, [("w_sc10", 512, [])]),
+    ("raw_last", 8192, [("silu0", 8192, []), ("w_sc11", 512, [])]),
+    ("r10", 4096, [
+        ("picked_a", 2048, []),
+        ("r12", 4096, [
+            ("z0", 4096, [("z1", 4096, []), ("picked_d", 2048, [])]),
+            ("picked_b", 6144, []),
+            ("x1a", 4096, [("z_sc0", 512, [])]),
+            ("part0", 8192, []),
+        ]),
+    ]),
+]
+
+
+def lay(tiles, offset, places):
+    for name, size, over in tiles:
+        span = max(size, lay(over, offset, places) - offset)
+        places[name] = (offset, span)
+        offset = offset + span
+    return offset
 
 
 def tile_list_ant_trail_residual_kernel(tc, tab_words, tab_scales, offs, w1, pos1, pos2, gain, w2_words, w2_scales, out):
     nc = tc.nc
+    places = {}
+    lay(LAID, 0, places)
     with ExitStack() as ctx:
         keep = ctx.enter_context(tc.tile_pool(name="keep", bufs=1))
         raws = ctx.enter_context(tc.tile_pool(name="raws", bufs=4))
@@ -56,6 +81,10 @@ def tile_list_ant_trail_residual_kernel(tc, tab_words, tab_scales, offs, w1, pos
         nc.vector.memset(warm[:], 0.0)
         nc.scalar.activation(out=warm[:], in_=warm[:], func=ACT.Silu)
 
+        def at(name, cols, dtype):
+            offset, span = places[name]
+            return laid.tile([P, span // WIDTH[dtype]], dtype, name=name, offset=offset, align_bytes=64)[:, :cols]
+
         raw, w_codes, w_sc, banks, h, x, z_codes, z_sc, picked, y = {}, {}, {}, {}, {}, {}, {}, {}, {}, {}
 
         for b in range(PASSES2):
@@ -69,44 +98,44 @@ def tile_list_ant_trail_residual_kernel(tc, tab_words, tab_scales, offs, w1, pos
             width = K_PASS // parts
             raw[b, a] = []
             for part in range(parts):
-                if (b, a) == (1, PASSES1 - 1):
-                    piece = laid.tile([P, PACK, width], F32, name="raw_last", offset=0, align_bytes=64)
+                if b == 1 and a > 0:
+                    piece = at("raw_mid" if a == 1 else "raw_last", PACK * width, F32).rearrange("p (j c) -> p j c", j=PACK)
                 else:
-                    piece = raws.tile([P, PACK, width], F32, name="raw")
+                    piece = raws.tile([P, PACK, width], F32, name="raw")[:]
                 c0 = b * K_PASS + part * width
-                nc.sync.dma_start(out=piece[:], in_=w1[a * K_PASS : (a + 1) * K_PASS, c0 : c0 + width].rearrange("(p j) c -> p j c", j=PACK))
+                nc.sync.dma_start(out=piece, in_=w1[a * K_PASS : (a + 1) * K_PASS, c0 : c0 + width].rearrange("(p j) c -> p j c", j=PACK))
                 raw[b, a].append(piece)
 
         staged = ((0, 4), (64, 4), (2, 8))
 
-        def place_rows(a):
-            first, step = staged[a]
-            for q in range(4):
+        def place_rows(planes):
+            for a, q in planes:
+                first, step = staged[a]
                 row = first + 4 * q * step
                 nc.sync.dma_start(out=v_sc[a][32 * q + 4 * a : 32 * q + 4 * a + 4, :].bitcast(I32), in_=v_rows[row : row + 3 * step + 1 : step, :].bitcast(I32))
 
+        planes = [(a, q) for a in (0, 2, 1) for q in range(4)]
         load_tab(0)
         nc.sync.dma_start(out=tab_sc[0:128:4, :].bitcast(I32), in_=tab_scales[0:2].rearrange("a q t -> (a q) t").bitcast(I32))
         nc.sync.dma_start(out=tab_sc[2:128:8, :].bitcast(I32), in_=tab_scales[2].bitcast(I32))
         nc.sync.dma_start(offs_t[:], offs)
         nc.sync.dma_start(out=w2_sc_raw[1:128:8, :, :].bitcast(I32), in_=w2_scales.rearrange("a q n -> q a n").bitcast(I32))
         nc.vector.tensor_copy(out=v_rows[:], in_=tab_sc[:].indirect(offs_t[:]))
-        load_w1(0, 0)
         load_tab(1)
-        nc.sync.dma_start(pos1_t[:], pos1)
-        place_rows(0)
+        load_w1(0, 0)
+        place_rows(planes[:6])
         load_w1(0, 1)
+        place_rows(planes[6:7])
         load_tab(2)
-        place_rows(1)
+        place_rows(planes[7:])
         load_w1(0, 2, 2)
-        place_rows(2)
         nc.sync.dma_start(out=w2_raw[:], in_=w2_words.rearrange("a p n -> p a n").bitcast(I32))
 
         def woven_w1(rounded, tiles):
             return rounded[:, :].rearrange("p (t m j) -> p m j t", t=tiles, j=PACK)
 
         def planar_w1(piece):
-            return piece[:].rearrange("p j (m t) -> p m j t", t=PACK)
+            return piece.rearrange("p j (m t) -> p m j t", t=PACK)
 
         def gpsimd_round(dst, src):
             nc.gpsimd.tensor_scalar(out=dst.rearrange("p m j t -> p m t j"), in0=src.rearrange("p m j t -> p m t j"), scalar1=1.0, scalar2=0.0, op0=ALU.mult, op1=ALU.add)
@@ -132,8 +161,6 @@ def tile_list_ant_trail_residual_kernel(tc, tab_words, tab_scales, offs, w1, pos
             w_sc[0, a] = keep.tile([P, K_PASS], U8, name="w_sc0%d" % a, align_bytes=64)
             quantise(0, a, rounded, 0, K_PASS, P if last else K_PASS)
 
-        def at(name, cols, dtype, offset):
-            return laid.tile([P, cols], dtype, name=name, offset=offset, align_bytes=64)
 
         def first_passes(b, order):
             for t in range(PACK):
@@ -193,6 +220,7 @@ def tile_list_ant_trail_residual_kernel(tc, tab_words, tab_scales, offs, w1, pos
             out=w2_w[:].bitcast(U16).rearrange("p a (b t m) -> p (a b) m t", t=PACK, m=P),
             in_=w2_raw[:].bitcast(U16).rearrange("p a (b m t) -> p (a b) m t", t=PACK, m=P),
         )
+        nc.sync.dma_start(pos1_t[:], pos1)
         load_w1(1, 0)
         nc.sync.dma_start(pos2_t[:], pos2)
         load_w1(1, 1)
@@ -204,23 +232,22 @@ def tile_list_ant_trail_residual_kernel(tc, tab_words, tab_scales, offs, w1, pos
         x0 = keep.tile([P, PACK, M], F32, name="x0", align_bytes=64)
         for t in range(PACK):
             pick1(0, t, x0[:, t, :])
-        r10 = at("r10", 8 * K_PASS, BF16, 11264)[:, : PACK * K_PASS]
+        r10 = at("r10", PACK * K_PASS, BF16)
         gpsimd_round(woven_w1(r10, PACK), planar_w1(raw[1, 0][0]))
-        w_sc[1, 0] = keep.tile([P, K_PASS], U8, name="w_sc10", align_bytes=64)
-        quantise(1, 0, r10, 0, K_PASS, K_PASS)
-        pick2(at("picked_a", 2 * M, F32, 8704), [(0, 0), (0, 1)])
         r11 = keep.tile([P, PACK * K_PASS], BF16, name="r11", tag="rounded0", align_bytes=64)
-        nc.scalar.copy(out=woven_w1(r11, PACK), in_=planar_w1(raw[1, 1][0]))
-        r12a = keep.tile([P, 2 * K_PASS], BF16, name="r12a", tag="rounded1", align_bytes=64)
-        nc.scalar.copy(out=woven_w1(r12a, 2), in_=planar_w1(raw[1, 2][0])[:, :, :, :2])
-        r12b = at("r12b", 12 * K_PASS, BF16, 18432)[:, : 2 * K_PASS]
-        gpsimd_round(woven_w1(r12b, 2), planar_w1(raw[1, 2][0])[:, :, :, 2:])
-        w_sc[1, 1] = at("w_sc11", K_PASS, U8, 0)
+        gpsimd_round(woven_w1(r11, PACK)[:, :GPSIMD_SHARE], planar_w1(raw[1, 1][0])[:, :GPSIMD_SHARE])
+        nc.scalar.copy(out=woven_w1(r11, PACK)[:, GPSIMD_SHARE:], in_=planar_w1(raw[1, 1][0])[:, GPSIMD_SHARE:])
+        w_sc[1, 0] = at("w_sc10", K_PASS, U8)
+        quantise(1, 0, r10, 0, K_PASS, K_PASS)
+        pick2(at("picked_a", M, F32), [(0, 0)])
+        r12 = at("r12", PACK * K_PASS, BF16)
+        gpsimd_round(woven_w1(r12, PACK)[:, :GPSIMD_SHARE], planar_w1(raw[1, 2][0])[:, :GPSIMD_SHARE])
+        nc.scalar.copy(out=woven_w1(r12, PACK)[:, GPSIMD_SHARE:], in_=planar_w1(raw[1, 2][0])[:, GPSIMD_SHARE:])
+        w_sc[1, 1] = at("w_sc11", K_PASS, U8)
         quantise(1, 1, r11, 0, K_PASS, K_PASS)
         w_sc[1, 2] = keep.tile([P, K_PASS], U8, name="w_sc12", align_bytes=64)
-        quantise(1, 2, r12a, 0, 2 * P, 2 * P)
-        quantise(1, 2, r12b, 2 * P, 2 * P, 2 * P)
-        pick2(at("picked_b", 2 * M, F32, 19456), [(0, 2), (0, 3)])
+        quantise(1, 2, r12, 0, K_PASS, K_PASS)
+        pick2(at("picked_b", 3 * M, F32), [(0, 1), (0, 2), (0, 3)])
         first_passes(1, (0, 1, 2))
 
         def product(engine, dst, src, other):
@@ -229,31 +256,32 @@ def tile_list_ant_trail_residual_kernel(tc, tab_words, tab_scales, offs, w1, pos
         def gains(b, cols):
             return gain_t[:, b, :].unsqueeze(1).to_broadcast([P, cols.stop - cols.start, PACK])
 
-        silu0 = laid.tile([P, M, PACK], F32, name="silu0", offset=512, align_bytes=64)
+        silu0 = at("silu0", PACK * M, F32).rearrange("p (m t) -> p m t", t=PACK)
         for cols in halves:
             nc.scalar.activation(out=woven(silu0, cols, 2), in_=planar(x0, cols, 2), func=ACT.Silu)
-        z0 = at("z0", PACK * M, BF16, 15360)
-        z0_w = z0[:].rearrange("p (m t) -> p m t", t=PACK)
-        part0 = at("part0", PACK * M, F32, 27648)[:].rearrange("p (m t) -> p m t", t=PACK)
-        both, squared = halves
+        z0 = at("z0", PACK * M, BF16)
+        z0_w = z0.rearrange("p (m t) -> p m t", t=PACK)
+        part0 = at("part0", PACK * M, F32).rearrange("p (m t) -> p m t", t=PACK)
+        squared = quarters[-1]
         nc.scalar.activation(out=part0[:, squared, :], in_=silu0[:, squared, :], func=ACT.Square)
-        product(nc.gpsimd, part0[:, both, :], silu0[:, both, :], gains(0, both))
-        product(nc.gpsimd, z0_w[:, both, :], part0[:, both, :], silu0[:, both, :])
+        for both in (halves[0], quarters[2]):
+            product(nc.gpsimd, part0[:, both, :], silu0[:, both, :], gains(0, both))
+            product(nc.gpsimd, z0_w[:, both, :], part0[:, both, :], silu0[:, both, :])
         product(nc.gpsimd, z0_w[:, squared, :], part0[:, squared, :], gains(0, squared))
-        pairs = [at("x1a", 2 * M, F32, 23552), keep.tile([P, 2 * M], F32, name="x1b", align_bytes=64)]
+        pairs = [at("x1a", 2 * M, F32), keep.tile([P, 2 * M], F32, name="x1b", align_bytes=64)]
         for t in range(PACK):
             pick1(1, t, pairs[t // 2][:, (t % 2) * M : (t % 2 + 1) * M])
 
         silu1 = silu(1, "w_codes12")
-        quantise_z(0, z0[:], at("z_sc0", M, U8, 23552))
-        pick2(at("picked_c", M, F32, 17408), [(1, 0)])
-        z1 = at("z1", PACK * M, BF16, 13312)
-        z1_w = z1[:].rearrange("p (m t) -> p m t", t=PACK)
+        quantise_z(0, z0, at("z_sc0", M, U8))
+        pick2(at("picked_d", M, F32), [(1, 0)])
+        z1 = at("z1", PACK * M, BF16)
+        z1_w = z1.rearrange("p (m t) -> p m t", t=PACK)
         squares1 = keep.tile([P, M, PACK], F32, name="squares1", tag="tab1", align_bytes=64)
         for cols in quarters:
             nc.scalar.activation(out=woven(squares1, cols, 2), in_=planar(silu1, cols, 2), func=ACT.Square)
             product(nc.vector, z1_w[:, cols, :], squares1[:, cols, :], gains(1, cols))
-        quantise_z(1, z1[:], keep.tile([P, M], U8, name="z_sc1", align_bytes=64))
+        quantise_z(1, z1, keep.tile([P, M], U8, name="z_sc1", align_bytes=64))
         pick2(keep.tile([P, M], F32, name="picked_last", tag="tab1", align_bytes=64), [(1, 1)])
 
         results = keep.tile([P, PASSES2 * PACK, M], F32, name="results", tag="tab0", align_bytes=64)
@@ -276,13 +304,14 @@ def tile_list_ant_trail_residual_kernel(tc, tab_words, tab_scales, offs, w1, pos
                     start=(a == 0),
                     stop=(a == PASSES2 - 1),
                 )
+        factors = keep.tile([P, len(by_gpsimd + fused), M], F32, name="factors", tag="tab2", align_bytes=64)
         factor = {}
-        for b, t in by_gpsimd + fused:
-            factor[b, t] = keep.tile([P, M], F32, name="factor%d%d" % (b, t), align_bytes=64)
-            nc.scalar.activation(out=factor[b, t][:], in_=y[b, t][:], func=ACT.Identity, bias=1.0)
+        for i, (b, t) in enumerate(by_gpsimd + fused):
+            factor[b, t] = factors[:, i, :]
+            nc.scalar.activation(out=factor[b, t], in_=y[b, t][:], func=ACT.Identity, bias=1.0)
         for b, t in by_gpsimd:
             result = results[:, PACK * b + t, :]
-            nc.gpsimd.tensor_tensor(out=result, in0=picked[b, t], in1=factor[b, t][:], op=ALU.mult)
+            nc.gpsimd.tensor_tensor(out=result, in0=picked[b, t], in1=factor[b, t], op=ALU.mult)
             nc.scalar.dma_start(out=out_rows[b, t], in_=result)
         for b, t in by_vector:
             result = results[:, PACK * b + t, :]

@@ -24,17 +24,16 @@ PASSES1 = K // K_PASS
 PASSES2 = H // K_PASS
 HALF = M // 2
 VECTOR_SHARE = 42
-GPSIMD_SHARE = 40
+GPSIMD_SHARE = 64
 QUARTER = M // 4
 WIDTH = {F32: 4, BF16: 2, U8: 1}
 LAID = [
-    ("raw_mid", 8192, [("w_sc10", 512, [])]),
     ("raw_last", 8192, [("silu0", 8192, []), ("w_sc11", 512, [])]),
     ("r10", 4096, [
-        ("picked_a", 2048, []),
+        ("picked_a", 4096, []),
         ("r12", 4096, [
             ("z0", 4096, [("z1", 4096, []), ("picked_d", 2048, [])]),
-            ("picked_b", 6144, []),
+            ("picked_b", 4096, []),
             ("x1a", 4096, [("z_sc0", 512, [])]),
             ("part0", 8192, []),
         ]),
@@ -98,8 +97,8 @@ def tile_list_ant_trail_residual_kernel(tc, tab_words, tab_scales, offs, w1, pos
             width = K_PASS // parts
             raw[b, a] = []
             for part in range(parts):
-                if b == 1 and a > 0:
-                    piece = at("raw_mid" if a == 1 else "raw_last", PACK * width, F32).rearrange("p (j c) -> p j c", j=PACK)
+                if (b, a) == (1, PASSES1 - 1):
+                    piece = at("raw_last", PACK * width, F32).rearrange("p (j c) -> p j c", j=PACK)
                 else:
                     piece = raws.tile([P, PACK, width], F32, name="raw")[:]
                 c0 = b * K_PASS + part * width
@@ -235,11 +234,10 @@ def tile_list_ant_trail_residual_kernel(tc, tab_words, tab_scales, offs, w1, pos
         r10 = at("r10", PACK * K_PASS, BF16)
         gpsimd_round(woven_w1(r10, PACK), planar_w1(raw[1, 0][0]))
         r11 = keep.tile([P, PACK * K_PASS], BF16, name="r11", tag="rounded0", align_bytes=64)
-        gpsimd_round(woven_w1(r11, PACK)[:, :GPSIMD_SHARE], planar_w1(raw[1, 1][0])[:, :GPSIMD_SHARE])
-        nc.scalar.copy(out=woven_w1(r11, PACK)[:, GPSIMD_SHARE:], in_=planar_w1(raw[1, 1][0])[:, GPSIMD_SHARE:])
-        w_sc[1, 0] = at("w_sc10", K_PASS, U8)
+        nc.scalar.copy(out=woven_w1(r11, PACK), in_=planar_w1(raw[1, 1][0]))
+        w_sc[1, 0] = keep.tile([P, K_PASS], U8, name="w_sc10", align_bytes=64)
         quantise(1, 0, r10, 0, K_PASS, K_PASS)
-        pick2(at("picked_a", M, F32), [(0, 0)])
+        pick2(at("picked_a", 2 * M, F32), [(0, 0), (0, 1)])
         r12 = at("r12", PACK * K_PASS, BF16)
         gpsimd_round(woven_w1(r12, PACK)[:, :GPSIMD_SHARE], planar_w1(raw[1, 2][0])[:, :GPSIMD_SHARE])
         nc.scalar.copy(out=woven_w1(r12, PACK)[:, GPSIMD_SHARE:], in_=planar_w1(raw[1, 2][0])[:, GPSIMD_SHARE:])
@@ -247,7 +245,7 @@ def tile_list_ant_trail_residual_kernel(tc, tab_words, tab_scales, offs, w1, pos
         quantise(1, 1, r11, 0, K_PASS, K_PASS)
         w_sc[1, 2] = keep.tile([P, K_PASS], U8, name="w_sc12", align_bytes=64)
         quantise(1, 2, r12, 0, K_PASS, K_PASS)
-        pick2(at("picked_b", 3 * M, F32), [(0, 1), (0, 2), (0, 3)])
+        pick2(at("picked_b", 2 * M, F32), [(0, 2), (0, 3)])
         first_passes(1, (0, 1, 2))
 
         def product(engine, dst, src, other):
@@ -262,11 +260,10 @@ def tile_list_ant_trail_residual_kernel(tc, tab_words, tab_scales, offs, w1, pos
         z0 = at("z0", PACK * M, BF16)
         z0_w = z0.rearrange("p (m t) -> p m t", t=PACK)
         part0 = at("part0", PACK * M, F32).rearrange("p (m t) -> p m t", t=PACK)
-        squared = quarters[-1]
+        both, squared = halves
         nc.scalar.activation(out=part0[:, squared, :], in_=silu0[:, squared, :], func=ACT.Square)
-        for both in (halves[0], quarters[2]):
-            product(nc.gpsimd, part0[:, both, :], silu0[:, both, :], gains(0, both))
-            product(nc.gpsimd, z0_w[:, both, :], part0[:, both, :], silu0[:, both, :])
+        product(nc.gpsimd, part0[:, both, :], silu0[:, both, :], gains(0, both))
+        product(nc.gpsimd, z0_w[:, both, :], part0[:, both, :], silu0[:, both, :])
         product(nc.gpsimd, z0_w[:, squared, :], part0[:, squared, :], gains(0, squared))
         pairs = [at("x1a", 2 * M, F32), keep.tile([P, 2 * M], F32, name="x1b", align_bytes=64)]
         for t in range(PACK):
@@ -287,7 +284,7 @@ def tile_list_ant_trail_residual_kernel(tc, tab_words, tab_scales, offs, w1, pos
         results = keep.tile([P, PASSES2 * PACK, M], F32, name="results", tag="tab0", align_bytes=64)
         out_rows = out.rearrange("(b p t) m -> b t p m", p=P, t=PACK)
         early = list(picked)
-        by_gpsimd, by_vector = early[:2], early[2:]
+        by_gpsimd, by_vector = early[:1], early[1:]
         fused = [(1, t) for t in range(PACK) if (1, t) not in picked]
         tiles = by_gpsimd + by_vector[:1] + fused + by_vector[1:]
         for a in range(PASSES2):

@@ -28,15 +28,13 @@ GPSIMD_SHARE = 64
 QUARTER = M // 4
 WIDTH = {F32: 4, BF16: 2, U8: 1}
 LAID = [
+    ("raw_first", 8192, [("picked_a", 4096, [])]),
     ("raw_last", 8192, [("silu0", 8192, []), ("w_sc11", 512, [])]),
-    ("r10", 4096, [
-        ("picked_a", 4096, []),
-        ("r12", 4096, [
-            ("z0", 4096, [("z1", 4096, []), ("picked_d", 2048, [])]),
-            ("picked_b", 4096, []),
-            ("x1a", 4096, [("z_sc0", 512, [])]),
-            ("part0", 8192, []),
-        ]),
+    ("r12", 4096, [
+        ("z0", 4096, [("z1", 4096, []), ("picked_d", 2048, [])]),
+        ("picked_b", 4096, []),
+        ("x1a", 4096, [("z_sc0", 512, [])]),
+        ("part0", 8192, []),
     ]),
 ]
 
@@ -55,7 +53,7 @@ def tile_list_ant_trail_residual_kernel(tc, tab_words, tab_scales, offs, w1, pos
     lay(LAID, 0, places)
     with ExitStack() as ctx:
         keep = ctx.enter_context(tc.tile_pool(name="keep", bufs=1))
-        raws = ctx.enter_context(tc.tile_pool(name="raws", bufs=4))
+        raws = ctx.enter_context(tc.tile_pool(name="raws", bufs=3))
         laid = ctx.enter_context(tc.tile_pool(name="laid", bufs=1))
         psum = ctx.enter_context(tc.psum_pool(name="psum", bufs=1))
 
@@ -97,8 +95,8 @@ def tile_list_ant_trail_residual_kernel(tc, tab_words, tab_scales, offs, w1, pos
             width = K_PASS // parts
             raw[b, a] = []
             for part in range(parts):
-                if (b, a) == (1, PASSES1 - 1):
-                    piece = at("raw_last", PACK * width, F32).rearrange("p (j c) -> p j c", j=PACK)
+                if b == 1 and a != 1:
+                    piece = at("raw_last" if a else "raw_first", PACK * width, F32).rearrange("p (j c) -> p j c", j=PACK)
                 else:
                     piece = raws.tile([P, PACK, width], F32, name="raw")[:]
                 c0 = b * K_PASS + part * width
@@ -178,17 +176,23 @@ def tile_list_ant_trail_residual_kernel(tc, tab_words, tab_scales, offs, w1, pos
                             stop=(a == order[-1]),
                         )
 
-        def pick1(b, t, into=None):
-            h[b, t] = keep.tile([P, S], F32, name="h%d%d" % (b, t), align_bytes=64)
+        def pick1(b, t, into=None, window=None):
+            if window is None:
+                window = keep.tile([P, S], F32, name="h%d%d" % (b, t), align_bytes=64)[:]
+            h[b, t] = window[:, :S]
             for half in range(2):
-                nc.scalar.copy(out=h[b, t][:, half * BANK : (half + 1) * BANK], in_=banks[b, t, half][:])
+                cols = slice(half * BANK, (half + 1) * BANK)
+                if (b, t, half) == (1, 0, 1):
+                    nc.vector.tensor_copy(out=h[b, t][:, cols], in_=banks[b, t, half][:])
+                else:
+                    nc.scalar.copy(out=h[b, t][:, cols], in_=banks[b, t, half][:])
             x[b, t] = into if into is not None else keep.tile([P, M], F32, name="x%d%d" % (b, t), align_bytes=64)[:]
-            nc.vector.tensor_copy(out=x[b, t], in_=h[b, t][:].indirect(pos1_t[:]))
+            nc.vector.tensor_copy(out=x[b, t], in_=window.indirect(pos1_t[:]))
 
         def pick2(group, tiles):
             for i, (b, t) in enumerate(tiles):
                 picked[b, t] = group[:, i * M : (i + 1) * M]
-                nc.vector.tensor_copy(out=picked[b, t], in_=h[b, t][:].indirect(pos2_t[:]))
+                nc.vector.tensor_copy(out=picked[b, t], in_=h[b, t].indirect(pos2_t[:]))
 
         def silu(b, tag):
             s = keep.tile([P, PACK, M], F32, name="silu%d" % b, tag=tag, align_bytes=64)
@@ -229,14 +233,16 @@ def tile_list_ant_trail_residual_kernel(tc, tab_words, tab_scales, offs, w1, pos
             nc.sync.dma_start(out=w2_sc[32 * q : 32 * q + 4, :, :].bitcast(I32), in_=w2_rows[1 + 32 * q : 32 * q + 32 : 8, :, :].bitcast(I32))
 
         x0 = keep.tile([P, PACK, M], F32, name="x0", align_bytes=64)
-        for t in range(PACK):
+        for t in range(PACK - 1):
             pick1(0, t, x0[:, t, :])
-        r10 = at("r10", PACK * K_PASS, BF16)
+        wide = keep.tile([P, 2 * S], F32, name="h03", align_bytes=64)
+        r10 = wide[:, S:].bitcast(BF16)
         gpsimd_round(woven_w1(r10, PACK), planar_w1(raw[1, 0][0]))
         r11 = keep.tile([P, PACK * K_PASS], BF16, name="r11", tag="rounded0", align_bytes=64)
         nc.scalar.copy(out=woven_w1(r11, PACK), in_=planar_w1(raw[1, 1][0]))
         w_sc[1, 0] = keep.tile([P, K_PASS], U8, name="w_sc10", align_bytes=64)
         quantise(1, 0, r10, 0, K_PASS, K_PASS)
+        pick1(0, 3, x0[:, 3, :], wide[:])
         pick2(at("picked_a", 2 * M, F32), [(0, 0), (0, 1)])
         r12 = at("r12", PACK * K_PASS, BF16)
         gpsimd_round(woven_w1(r12, PACK)[:, :GPSIMD_SHARE], planar_w1(raw[1, 2][0])[:, :GPSIMD_SHARE])
@@ -286,7 +292,7 @@ def tile_list_ant_trail_residual_kernel(tc, tab_words, tab_scales, offs, w1, pos
         early = list(picked)
         by_gpsimd, by_vector = early[:1], early[1:]
         fused = [(1, t) for t in range(PACK) if (1, t) not in picked]
-        tiles = by_gpsimd + by_vector[:1] + fused + by_vector[1:]
+        tiles = early[:3] + fused + early[3:]
         for a in range(PASSES2):
             for b, t in tiles:
                 if a == 0:
@@ -317,5 +323,5 @@ def tile_list_ant_trail_residual_kernel(tc, tab_words, tab_scales, offs, w1, pos
         for b, t in fused:
             result = results[:, PACK * b + t, :]
             for cols in halves if (b, t) == fused[-1] else [slice(0, M)]:
-                nc.vector.tensor_tensor(out=result[:, cols], in0=h[b, t][:].indirect(pos2_t[:, cols.start // 16 : cols.stop // 16]), in1=factor[b, t][:, cols], op=ALU.mult)
+                nc.vector.tensor_tensor(out=result[:, cols], in0=h[b, t].indirect(pos2_t[:, cols.start // 16 : cols.stop // 16]), in1=factor[b, t][:, cols], op=ALU.mult)
                 nc.sync.dma_start(out=out_rows[b, t][:, cols], in_=result[:, cols])

@@ -24,15 +24,16 @@ PASSES1 = K // K_PASS
 PASSES2 = H // K_PASS
 HALF = M // 2
 VECTOR_SHARE = 42
-GPSIMD_SHARE = 64
+GPSIMD_SHARE = 52
 QUARTER = M // 4
 WIDTH = {F32: 4, BF16: 2, U8: 1}
 LAID = [
-    ("raw_first", 8192, [("picked_a", 4096, [])]),
+    ("raw_first", 8192, [("picked_a", 2048, [])]),
     ("raw_last", 8192, [("silu0", 8192, []), ("w_sc11", 512, [])]),
     ("r12", 4096, [
         ("z0", 4096, [("z1", 4096, []), ("picked_d", 2048, [])]),
-        ("picked_b", 4096, []),
+        ("picked_b", 6144, []),
+        ("w2_w1", 2048, []),
         ("x1a", 4096, [("z_sc0", 512, [])]),
         ("part0", 8192, []),
     ]),
@@ -62,7 +63,6 @@ def tile_list_ant_trail_residual_kernel(tc, tab_words, tab_scales, offs, w1, pos
         pos2_t = keep.tile([P, M // 16], U16, name="pos2_t")
         tab = [keep.tile([P, T], U32, name="tab%d" % a, align_bytes=64) for a in range(PASSES1)]
         tab_sc = keep.tile([P, T], U8, name="tab_sc", align_bytes=64)
-        w2_raw = keep.tile([P, PASSES2, H // 2], I32, name="w2_raw", align_bytes=64)
         w2_sc_raw = keep.tile([P, PASSES2, H], U8, name="w2_sc_raw", align_bytes=64)
         gain_t = keep.tile([P, PASSES2, PACK], F32, name="gain_t")
         v_rows = keep.tile([P, S], U8, name="v_rows", align_bytes=64)
@@ -70,7 +70,6 @@ def tile_list_ant_trail_residual_kernel(tc, tab_words, tab_scales, offs, w1, pos
         w2_rows = keep.tile([P, PASSES2, H], U8, name="w2_rows", align_bytes=64)
         w2_sc = keep.tile([P, PASSES2, H], U8, name="w2_sc", align_bytes=64)
         v_words = [keep.tile([P, S], U32, name="v_words%d" % a, align_bytes=64) for a in range(PASSES1)]
-        w2_w = keep.tile([P, PASSES2, 2 * H], U8, name="w2_w", align_bytes=64)
 
         for plane in [tab_sc, w2_sc_raw] + v_sc + [w2_sc]:
             nc.vector.memset(plane[:].bitcast(I32), 0)
@@ -82,7 +81,7 @@ def tile_list_ant_trail_residual_kernel(tc, tab_words, tab_scales, offs, w1, pos
             offset, span = places[name]
             return laid.tile([P, span // WIDTH[dtype]], dtype, name=name, offset=offset, align_bytes=64)[:, :cols]
 
-        raw, w_codes, w_sc, banks, h, x, z_codes, z_sc, picked, y = {}, {}, {}, {}, {}, {}, {}, {}, {}, {}
+        raw, w_codes, w_sc, banks, h, x, z_codes, z_sc, picked, y, w2_w, w2_raw = {}, {}, {}, {}, {}, {}, {}, {}, {}, {}, {}, {}
 
         for b in range(PASSES2):
             for a in range(PASSES1):
@@ -126,7 +125,6 @@ def tile_list_ant_trail_residual_kernel(tc, tab_words, tab_scales, offs, w1, pos
         load_tab(2)
         place_rows(planes[7:])
         load_w1(0, 2, 2)
-        nc.sync.dma_start(out=w2_raw[:], in_=w2_words.rearrange("a p n -> p a n").bitcast(I32))
 
         def woven_w1(rounded, tiles):
             return rounded[:, :].rearrange("p (t m j) -> p m j t", t=tiles, j=PACK)
@@ -159,6 +157,19 @@ def tile_list_ant_trail_residual_kernel(tc, tab_words, tab_scales, offs, w1, pos
             quantise(0, a, rounded, 0, K_PASS, P if last else K_PASS)
 
 
+        def load_w2(a):
+            w2_raw[a] = keep.tile([P, H // 2], I32, name="w2_raw%d" % a, align_bytes=64)
+            nc.sync.dma_start(out=w2_raw[a][:], in_=w2_words[a].bitcast(I32))
+
+        def reorder_w2(engine, a, into):
+            w2_w[a] = into
+            engine.tensor_copy(
+                out=into.bitcast(U16).rearrange("p (b t m) -> p b m t", t=PACK, m=P),
+                in_=w2_raw[a][:].bitcast(U16).rearrange("p (b m t) -> p b m t", t=PACK, m=P),
+            )
+
+        load_w2(0)
+
         def first_passes(b, order):
             for t in range(PACK):
                 for a in order:
@@ -182,7 +193,7 @@ def tile_list_ant_trail_residual_kernel(tc, tab_words, tab_scales, offs, w1, pos
             h[b, t] = window[:, :S]
             for half in range(2):
                 cols = slice(half * BANK, (half + 1) * BANK)
-                if (b, t, half) == (1, 0, 1):
+                if (b, t, half) == (0, 0, 1):
                     nc.vector.tensor_copy(out=h[b, t][:, cols], in_=banks[b, t, half][:])
                 else:
                     nc.scalar.copy(out=h[b, t][:, cols], in_=banks[b, t, half][:])
@@ -219,15 +230,13 @@ def tile_list_ant_trail_residual_kernel(tc, tab_words, tab_scales, offs, w1, pos
             quantise_first(a)
         nc.vector.tensor_copy(out=w2_rows[:].rearrange("p a (b t m) -> p (a b) m t", t=PACK, m=P), in_=w2_sc_raw[:].rearrange("p a (b m t) -> p (a b) m t", t=PACK, m=P))
         first_passes(0, (0, 1, 2))
-        nc.vector.tensor_copy(
-            out=w2_w[:].bitcast(U16).rearrange("p a (b t m) -> p (a b) m t", t=PACK, m=P),
-            in_=w2_raw[:].bitcast(U16).rearrange("p a (b m t) -> p (a b) m t", t=PACK, m=P),
-        )
+        reorder_w2(nc.vector, 0, keep.tile([P, 2 * H], U8, name="w2_w0", align_bytes=64)[:])
         nc.sync.dma_start(pos1_t[:], pos1)
         load_w1(1, 0)
         nc.sync.dma_start(pos2_t[:], pos2)
         load_w1(1, 1)
         load_w1(1, 2)
+        load_w2(1)
         nc.sync.dma_start(out=gain_t[:], in_=gain.rearrange("(b p t) -> p b t", p=P, t=PACK))
         for q in range(4):
             nc.sync.dma_start(out=w2_sc[32 * q : 32 * q + 4, :, :].bitcast(I32), in_=w2_rows[1 + 32 * q : 32 * q + 32 : 8, :, :].bitcast(I32))
@@ -243,7 +252,7 @@ def tile_list_ant_trail_residual_kernel(tc, tab_words, tab_scales, offs, w1, pos
         w_sc[1, 0] = keep.tile([P, K_PASS], U8, name="w_sc10", align_bytes=64)
         quantise(1, 0, r10, 0, K_PASS, K_PASS)
         pick1(0, 3, x0[:, 3, :], wide[:])
-        pick2(at("picked_a", 2 * M, F32), [(0, 0), (0, 1)])
+        pick2(at("picked_a", M, F32), [(0, 0)])
         r12 = at("r12", PACK * K_PASS, BF16)
         gpsimd_round(woven_w1(r12, PACK)[:, :GPSIMD_SHARE], planar_w1(raw[1, 2][0])[:, :GPSIMD_SHARE])
         nc.scalar.copy(out=woven_w1(r12, PACK)[:, GPSIMD_SHARE:], in_=planar_w1(raw[1, 2][0])[:, GPSIMD_SHARE:])
@@ -251,7 +260,8 @@ def tile_list_ant_trail_residual_kernel(tc, tab_words, tab_scales, offs, w1, pos
         quantise(1, 1, r11, 0, K_PASS, K_PASS)
         w_sc[1, 2] = keep.tile([P, K_PASS], U8, name="w_sc12", align_bytes=64)
         quantise(1, 2, r12, 0, K_PASS, K_PASS)
-        pick2(at("picked_b", 2 * M, F32), [(0, 2), (0, 3)])
+        pick2(at("picked_b", 3 * M, F32), [(0, 1), (0, 2), (0, 3)])
+        reorder_w2(nc.vector, 1, at("w2_w1", 2 * H, U8))
         first_passes(1, (0, 1, 2))
 
         def product(engine, dst, src, other):
@@ -300,7 +310,7 @@ def tile_list_ant_trail_residual_kernel(tc, tab_words, tab_scales, offs, w1, pos
                 c0 = b * K_PASS + t * P
                 nc.tensor.matmul_mx(
                     out=y[b, t][:],
-                    lhsT=w2_w[:, a, 2 * c0 : 2 * (c0 + P)].bitcast(FP4X4),
+                    lhsT=w2_w[a][:, 2 * c0 : 2 * (c0 + P)].bitcast(FP4X4),
                     lhsT_scale=w2_sc[:, a, c0 : c0 + P],
                     rhs=z_codes[a][:].bitcast(FP8X4),
                     rhs_scale=z_sc[a][:],

@@ -31,11 +31,10 @@ LAID = [
     ("raw_first", 8192, [("picked_a", 2048, [])]),
     ("raw_last", 8192, [("silu0", 8192, []), ("w_sc11", 512, [])]),
     ("r12", 4096, [
-        ("z0", 4096, [("z1", 4096, []), ("picked_d", 2048, [])]),
+        ("z0", 4096, [("z1", 4096, []), ("picked_d", 2048, []), ("w2_w11", 1024, [])]),
         ("picked_b", 6144, []),
-        ("w2_w1", 2048, []),
         ("x1a", 4096, [("z_sc0", 512, [])]),
-        ("part0", 8192, []),
+        ("part0", 8192, [("w2_w10", 1024, [])]),
     ]),
 ]
 
@@ -161,11 +160,11 @@ def tile_list_ant_trail_residual_kernel(tc, tab_words, tab_scales, offs, w1, pos
             w2_raw[a] = keep.tile([P, H // 2], I32, name="w2_raw%d" % a, align_bytes=64)
             nc.sync.dma_start(out=w2_raw[a][:], in_=w2_words[a].bitcast(I32))
 
-        def reorder_w2(engine, a, into):
-            w2_w[a] = into
+        def reorder_w2(engine, order, a, b, into):
+            w2_w[a, b] = into
             engine.tensor_copy(
-                out=into.bitcast(U16).rearrange("p (b t m) -> p b m t", t=PACK, m=P),
-                in_=w2_raw[a][:].bitcast(U16).rearrange("p (b m t) -> p b m t", t=PACK, m=P),
+                out=into.bitcast(U16).rearrange("p (t m) -> p %s" % order, t=PACK),
+                in_=w2_raw[a][:].bitcast(U16)[:, b * K_PASS : (b + 1) * K_PASS].rearrange("p (m t) -> p %s" % order, t=PACK),
             )
 
         load_w2(0)
@@ -230,7 +229,8 @@ def tile_list_ant_trail_residual_kernel(tc, tab_words, tab_scales, offs, w1, pos
             quantise_first(a)
         nc.vector.tensor_copy(out=w2_rows[:].rearrange("p a (b t m) -> p (a b) m t", t=PACK, m=P), in_=w2_sc_raw[:].rearrange("p a (b m t) -> p (a b) m t", t=PACK, m=P))
         first_passes(0, (0, 1, 2))
-        reorder_w2(nc.vector, 0, keep.tile([P, 2 * H], U8, name="w2_w0", align_bytes=64)[:])
+        for b in range(PASSES2):
+            reorder_w2(nc.vector, "m t", 0, b, keep.tile([P, H], U8, name="w2_w0%d" % b, align_bytes=64)[:])
         nc.sync.dma_start(pos1_t[:], pos1)
         load_w1(1, 0)
         nc.sync.dma_start(pos2_t[:], pos2)
@@ -261,7 +261,6 @@ def tile_list_ant_trail_residual_kernel(tc, tab_words, tab_scales, offs, w1, pos
         w_sc[1, 2] = keep.tile([P, K_PASS], U8, name="w_sc12", align_bytes=64)
         quantise(1, 2, r12, 0, K_PASS, K_PASS)
         pick2(at("picked_b", 3 * M, F32), [(0, 1), (0, 2), (0, 3)])
-        reorder_w2(nc.vector, 1, at("w2_w1", 2 * H, U8))
         first_passes(1, (0, 1, 2))
 
         def product(engine, dst, src, other):
@@ -281,6 +280,7 @@ def tile_list_ant_trail_residual_kernel(tc, tab_words, tab_scales, offs, w1, pos
         product(nc.gpsimd, part0[:, both, :], silu0[:, both, :], gains(0, both))
         product(nc.gpsimd, z0_w[:, both, :], part0[:, both, :], silu0[:, both, :])
         product(nc.gpsimd, z0_w[:, squared, :], part0[:, squared, :], gains(0, squared))
+        reorder_w2(nc.gpsimd, "t m", 1, 0, at("w2_w10", H, U8))
         pairs = [at("x1a", 2 * M, F32), keep.tile([P, 2 * M], F32, name="x1b", align_bytes=64)]
         for t in range(PACK):
             pick1(1, t, pairs[t // 2][:, (t % 2) * M : (t % 2 + 1) * M])
@@ -288,6 +288,7 @@ def tile_list_ant_trail_residual_kernel(tc, tab_words, tab_scales, offs, w1, pos
         silu1 = silu(1, "w_codes12")
         quantise_z(0, z0, at("z_sc0", M, U8))
         pick2(at("picked_d", M, F32), [(1, 0)])
+        reorder_w2(nc.gpsimd, "t m", 1, 1, at("w2_w11", H, U8))
         z1 = at("z1", PACK * M, BF16)
         z1_w = z1.rearrange("p (m t) -> p m t", t=PACK)
         squares1 = keep.tile([P, M, PACK], F32, name="squares1", tag="tab1", align_bytes=64)
@@ -310,7 +311,7 @@ def tile_list_ant_trail_residual_kernel(tc, tab_words, tab_scales, offs, w1, pos
                 c0 = b * K_PASS + t * P
                 nc.tensor.matmul_mx(
                     out=y[b, t][:],
-                    lhsT=w2_w[a][:, 2 * c0 : 2 * (c0 + P)].bitcast(FP4X4),
+                    lhsT=w2_w[a, b][:, 2 * t * P : 2 * (t + 1) * P].bitcast(FP4X4),
                     lhsT_scale=w2_sc[:, a, c0 : c0 + P],
                     rhs=z_codes[a][:].bitcast(FP8X4),
                     rhs_scale=z_sc[a][:],

@@ -25,6 +25,7 @@ PASSES2 = H // K_PASS
 HALF = M // 2
 VECTOR_SHARE = 42
 GPSIMD_SHARE = 52
+GPSIMD_EARLY_SHARE = 22
 QUARTER = M // 4
 WIDTH = {F32: 4, BF16: 2, U8: 1}
 LAID = [
@@ -248,7 +249,8 @@ def tile_list_ant_trail_residual_kernel(tc, tab_words, tab_scales, offs, w1, pos
         r10 = wide[:, S:].bitcast(BF16)
         gpsimd_round(woven_w1(r10, PACK), planar_w1(raw[1, 0][0]))
         r11 = keep.tile([P, PACK * K_PASS], BF16, name="r11", tag="rounded0", align_bytes=64)
-        nc.scalar.copy(out=woven_w1(r11, PACK), in_=planar_w1(raw[1, 1][0]))
+        gpsimd_round(woven_w1(r11, PACK)[:, :GPSIMD_EARLY_SHARE], planar_w1(raw[1, 1][0])[:, :GPSIMD_EARLY_SHARE])
+        nc.scalar.copy(out=woven_w1(r11, PACK)[:, GPSIMD_EARLY_SHARE:], in_=planar_w1(raw[1, 1][0])[:, GPSIMD_EARLY_SHARE:])
         w_sc[1, 0] = keep.tile([P, K_PASS], U8, name="w_sc10", align_bytes=64)
         quantise(1, 0, r10, 0, K_PASS, K_PASS)
         pick1(0, 3, x0[:, 3, :], wide[:])

@@ -24,19 +24,15 @@ PASSES1 = K // K_PASS
 PASSES2 = H // K_PASS
 HALF = M // 2
 VECTOR_SHARE = 42
-GPSIMD_SHARE = 52
+GPSIMD_SHARE = 56
 GPSIMD_EARLY_SHARE = 22
 QUARTER = M // 4
 WIDTH = {F32: 4, BF16: 2, U8: 1}
 LAID = [
-    ("raw_first", 8192, [("picked_a", 2048, [])]),
+    ("raw_first", 8192, [("x03", 2048, []), ("picked_a", 2048, [])]),
     ("raw_last", 8192, [("silu0", 8192, []), ("w_sc11", 512, [])]),
-    ("r12", 4096, [
-        ("z0", 4096, [("z1", 4096, []), ("picked_d", 2048, []), ("w2_w11", 1024, [])]),
-        ("picked_b", 6144, []),
-        ("x1a", 4096, [("z_sc0", 512, [])]),
-        ("part0", 8192, [("w2_w10", 1024, [])]),
-    ]),
+    ("r10", 4096, [("r12", 4096, [("picked_b", 4096, []), ("x1a", 4096, [("picked_c", 2048, []), ("z_sc0", 512, [])])])]),
+    ("z0", 4096, [("z1", 4096, [])]),
 ]
 
 
@@ -163,7 +159,7 @@ def tile_list_ant_trail_residual_kernel(tc, tab_words, tab_scales, offs, w1, pos
 
         def reorder_w2(engine, order, a, b, into):
             w2_w[a, b] = into
-            engine.tensor_copy(
+            engine(
                 out=into.bitcast(U16).rearrange("p (t m) -> p %s" % order, t=PACK),
                 in_=w2_raw[a][:].bitcast(U16)[:, b * K_PASS : (b + 1) * K_PASS].rearrange("p (m t) -> p %s" % order, t=PACK),
             )
@@ -231,7 +227,7 @@ def tile_list_ant_trail_residual_kernel(tc, tab_words, tab_scales, offs, w1, pos
         nc.vector.tensor_copy(out=w2_rows[:].rearrange("p a (b t m) -> p (a b) m t", t=PACK, m=P), in_=w2_sc_raw[:].rearrange("p a (b m t) -> p (a b) m t", t=PACK, m=P))
         first_passes(0, (0, 1, 2))
         for b in range(PASSES2):
-            reorder_w2(nc.vector, "m t", 0, b, keep.tile([P, H], U8, name="w2_w0%d" % b, align_bytes=64)[:])
+            reorder_w2(nc.vector.tensor_copy, "m t", 0, b, keep.tile([P, H], U8, name="w2_w0%d" % b, align_bytes=64)[:])
         nc.sync.dma_start(pos1_t[:], pos1)
         load_w1(1, 0)
         nc.sync.dma_start(pos2_t[:], pos2)
@@ -242,27 +238,26 @@ def tile_list_ant_trail_residual_kernel(tc, tab_words, tab_scales, offs, w1, pos
         for q in range(4):
             nc.sync.dma_start(out=w2_sc[32 * q : 32 * q + 4, :, :].bitcast(I32), in_=w2_rows[1 + 32 * q : 32 * q + 32 : 8, :, :].bitcast(I32))
 
-        x0 = keep.tile([P, PACK, M], F32, name="x0", align_bytes=64)
         for t in range(PACK - 1):
-            pick1(0, t, x0[:, t, :])
-        wide = keep.tile([P, 2 * S], F32, name="h03", align_bytes=64)
-        r10 = wide[:, S:].bitcast(BF16)
+            pick1(0, t)
+        r10 = at("r10", PACK * K_PASS, BF16)
         gpsimd_round(woven_w1(r10, PACK), planar_w1(raw[1, 0][0]))
         r11 = keep.tile([P, PACK * K_PASS], BF16, name="r11", tag="rounded0", align_bytes=64)
         gpsimd_round(woven_w1(r11, PACK)[:, :GPSIMD_EARLY_SHARE], planar_w1(raw[1, 1][0])[:, :GPSIMD_EARLY_SHARE])
-        nc.scalar.copy(out=woven_w1(r11, PACK)[:, GPSIMD_EARLY_SHARE:], in_=planar_w1(raw[1, 1][0])[:, GPSIMD_EARLY_SHARE:])
         w_sc[1, 0] = keep.tile([P, K_PASS], U8, name="w_sc10", align_bytes=64)
         quantise(1, 0, r10, 0, K_PASS, K_PASS)
-        pick1(0, 3, x0[:, 3, :], wide[:])
+        pick1(0, 3, at("x03", M, F32))
         pick2(at("picked_a", M, F32), [(0, 0)])
+        nc.scalar.copy(out=woven_w1(r11, PACK)[:, GPSIMD_EARLY_SHARE:], in_=planar_w1(raw[1, 1][0])[:, GPSIMD_EARLY_SHARE:])
         r12 = at("r12", PACK * K_PASS, BF16)
         gpsimd_round(woven_w1(r12, PACK)[:, :GPSIMD_SHARE], planar_w1(raw[1, 2][0])[:, :GPSIMD_SHARE])
         nc.scalar.copy(out=woven_w1(r12, PACK)[:, GPSIMD_SHARE:], in_=planar_w1(raw[1, 2][0])[:, GPSIMD_SHARE:])
         w_sc[1, 1] = at("w_sc11", K_PASS, U8)
-        quantise(1, 1, r11, 0, K_PASS, K_PASS)
         w_sc[1, 2] = keep.tile([P, K_PASS], U8, name="w_sc12", align_bytes=64)
-        quantise(1, 2, r12, 0, K_PASS, K_PASS)
-        pick2(at("picked_b", 3 * M, F32), [(0, 1), (0, 2), (0, 3)])
+        for c0 in (0, 2 * P):
+            quantise(1, 1, r11[:, PACK * c0 :], c0, 2 * P, 2 * P)
+            quantise(1, 2, r12[:, PACK * c0 :], c0, 2 * P, 2 * P)
+        pick2(at("picked_b", 2 * M, F32), [(0, 1), (0, 2)])
         first_passes(1, (0, 1, 2))
 
         def product(engine, dst, src, other):
@@ -271,55 +266,61 @@ def tile_list_ant_trail_residual_kernel(tc, tab_words, tab_scales, offs, w1, pos
         def gains(b, cols):
             return gain_t[:, b, :].unsqueeze(1).to_broadcast([P, cols.stop - cols.start, PACK])
 
-        silu0 = at("silu0", PACK * M, F32).rearrange("p (m t) -> p m t", t=PACK)
-        for cols in halves:
-            nc.scalar.activation(out=woven(silu0, cols, 2), in_=planar(x0, cols, 2), func=ACT.Silu)
+        silu0 = at("silu0", PACK * M, F32).rearrange("p (t m) -> p t m", t=PACK)
+        gained0 = keep.tile([P, PACK, M], F32, name="gained0", align_bytes=64)
+        for t in range(PACK):
+            nc.scalar.activation(out=silu0[:, t, :], in_=x[0, t], func=ACT.Silu)
+            nc.gpsimd.tensor_scalar(out=gained0[:, t, :], in0=silu0[:, t, :], scalar1=gain_t[:, 0, t : t + 1], scalar2=0.0, op0=ALU.mult, op1=ALU.add)
         z0 = at("z0", PACK * M, BF16)
         z0_w = z0.rearrange("p (m t) -> p m t", t=PACK)
-        part0 = at("part0", PACK * M, F32).rearrange("p (m t) -> p m t", t=PACK)
-        both, squared = halves
-        nc.scalar.activation(out=part0[:, squared, :], in_=silu0[:, squared, :], func=ACT.Square)
-        product(nc.gpsimd, part0[:, both, :], silu0[:, both, :], gains(0, both))
-        product(nc.gpsimd, z0_w[:, both, :], part0[:, both, :], silu0[:, both, :])
-        product(nc.gpsimd, z0_w[:, squared, :], part0[:, squared, :], gains(0, squared))
-        reorder_w2(nc.gpsimd, "t m", 1, 0, at("w2_w10", H, U8))
+        for cols in halves:
+            product(nc.gpsimd, woven(z0_w, cols, 2), planar(gained0, cols, 2), planar(silu0, cols, 2))
         pairs = [at("x1a", 2 * M, F32), keep.tile([P, 2 * M], F32, name="x1b", align_bytes=64)]
         for t in range(PACK):
             pick1(1, t, pairs[t // 2][:, (t % 2) * M : (t % 2 + 1) * M])
 
         silu1 = silu(1, "w_codes12")
+        pick2(at("picked_c", M, F32), [(0, 3)])
         quantise_z(0, z0, at("z_sc0", M, U8))
-        pick2(at("picked_d", M, F32), [(1, 0)])
-        reorder_w2(nc.gpsimd, "t m", 1, 1, at("w2_w11", H, U8))
         z1 = at("z1", PACK * M, BF16)
         z1_w = z1.rearrange("p (m t) -> p m t", t=PACK)
         squares1 = keep.tile([P, M, PACK], F32, name="squares1", tag="tab1", align_bytes=64)
         for cols in quarters:
             nc.scalar.activation(out=woven(squares1, cols, 2), in_=planar(silu1, cols, 2), func=ACT.Square)
             product(nc.vector, z1_w[:, cols, :], squares1[:, cols, :], gains(1, cols))
+        w2_last = keep.tile([P, PASSES2, H], U8, name="w2_last", tag="w_codes12", align_bytes=64)
+        for b in range(PASSES2):
+            reorder_w2(nc.scalar.copy, "m t", 1, b, w2_last[:, b, :])
         quantise_z(1, z1, keep.tile([P, M], U8, name="z_sc1", align_bytes=64))
-        pick2(keep.tile([P, M], F32, name="picked_last", tag="tab1", align_bytes=64), [(1, 1)])
+        pick2(keep.tile([P, M], F32, name="picked_last", tag="tab1", align_bytes=64), [(1, 0)])
 
         results = keep.tile([P, PASSES2 * PACK, M], F32, name="results", tag="tab0", align_bytes=64)
         out_rows = out.rearrange("(b p t) m -> b t p m", p=P, t=PACK)
         early = list(picked)
         by_gpsimd, by_vector = early[:1], early[1:]
         fused = [(1, t) for t in range(PACK) if (1, t) not in picked]
-        tiles = early[:3] + fused + early[3:]
+
+        def second_pass(b, t, a, first):
+            if first:
+                y[b, t] = psum.tile([P, BANK], F32, name="bank%d" % (PACK * b + t))
+            c0 = b * K_PASS + t * P
+            nc.tensor.matmul_mx(
+                out=y[b, t][:],
+                lhsT=w2_w[a, b][:, 2 * t * P : 2 * (t + 1) * P].bitcast(FP4X4),
+                lhsT_scale=w2_sc[:, a, c0 : c0 + P],
+                rhs=z_codes[a][:].bitcast(FP8X4),
+                rhs_scale=z_sc[a][:],
+                start=first,
+                stop=not first,
+            )
+
+        ahead = [by_vector[0]] + by_gpsimd + by_vector[1:3]
         for a in range(PASSES2):
-            for b, t in tiles:
-                if a == 0:
-                    y[b, t] = psum.tile([P, BANK], F32, name="bank%d" % (PACK * b + t))
-                c0 = b * K_PASS + t * P
-                nc.tensor.matmul_mx(
-                    out=y[b, t][:],
-                    lhsT=w2_w[a, b][:, 2 * t * P : 2 * (t + 1) * P].bitcast(FP4X4),
-                    lhsT_scale=w2_sc[:, a, c0 : c0 + P],
-                    rhs=z_codes[a][:].bitcast(FP8X4),
-                    rhs_scale=z_sc[a][:],
-                    start=(a == 0),
-                    stop=(a == PASSES2 - 1),
-                )
+            for b, t in ahead:
+                second_pass(b, t, a, a == 0)
+        for b, t in fused[:1] + by_vector[3:] + fused[1:]:
+            for a in (1, 0):
+                second_pass(b, t, a, a == 1)
         factors = keep.tile([P, len(by_gpsimd + fused), M], F32, name="factors", tag="tab2", align_bytes=64)
         factor = {}
         for i, (b, t) in enumerate(by_gpsimd + fused):

@@ -1,6 +1,7 @@
 from contextlib import ExitStack
 
 import concourse.mybir as mybir
+from concourse.masks import make_identity
 
 K, H, T, S, M = 1536, 1024, 4096, 1024, 512
 FLOPS = 2 * K * H * S + 2 * H * H * M
@@ -26,13 +27,15 @@ HALF = M // 2
 VECTOR_SHARE = 42
 GPSIMD_SHARE = 56
 GPSIMD_EARLY_SHARE = 22
-QUARTER = M // 4
+GPSIMD_COLUMNS = 176
+PIECE = (M - GPSIMD_COLUMNS) // 3
 WIDTH = {F32: 4, BF16: 2, U8: 1}
 LAID = [
     ("raw_first", 8192, [("x03", 2048, []), ("picked_a", 2048, [])]),
     ("raw_last", 8192, [("silu0", 8192, []), ("w_sc11", 512, [])]),
     ("r10", 4096, [("r12", 4096, [("picked_b", 4096, []), ("x1a", 4096, [("picked_c", 2048, []), ("z_sc0", 512, [])])])]),
     ("z0", 4096, [("z1", 4096, [])]),
+    ("x1b", 4096, [("w2_last", 2048, [])]),
 ]
 
 
@@ -72,6 +75,11 @@ def tile_list_ant_trail_residual_kernel(tc, tab_words, tab_scales, offs, w1, pos
         warm = keep.tile([P, 8], F32, name="warm")
         nc.vector.memset(warm[:], 0.0)
         nc.scalar.activation(out=warm[:], in_=warm[:], func=ACT.Silu)
+
+        identity = keep.tile([P, P], F32, name="identity", align_bytes=64)
+        make_identity(nc, identity[:])
+        gain_rows = keep.tile([P, P], F32, name="gain_rows", align_bytes=64)
+        nc.vector.memset(gain_rows[:], 0.0)
 
         def at(name, cols, dtype):
             offset, span = places[name]
@@ -219,7 +227,7 @@ def tile_list_ant_trail_residual_kernel(tc, tab_words, tab_scales, offs, w1, pos
             nc.vector.quantize_mx(out=z_codes[b][:].bitcast(FP8X4), scales=z_sc[b][:], in_=z)
 
         halves = [slice(u * HALF, (u + 1) * HALF) for u in range(2)]
-        quarters = [slice(u * QUARTER, (u + 1) * QUARTER) for u in range(4)]
+        pieces = [slice(c, c + PIECE) for c in range(GPSIMD_COLUMNS, M, PIECE)]
 
         for a in range(PASSES1):
             nc.vector.tensor_copy(out=v_words[a][:], in_=tab[a][:].indirect(offs_t[:]))
@@ -237,6 +245,9 @@ def tile_list_ant_trail_residual_kernel(tc, tab_words, tab_scales, offs, w1, pos
         nc.sync.dma_start(out=gain_t[:], in_=gain.rearrange("(b p t) -> p b t", p=P, t=PACK))
         for q in range(4):
             nc.sync.dma_start(out=w2_sc[32 * q : 32 * q + 4, :, :].bitcast(I32), in_=w2_rows[1 + 32 * q : 32 * q + 32 : 8, :, :].bitcast(I32))
+
+        with nc.allow_non_contiguous_dma(reason="row t holds the gains of channels 4 p + t"):
+            nc.sync.dma_start(out=gain_rows[:PACK, :], in_=gain[K_PASS:].rearrange("(p t) -> t p", t=PACK))
 
         for t in range(PACK - 1):
             pick1(0, t)
@@ -263,32 +274,39 @@ def tile_list_ant_trail_residual_kernel(tc, tab_words, tab_scales, offs, w1, pos
         def product(engine, dst, src, other):
             engine.tensor_tensor(out=dst, in0=src, in1=other, op=ALU.mult)
 
-        def gains(b, cols):
-            return gain_t[:, b, :].unsqueeze(1).to_broadcast([P, cols.stop - cols.start, PACK])
+        def gained(dst, src, b, t):
+            nc.gpsimd.tensor_scalar(out=dst, in0=src, scalar1=gain_t[:, b, t : t + 1], scalar2=0.0, op0=ALU.mult, op1=ALU.add)
 
         silu0 = at("silu0", PACK * M, F32).rearrange("p (t m) -> p t m", t=PACK)
         gained0 = keep.tile([P, PACK, M], F32, name="gained0", align_bytes=64)
         for t in range(PACK):
             nc.scalar.activation(out=silu0[:, t, :], in_=x[0, t], func=ACT.Silu)
-            nc.gpsimd.tensor_scalar(out=gained0[:, t, :], in0=silu0[:, t, :], scalar1=gain_t[:, 0, t : t + 1], scalar2=0.0, op0=ALU.mult, op1=ALU.add)
+            gained(gained0[:, t, :], silu0[:, t, :], 0, t)
         z0 = at("z0", PACK * M, BF16)
         z0_w = z0.rearrange("p (m t) -> p m t", t=PACK)
         for cols in halves:
             product(nc.gpsimd, woven(z0_w, cols, 2), planar(gained0, cols, 2), planar(silu0, cols, 2))
-        pairs = [at("x1a", 2 * M, F32), keep.tile([P, 2 * M], F32, name="x1b", align_bytes=64)]
+        pairs = [at("x1a", 2 * M, F32), at("x1b", 2 * M, F32)]
         for t in range(PACK):
             pick1(1, t, pairs[t // 2][:, (t % 2) * M : (t % 2 + 1) * M])
 
         silu1 = silu(1, "w_codes12")
-        pick2(at("picked_c", M, F32), [(0, 3)])
         quantise_z(0, z0, at("z_sc0", M, U8))
+        pick2(at("picked_c", M, F32), [(0, 3)])
+        gain_bank = psum.tile([P, P], F32, name="bank7")
+        nc.tensor.transpose(gain_bank[:], gain_rows[:], identity[:])
+        first = slice(0, GPSIMD_COLUMNS)
+        gained1 = keep.tile([P, PACK, GPSIMD_COLUMNS], F32, name="gained1", align_bytes=64)
+        for t in range(PACK):
+            gained(gained1[:, t, :], silu1[:, t, first], 1, t)
         z1 = at("z1", PACK * M, BF16)
         z1_w = z1.rearrange("p (m t) -> p m t", t=PACK)
         squares1 = keep.tile([P, M, PACK], F32, name="squares1", tag="tab1", align_bytes=64)
-        for cols in quarters:
+        product(nc.gpsimd, woven(z1_w, first, 2), planar(gained1, first, 2), planar(silu1, first, 2))
+        for cols in pieces:
             nc.scalar.activation(out=woven(squares1, cols, 2), in_=planar(silu1, cols, 2), func=ACT.Square)
-            product(nc.vector, z1_w[:, cols, :], squares1[:, cols, :], gains(1, cols))
-        w2_last = keep.tile([P, PASSES2, H], U8, name="w2_last", tag="w_codes12", align_bytes=64)
+            product(nc.vector, z1_w[:, cols, :], squares1[:, cols, :], gain_bank[:, :PACK].unsqueeze(1).to_broadcast([P, PIECE, PACK]))
+        w2_last = at("w2_last", PASSES2 * H, U8).rearrange("p (b n) -> p b n", b=PASSES2)
         for b in range(PASSES2):
             reorder_w2(nc.scalar.copy, "m t", 1, b, w2_last[:, b, :])
         quantise_z(1, z1, keep.tile([P, M], U8, name="z_sc1", align_bytes=64))
@@ -314,11 +332,11 @@ def tile_list_ant_trail_residual_kernel(tc, tab_words, tab_scales, offs, w1, pos
                 stop=not first,
             )
 
-        ahead = [by_vector[0]] + by_gpsimd + by_vector[1:3]
+        ahead = [by_vector[0]] + by_gpsimd + by_vector[1:] + fused[:1]
         for a in range(PASSES2):
             for b, t in ahead:
                 second_pass(b, t, a, a == 0)
-        for b, t in fused[:1] + by_vector[3:] + fused[1:]:
+        for b, t in fused[1:]:
             for a in (1, 0):
                 second_pass(b, t, a, a == 1)
         factors = keep.tile([P, len(by_gpsimd + fused), M], F32, name="factors", tag="tab2", align_bytes=64)

@@ -25,14 +25,14 @@ PASSES1 = K // K_PASS
 PASSES2 = H // K_PASS
 HALF = M // 2
 VECTOR_SHARE = 42
-GPSIMD_SHARE = 56
+GPSIMD_SHARE = 20
 GPSIMD_EARLY_SHARE = 22
-GPSIMD_COLUMNS = 176
+GPSIMD_COLUMNS = 128
 PIECE = (M - GPSIMD_COLUMNS) // 3
 WIDTH = {F32: 4, BF16: 2, U8: 1}
 LAID = [
     ("raw_first", 8192, [("x03", 2048, []), ("picked_a", 2048, [])]),
-    ("raw_last", 8192, [("silu0", 8192, []), ("w_sc11", 512, [])]),
+    ("raw_last", 4096, [("silu0", 8192, []), ("w_sc11", 512, [])]),
     ("r10", 4096, [("r12", 4096, [("picked_b", 4096, []), ("x1a", 4096, [("picked_c", 2048, []), ("z_sc0", 512, [])])])]),
     ("z0", 4096, [("z1", 4096, [])]),
     ("x1b", 4096, [("w2_last", 2048, [])]),
@@ -98,7 +98,7 @@ def tile_list_ant_trail_residual_kernel(tc, tab_words, tab_scales, offs, w1, pos
             width = K_PASS // parts
             raw[b, a] = []
             for part in range(parts):
-                if b == 1 and a != 1:
+                if (b, a, part) in ((1, 0, 0), (1, 2, 1)):
                     piece = at("raw_last" if a else "raw_first", PACK * width, F32).rearrange("p (j c) -> p j c", j=PACK)
                 else:
                     piece = raws.tile([P, PACK, width], F32, name="raw")[:]
@@ -240,7 +240,7 @@ def tile_list_ant_trail_residual_kernel(tc, tab_words, tab_scales, offs, w1, pos
         load_w1(1, 0)
         nc.sync.dma_start(pos2_t[:], pos2)
         load_w1(1, 1)
-        load_w1(1, 2)
+        load_w1(1, 2, 2)
         load_w2(1)
         nc.sync.dma_start(out=gain_t[:], in_=gain.rearrange("(b p t) -> p b t", p=P, t=PACK))
         for q in range(4):
@@ -261,8 +261,10 @@ def tile_list_ant_trail_residual_kernel(tc, tab_words, tab_scales, offs, w1, pos
         pick2(at("picked_a", M, F32), [(0, 0)])
         nc.scalar.copy(out=woven_w1(r11, PACK)[:, GPSIMD_EARLY_SHARE:], in_=planar_w1(raw[1, 1][0])[:, GPSIMD_EARLY_SHARE:])
         r12 = at("r12", PACK * K_PASS, BF16)
-        gpsimd_round(woven_w1(r12, PACK)[:, :GPSIMD_SHARE], planar_w1(raw[1, 2][0])[:, :GPSIMD_SHARE])
-        nc.scalar.copy(out=woven_w1(r12, PACK)[:, GPSIMD_SHARE:], in_=planar_w1(raw[1, 2][0])[:, GPSIMD_SHARE:])
+        last = woven_w1(r12, PACK)[:, P // 2 :]
+        gpsimd_round(woven_w1(r12, PACK)[:, : P // 2], planar_w1(raw[1, 2][0]))
+        gpsimd_round(last[:, :GPSIMD_SHARE], planar_w1(raw[1, 2][1])[:, :GPSIMD_SHARE])
+        nc.scalar.copy(out=last[:, GPSIMD_SHARE:], in_=planar_w1(raw[1, 2][1])[:, GPSIMD_SHARE:])
         w_sc[1, 1] = at("w_sc11", K_PASS, U8)
         w_sc[1, 2] = keep.tile([P, K_PASS], U8, name="w_sc12", align_bytes=64)
         for c0 in (0, 2 * P):
@@ -291,8 +293,8 @@ def tile_list_ant_trail_residual_kernel(tc, tab_words, tab_scales, offs, w1, pos
             pick1(1, t, pairs[t // 2][:, (t % 2) * M : (t % 2 + 1) * M])
 
         silu1 = silu(1, "w_codes12")
-        quantise_z(0, z0, at("z_sc0", M, U8))
         pick2(at("picked_c", M, F32), [(0, 3)])
+        quantise_z(0, z0, at("z_sc0", M, U8))
         gain_bank = psum.tile([P, P], F32, name="bank7")
         nc.tensor.transpose(gain_bank[:], gain_rows[:], identity[:])
         first = slice(0, GPSIMD_COLUMNS)

@@ -25,7 +25,7 @@ PASSES1 = K // K_PASS
 PASSES2 = H // K_PASS
 HALF = M // 2
 VECTOR_SHARE = 42
-GPSIMD_SHARE = 20
+GPSIMD_SHARE = 32
 GPSIMD_EARLY_SHARE = 22
 GPSIMD_COLUMNS = 128
 PIECE = (M - GPSIMD_COLUMNS) // 3
@@ -137,7 +137,7 @@ def tile_list_ant_trail_residual_kernel(tc, tab_words, tab_scales, offs, w1, pos
             return piece.rearrange("p j (m t) -> p m j t", t=PACK)
 
         def gpsimd_round(dst, src):
-            nc.gpsimd.tensor_scalar(out=dst.rearrange("p m j t -> p m t j"), in0=src.rearrange("p m j t -> p m t j"), scalar1=1.0, scalar2=0.0, op0=ALU.mult, op1=ALU.add)
+            nc.gpsimd.tensor_scalar(out=dst, in0=src, scalar1=1.0, scalar2=0.0, op0=ALU.mult, op1=ALU.add)
 
         def quantise(b, a, rounded, c0, width, step):
             for c in range(0, width, step):

@@ -25,8 +25,8 @@ PASSES1 = K // K_PASS
 PASSES2 = H // K_PASS
 HALF = M // 2
 VECTOR_SHARE = 42
-GPSIMD_SHARE = 32
-GPSIMD_EARLY_SHARE = 22
+GPSIMD_SHARE = 72
+GPSIMD_EARLY_SHARE = 44
 GPSIMD_COLUMNS = 128
 PIECE = (M - GPSIMD_COLUMNS) // 3
 WIDTH = {F32: 4, BF16: 2, U8: 1}
@@ -94,15 +94,14 @@ def tile_list_ant_trail_residual_kernel(tc, tab_words, tab_scales, offs, w1, pos
         def load_tab(a):
             nc.sync.dma_start(out=tab[a][:].bitcast(I32), in_=tab_words[a].rearrange("p t i -> p (t i)").bitcast(I32))
 
-        def load_w1(b, a, parts=1):
-            width = K_PASS // parts
+        def load_w1(b, a, cut=K_PASS):
             raw[b, a] = []
-            for part in range(parts):
+            for part, (c0, width) in enumerate([(0, cut), (cut, K_PASS - cut)][: 1 if cut == K_PASS else 2]):
                 if (b, a, part) in ((1, 0, 0), (1, 2, 1)):
                     piece = at("raw_last" if a else "raw_first", PACK * width, F32).rearrange("p (j c) -> p j c", j=PACK)
                 else:
                     piece = raws.tile([P, PACK, width], F32, name="raw")[:]
-                c0 = b * K_PASS + part * width
+                c0 = c0 + b * K_PASS
                 nc.sync.dma_start(out=piece, in_=w1[a * K_PASS : (a + 1) * K_PASS, c0 : c0 + width].rearrange("(p j) c -> p j c", j=PACK))
                 raw[b, a].append(piece)
 
@@ -128,7 +127,7 @@ def tile_list_ant_trail_residual_kernel(tc, tab_words, tab_scales, offs, w1, pos
         place_rows(planes[6:7])
         load_tab(2)
         place_rows(planes[7:])
-        load_w1(0, 2, 2)
+        load_w1(0, 2, K_PASS // 2)
 
         def woven_w1(rounded, tiles):
             return rounded[:, :].rearrange("p (t m j) -> p m j t", t=tiles, j=PACK)
@@ -240,7 +239,7 @@ def tile_list_ant_trail_residual_kernel(tc, tab_words, tab_scales, offs, w1, pos
         load_w1(1, 0)
         nc.sync.dma_start(pos2_t[:], pos2)
         load_w1(1, 1)
-        load_w1(1, 2, 2)
+        load_w1(1, 2, PACK * GPSIMD_SHARE)
         load_w2(1)
         nc.sync.dma_start(out=gain_t[:], in_=gain.rearrange("(b p t) -> p b t", p=P, t=PACK))
         for q in range(4):
@@ -261,10 +260,8 @@ def tile_list_ant_trail_residual_kernel(tc, tab_words, tab_scales, offs, w1, pos
         pick2(at("picked_a", M, F32), [(0, 0)])
         nc.scalar.copy(out=woven_w1(r11, PACK)[:, GPSIMD_EARLY_SHARE:], in_=planar_w1(raw[1, 1][0])[:, GPSIMD_EARLY_SHARE:])
         r12 = at("r12", PACK * K_PASS, BF16)
-        last = woven_w1(r12, PACK)[:, P // 2 :]
-        gpsimd_round(woven_w1(r12, PACK)[:, : P // 2], planar_w1(raw[1, 2][0]))
-        gpsimd_round(last[:, :GPSIMD_SHARE], planar_w1(raw[1, 2][1])[:, :GPSIMD_SHARE])
-        nc.scalar.copy(out=last[:, GPSIMD_SHARE:], in_=planar_w1(raw[1, 2][1])[:, GPSIMD_SHARE:])
+        gpsimd_round(woven_w1(r12, PACK)[:, :GPSIMD_SHARE], planar_w1(raw[1, 2][0]))
+        nc.scalar.copy(out=woven_w1(r12, PACK)[:, GPSIMD_SHARE:], in_=planar_w1(raw[1, 2][1]))
         w_sc[1, 1] = at("w_sc11", K_PASS, U8)
         w_sc[1, 2] = keep.tile([P, K_PASS], U8, name="w_sc12", align_bytes=64)
         for c0 in (0, 2 * P):
@@ -293,8 +290,8 @@ def tile_list_ant_trail_residual_kernel(tc, tab_words, tab_scales, offs, w1, pos
             pick1(1, t, pairs[t // 2][:, (t % 2) * M : (t % 2 + 1) * M])
 
         silu1 = silu(1, "w_codes12")
-        pick2(at("picked_c", M, F32), [(0, 3)])
         quantise_z(0, z0, at("z_sc0", M, U8))
+        pick2(at("picked_c", M, F32), [(0, 3)])
         gain_bank = psum.tile([P, P], F32, name="bank7")
         nc.tensor.transpose(gain_bank[:], gain_rows[:], identity[:])
         first = slice(0, GPSIMD_COLUMNS)

@@ -33,7 +33,8 @@ WIDTH = {F32: 4, BF16: 2, U8: 1}
 LAID = [
     ("raw_first", 8192, [("x03", 2048, []), ("picked_a", 2048, [])]),
     ("raw_last", 4096, [("silu0", 8192, []), ("w_sc11", 512, [])]),
-    ("r10", 4096, [("r12", 4096, [("picked_b", 4096, []), ("x1a", 4096, [("picked_c", 2048, []), ("z_sc0", 512, [])])])]),
+    ("r11", 4096, [("picked_b", 4096, [])]),
+    ("r10", 4096, [("r12", 4096, [("x1a", 4096, [("picked_c", 2048, []), ("z_sc0", 512, [])])])]),
     ("z0", 4096, [("z1", 4096, [])]),
     ("x1b", 4096, [("w2_last", 2048, [])]),
 ]
@@ -196,7 +197,7 @@ def tile_list_ant_trail_residual_kernel(tc, tab_words, tab_scales, offs, w1, pos
             h[b, t] = window[:, :S]
             for half in range(2):
                 cols = slice(half * BANK, (half + 1) * BANK)
-                if (b, t, half) == (0, 0, 1):
+                if (b, t, half) == (0, 0, 0):
                     nc.vector.tensor_copy(out=h[b, t][:, cols], in_=banks[b, t, half][:])
                 else:
                     nc.scalar.copy(out=h[b, t][:, cols], in_=banks[b, t, half][:])
@@ -220,13 +221,14 @@ def tile_list_ant_trail_residual_kernel(tc, tab_words, tab_scales, offs, w1, pos
         def woven(tile, cols, run):
             return tile[:, cols, :].rearrange("p (c i) t -> p c t i", i=run)
 
-        def quantise_z(b, z, scales):
+        def quantise_z(b, z, scales, step=M):
             z_codes[b] = keep.tile([P, M], U32, name="z_codes%d" % b, align_bytes=64)
             z_sc[b] = scales
-            nc.vector.quantize_mx(out=z_codes[b][:].bitcast(FP8X4), scales=z_sc[b][:], in_=z)
+            for c in range(0, M, step):
+                nc.vector.quantize_mx(out=z_codes[b][:, c : c + step].bitcast(FP8X4), scales=z_sc[b][:, c : c + step], in_=z[:, PACK * c : PACK * (c + step)])
 
         halves = [slice(u * HALF, (u + 1) * HALF) for u in range(2)]
-        pieces = [slice(c, c + PIECE) for c in range(GPSIMD_COLUMNS, M, PIECE)]
+        pieces = [slice(0, PIECE), slice(PIECE, HALF), slice(HALF + GPSIMD_COLUMNS, M)]
 
         for a in range(PASSES1):
             nc.vector.tensor_copy(out=v_words[a][:], in_=tab[a][:].indirect(offs_t[:]))
@@ -252,7 +254,7 @@ def tile_list_ant_trail_residual_kernel(tc, tab_words, tab_scales, offs, w1, pos
             pick1(0, t)
         r10 = at("r10", PACK * K_PASS, BF16)
         gpsimd_round(woven_w1(r10, PACK), planar_w1(raw[1, 0][0]))
-        r11 = keep.tile([P, PACK * K_PASS], BF16, name="r11", tag="rounded0", align_bytes=64)
+        r11 = at("r11", PACK * K_PASS, BF16)
         gpsimd_round(woven_w1(r11, PACK)[:, :GPSIMD_EARLY_SHARE], planar_w1(raw[1, 1][0])[:, :GPSIMD_EARLY_SHARE])
         w_sc[1, 0] = keep.tile([P, K_PASS], U8, name="w_sc10", align_bytes=64)
         quantise(1, 0, r10, 0, K_PASS, K_PASS)
@@ -294,21 +296,21 @@ def tile_list_ant_trail_residual_kernel(tc, tab_words, tab_scales, offs, w1, pos
         pick2(at("picked_c", M, F32), [(0, 3)])
         gain_bank = psum.tile([P, P], F32, name="bank7")
         nc.tensor.transpose(gain_bank[:], gain_rows[:], identity[:])
-        first = slice(0, GPSIMD_COLUMNS)
+        first = slice(HALF, HALF + GPSIMD_COLUMNS)
         gained1 = keep.tile([P, PACK, GPSIMD_COLUMNS], F32, name="gained1", align_bytes=64)
         for t in range(PACK):
             gained(gained1[:, t, :], silu1[:, t, first], 1, t)
         z1 = at("z1", PACK * M, BF16)
         z1_w = z1.rearrange("p (m t) -> p m t", t=PACK)
         squares1 = keep.tile([P, M, PACK], F32, name="squares1", tag="tab1", align_bytes=64)
-        product(nc.gpsimd, woven(z1_w, first, 2), planar(gained1, first, 2), planar(silu1, first, 2))
+        product(nc.gpsimd, woven(z1_w, first, 2), planar(gained1, slice(0, GPSIMD_COLUMNS), 2), planar(silu1, first, 2))
         for cols in pieces:
             nc.scalar.activation(out=woven(squares1, cols, 2), in_=planar(silu1, cols, 2), func=ACT.Square)
             product(nc.vector, z1_w[:, cols, :], squares1[:, cols, :], gain_bank[:, :PACK].unsqueeze(1).to_broadcast([P, PIECE, PACK]))
         w2_last = at("w2_last", PASSES2 * H, U8).rearrange("p (b n) -> p b n", b=PASSES2)
         for b in range(PASSES2):
             reorder_w2(nc.scalar.copy, "m t", 1, b, w2_last[:, b, :])
-        quantise_z(1, z1, keep.tile([P, M], U8, name="z_sc1", align_bytes=64))
+        quantise_z(1, z1, keep.tile([P, M], U8, name="z_sc1", align_bytes=64), HALF)
         pick2(keep.tile([P, M], F32, name="picked_last", tag="tab1", align_bytes=64), [(1, 0)])
 
         results = keep.tile([P, PASSES2 * PACK, M], F32, name="results", tag="tab0", align_bytes=64)

from contextlib import ExitStack

import concourse.mybir as mybir
from concourse.masks import make_identity

K, H, T, S, M = 1536, 1024, 4096, 1024, 512
FLOPS = 2 * K * H * S + 2 * H * H * M

F32 = mybir.dt.float32
BF16 = mybir.dt.bfloat16
I32 = mybir.dt.int32
U32 = mybir.dt.uint32
U16 = mybir.dt.uint16
U8 = mybir.dt.uint8
FP8X4 = mybir.dt.float8_e4m3fn_x4
FP4X4 = mybir.dt.float4_e2m1fn_x4
ACT = mybir.ActivationFunctionType
ALU = mybir.AluOpType

P = 128
PACK = 4
K_PASS = P * PACK
BANK = 512
PASSES1 = K // K_PASS
PASSES2 = H // K_PASS
HALF = M // 2
VECTOR_SHARE = 42
GPSIMD_SHARE = 72
GPSIMD_EARLY_SHARE = 44
GPSIMD_COLUMNS = 128
PIECE = (M - GPSIMD_COLUMNS) // 3
WIDTH = {F32: 4, BF16: 2, U8: 1}
LAID = [
    ("raw_first", 8192, [("x03", 2048, []), ("picked_a", 2048, [])]),
    ("raw_last", 4096, [("silu0", 8192, []), ("w_sc11", 512, [])]),
    ("r11", 4096, [("picked_b", 4096, [])]),
    ("r10", 4096, [("r12", 4096, [("x1a", 4096, [("picked_c", 2048, []), ("z_sc0", 512, [])])])]),
    ("z0", 4096, [("z1", 4096, [])]),
    ("x1b", 4096, [("w2_last", 2048, [])]),
]


def lay(tiles, offset, places):
    for name, size, over in tiles:
        span = max(size, lay(over, offset, places) - offset)
        places[name] = (offset, span)
        offset = offset + span
    return offset


def tile_list_ant_trail_residual_kernel(tc, tab_words, tab_scales, offs, w1, pos1, pos2, gain, w2_words, w2_scales, out):
    nc = tc.nc
    places = {}
    lay(LAID, 0, places)
    with ExitStack() as ctx:
        keep = ctx.enter_context(tc.tile_pool(name="keep", bufs=1))
        raws = ctx.enter_context(tc.tile_pool(name="raws", bufs=3))
        laid = ctx.enter_context(tc.tile_pool(name="laid", bufs=1))
        psum = ctx.enter_context(tc.psum_pool(name="psum", bufs=1))

        offs_t = keep.tile([P, S // 16], U16, name="offs_t")
        pos1_t = keep.tile([P, M // 16], U16, name="pos1_t")
        pos2_t = keep.tile([P, M // 16], U16, name="pos2_t")
        tab = [keep.tile([P, T], U32, name="tab%d" % a, align_bytes=64) for a in range(PASSES1)]
        tab_sc = keep.tile([P, T], U8, name="tab_sc", align_bytes=64)
        w2_sc_raw = keep.tile([P, PASSES2, H], U8, name="w2_sc_raw", align_bytes=64)
        gain_t = keep.tile([P, PASSES2, PACK], F32, name="gain_t")
        v_rows = keep.tile([P, S], U8, name="v_rows", align_bytes=64)
        v_sc = [keep.tile([P, S], U8, name="v_sc%d" % a, align_bytes=64) for a in range(PASSES1)]
        w2_rows = keep.tile([P, PASSES2, H], U8, name="w2_rows", align_bytes=64)
        w2_sc = keep.tile([P, PASSES2, H], U8, name="w2_sc", align_bytes=64)
        v_words = [keep.tile([P, S], U32, name="v_words%d" % a, align_bytes=64) for a in range(PASSES1)]

        for plane in [tab_sc, w2_sc_raw] + v_sc + [w2_sc]:
            nc.vector.memset(plane[:].bitcast(I32), 0)
        warm = keep.tile([P, 8], F32, name="warm")
        nc.vector.memset(warm[:], 0.0)
        nc.scalar.activation(out=warm[:], in_=warm[:], func=ACT.Silu)

        identity = keep.tile([P, P], F32, name="identity", align_bytes=64)
        make_identity(nc, identity[:])
        gain_rows = keep.tile([P, P], F32, name="gain_rows", align_bytes=64)
        nc.vector.memset(gain_rows[:], 0.0)

        def at(name, cols, dtype):
            offset, span = places[name]
            return laid.tile([P, span // WIDTH[dtype]], dtype, name=name, offset=offset, align_bytes=64)[:, :cols]

        raw, w_codes, w_sc, banks, h, x, z_codes, z_sc, picked, y, w2_w, w2_raw = {}, {}, {}, {}, {}, {}, {}, {}, {}, {}, {}, {}

        for b in range(PASSES2):
            for a in range(PASSES1):
                w_codes[b, a] = keep.tile([P, K_PASS], U32, name="w_codes%d%d" % (b, a), align_bytes=64)

        def load_tab(a):
            nc.sync.dma_start(out=tab[a][:].bitcast(I32), in_=tab_words[a].rearrange("p t i -> p (t i)").bitcast(I32))

        def load_w1(b, a, cut=K_PASS):
            raw[b, a] = []
            for part, (c0, width) in enumerate([(0, cut), (cut, K_PASS - cut)][: 1 if cut == K_PASS else 2]):
                if (b, a, part) in ((1, 0, 0), (1, 2, 1)):
                    piece = at("raw_last" if a else "raw_first", PACK * width, F32).rearrange("p (j c) -> p j c", j=PACK)
                else:
                    piece = raws.tile([P, PACK, width], F32, name="raw")[:]
                c0 = c0 + b * K_PASS
                nc.sync.dma_start(out=piece, in_=w1[a * K_PASS : (a + 1) * K_PASS, c0 : c0 + width].rearrange("(p j) c -> p j c", j=PACK))
                raw[b, a].append(piece)

        staged = ((0, 4), (64, 4), (2, 8))

        def place_rows(planes):
            for a, q in planes:
                first, step = staged[a]
                row = first + 4 * q * step
                nc.sync.dma_start(out=v_sc[a][32 * q + 4 * a : 32 * q + 4 * a + 4, :].bitcast(I32), in_=v_rows[row : row + 3 * step + 1 : step, :].bitcast(I32))

        planes = [(a, q) for a in (0, 2, 1) for q in range(4)]
        load_tab(0)
        nc.sync.dma_start(out=tab_sc[0:128:4, :].bitcast(I32), in_=tab_scales[0:2].rearrange("a q t -> (a q) t").bitcast(I32))
        nc.sync.dma_start(out=tab_sc[2:128:8, :].bitcast(I32), in_=tab_scales[2].bitcast(I32))
        nc.sync.dma_start(offs_t[:], offs)
        nc.sync.dma_start(out=w2_sc_raw[1:128:8, :, :].bitcast(I32), in_=w2_scales.rearrange("a q n -> q a n").bitcast(I32))
        nc.vector.tensor_copy(out=v_rows[:], in_=tab_sc[:].indirect(offs_t[:]))
        load_tab(1)
        load_w1(0, 0)
        place_rows(planes[:6])
        load_w1(0, 1)
        place_rows(planes[6:7])
        load_tab(2)
        place_rows(planes[7:])
        load_w1(0, 2, K_PASS // 2)

        def woven_w1(rounded, tiles):
            return rounded[:, :].rearrange("p (t m j) -> p m j t", t=tiles, j=PACK)

        def planar_w1(piece):
            return piece.rearrange("p j (m t) -> p m j t", t=PACK)

        def gpsimd_round(dst, src):
            nc.gpsimd.tensor_scalar(out=dst, in0=src, scalar1=1.0, scalar2=0.0, op0=ALU.mult, op1=ALU.add)

        def quantise(b, a, rounded, c0, width, step):
            for c in range(0, width, step):
                cols = slice(c0 + c, c0 + c + step)
                nc.vector.quantize_mx(out=w_codes[b, a][:, cols].bitcast(FP8X4), scales=w_sc[b, a][:, cols], in_=rounded[:, PACK * c : PACK * (c + step)])

        def quantise_first(a):
            rounded = keep.tile([P, PACK * K_PASS], BF16, name="rounded%d" % a, align_bytes=64)
            dst = woven_w1(rounded, PACK)
            last = a == PASSES1 - 1
            m0 = 0
            for piece in raw[0, a]:
                src = planar_w1(piece)
                count = src.shape[1]
                share = VECTOR_SHARE if last and m0 + count == P else 0
                if share:
                    nc.vector.tensor_copy(out=dst[:, m0 : m0 + share], in_=src[:, :share])
                nc.scalar.copy(out=dst[:, m0 + share : m0 + count], in_=src[:, share:])
                m0 = m0 + count
            w_sc[0, a] = keep.tile([P, K_PASS], U8, name="w_sc0%d" % a, align_bytes=64)
            quantise(0, a, rounded, 0, K_PASS, P if last else K_PASS)


        def load_w2(a):
            w2_raw[a] = keep.tile([P, H // 2], I32, name="w2_raw%d" % a, align_bytes=64)
            nc.sync.dma_start(out=w2_raw[a][:], in_=w2_words[a].bitcast(I32))

        def reorder_w2(engine, order, a, b, into):
            w2_w[a, b] = into
            engine(
                out=into.bitcast(U16).rearrange("p (t m) -> p %s" % order, t=PACK),
                in_=w2_raw[a][:].bitcast(U16)[:, b * K_PASS : (b + 1) * K_PASS].rearrange("p (m t) -> p %s" % order, t=PACK),
            )

        load_w2(0)

        def first_passes(b, order):
            for t in range(PACK):
                for a in order:
                    for half in range(2):
                        if a == order[0]:
                            banks[b, t, half] = psum.tile([P, BANK], F32, name="bank%d" % (2 * t + half))
                        cols = slice(half * BANK, (half + 1) * BANK)
                        nc.tensor.matmul_mx(
                            out=banks[b, t, half][:],
                            lhsT=w_codes[b, a][:, t * P : (t + 1) * P].bitcast(FP8X4),
                            lhsT_scale=w_sc[b, a][:, t * P : (t + 1) * P],
                            rhs=v_words[a][:, cols].bitcast(FP8X4),
                            rhs_scale=v_sc[a][4 * a :, cols],
                            start=(a == order[0]),
                            stop=(a == order[-1]),
                        )

        def pick1(b, t, into=None, window=None):
            if window is None:
                window = keep.tile([P, S], F32, name="h%d%d" % (b, t), align_bytes=64)[:]
            h[b, t] = window[:, :S]
            for half in range(2):
                cols = slice(half * BANK, (half + 1) * BANK)
                if (b, t, half) == (0, 0, 0):
                    nc.vector.tensor_copy(out=h[b, t][:, cols], in_=banks[b, t, half][:])
                else:
                    nc.scalar.copy(out=h[b, t][:, cols], in_=banks[b, t, half][:])
            x[b, t] = into if into is not None else keep.tile([P, M], F32, name="x%d%d" % (b, t), align_bytes=64)[:]
            nc.vector.tensor_copy(out=x[b, t], in_=window.indirect(pos1_t[:]))

        def pick2(group, tiles):
            for i, (b, t) in enumerate(tiles):
                picked[b, t] = group[:, i * M : (i + 1) * M]
                nc.vector.tensor_copy(out=picked[b, t], in_=h[b, t].indirect(pos2_t[:]))

        def silu(b, tag):
            s = keep.tile([P, PACK, M], F32, name="silu%d" % b, tag=tag, align_bytes=64)
            for t in range(PACK):
                nc.scalar.activation(out=s[:, t, :], in_=x[b, t], func=ACT.Silu)
            return s

        def planar(tile, cols, run):
            return tile[:, :, cols].rearrange("p t (c i) -> p c t i", i=run)

        def woven(tile, cols, run):
            return tile[:, cols, :].rearrange("p (c i) t -> p c t i", i=run)

        def quantise_z(b, z, scales, step=M):
            z_codes[b] = keep.tile([P, M], U32, name="z_codes%d" % b, align_bytes=64)
            z_sc[b] = scales
            for c in range(0, M, step):
                nc.vector.quantize_mx(out=z_codes[b][:, c : c + step].bitcast(FP8X4), scales=z_sc[b][:, c : c + step], in_=z[:, PACK * c : PACK * (c + step)])

        halves = [slice(u * HALF, (u + 1) * HALF) for u in range(2)]
        pieces = [slice(0, PIECE), slice(PIECE, HALF), slice(HALF + GPSIMD_COLUMNS, M)]

        for a in range(PASSES1):
            nc.vector.tensor_copy(out=v_words[a][:], in_=tab[a][:].indirect(offs_t[:]))
            quantise_first(a)
        nc.vector.tensor_copy(out=w2_rows[:].rearrange("p a (b t m) -> p (a b) m t", t=PACK, m=P), in_=w2_sc_raw[:].rearrange("p a (b m t) -> p (a b) m t", t=PACK, m=P))
        first_passes(0, (0, 1, 2))
        for b in range(PASSES2):
            reorder_w2(nc.vector.tensor_copy, "m t", 0, b, keep.tile([P, H], U8, name="w2_w0%d" % b, align_bytes=64)[:])
        nc.sync.dma_start(pos1_t[:], pos1)
        load_w1(1, 0)
        nc.sync.dma_start(pos2_t[:], pos2)
        load_w1(1, 1)
        load_w1(1, 2, PACK * GPSIMD_SHARE)
        load_w2(1)
        nc.sync.dma_start(out=gain_t[:], in_=gain.rearrange("(b p t) -> p b t", p=P, t=PACK))
        for q in range(4):
            nc.sync.dma_start(out=w2_sc[32 * q : 32 * q + 4, :, :].bitcast(I32), in_=w2_rows[1 + 32 * q : 32 * q + 32 : 8, :, :].bitcast(I32))

        with nc.allow_non_contiguous_dma(reason="row t holds the gains of channels 4 p + t"):
            nc.sync.dma_start(out=gain_rows[:PACK, :], in_=gain[K_PASS:].rearrange("(p t) -> t p", t=PACK))

        for t in range(PACK - 1):
            pick1(0, t)
        r10 = at("r10", PACK * K_PASS, BF16)
        gpsimd_round(woven_w1(r10, PACK), planar_w1(raw[1, 0][0]))
        r11 = at("r11", PACK * K_PASS, BF16)
        gpsimd_round(woven_w1(r11, PACK)[:, :GPSIMD_EARLY_SHARE], planar_w1(raw[1, 1][0])[:, :GPSIMD_EARLY_SHARE])
        w_sc[1, 0] = keep.tile([P, K_PASS], U8, name="w_sc10", align_bytes=64)
        quantise(1, 0, r10, 0, K_PASS, K_PASS)
        pick1(0, 3, at("x03", M, F32))
        pick2(at("picked_a", M, F32), [(0, 0)])
        nc.scalar.copy(out=woven_w1(r11, PACK)[:, GPSIMD_EARLY_SHARE:], in_=planar_w1(raw[1, 1][0])[:, GPSIMD_EARLY_SHARE:])
        r12 = at("r12", PACK * K_PASS, BF16)
        gpsimd_round(woven_w1(r12, PACK)[:, :GPSIMD_SHARE], planar_w1(raw[1, 2][0]))
        nc.scalar.copy(out=woven_w1(r12, PACK)[:, GPSIMD_SHARE:], in_=planar_w1(raw[1, 2][1]))
        w_sc[1, 1] = at("w_sc11", K_PASS, U8)
        w_sc[1, 2] = keep.tile([P, K_PASS], U8, name="w_sc12", align_bytes=64)
        for c0 in (0, 2 * P):
            quantise(1, 1, r11[:, PACK * c0 :], c0, 2 * P, 2 * P)
            quantise(1, 2, r12[:, PACK * c0 :], c0, 2 * P, 2 * P)
        pick2(at("picked_b", 2 * M, F32), [(0, 1), (0, 2)])
        first_passes(1, (0, 1, 2))

        def product(engine, dst, src, other):
            engine.tensor_tensor(out=dst, in0=src, in1=other, op=ALU.mult)

        def gained(dst, src, b, t):
            nc.gpsimd.tensor_scalar(out=dst, in0=src, scalar1=gain_t[:, b, t : t + 1], scalar2=0.0, op0=ALU.mult, op1=ALU.add)

        silu0 = at("silu0", PACK * M, F32).rearrange("p (t m) -> p t m", t=PACK)
        gained0 = keep.tile([P, PACK, M], F32, name="gained0", align_bytes=64)
        for t in range(PACK):
            nc.scalar.activation(out=silu0[:, t, :], in_=x[0, t], func=ACT.Silu)
            gained(gained0[:, t, :], silu0[:, t, :], 0, t)
        z0 = at("z0", PACK * M, BF16)
        z0_w = z0.rearrange("p (m t) -> p m t", t=PACK)
        for cols in halves:
            product(nc.gpsimd, woven(z0_w, cols, 2), planar(gained0, cols, 2), planar(silu0, cols, 2))
        pairs = [at("x1a", 2 * M, F32), at("x1b", 2 * M, F32)]
        for t in range(PACK):
            pick1(1, t, pairs[t // 2][:, (t % 2) * M : (t % 2 + 1) * M])

        silu1 = silu(1, "w_codes12")
        quantise_z(0, z0, at("z_sc0", M, U8))
        pick2(at("picked_c", M, F32), [(0, 3)])
        gain_bank = psum.tile([P, P], F32, name="bank7")
        nc.tensor.transpose(gain_bank[:], gain_rows[:], identity[:])
        first = slice(HALF, HALF + GPSIMD_COLUMNS)
        gained1 = keep.tile([P, PACK, GPSIMD_COLUMNS], F32, name="gained1", align_bytes=64)
        for t in range(PACK):
            gained(gained1[:, t, :], silu1[:, t, first], 1, t)
        z1 = at("z1", PACK * M, BF16)
        z1_w = z1.rearrange("p (m t) -> p m t", t=PACK)
        squares1 = keep.tile([P, M, PACK], F32, name="squares1", tag="tab1", align_bytes=64)
        product(nc.gpsimd, woven(z1_w, first, 2), planar(gained1, slice(0, GPSIMD_COLUMNS), 2), planar(silu1, first, 2))
        for cols in pieces:
            nc.scalar.activation(out=woven(squares1, cols, 2), in_=planar(silu1, cols, 2), func=ACT.Square)
            product(nc.vector, z1_w[:, cols, :], squares1[:, cols, :], gain_bank[:, :PACK].unsqueeze(1).to_broadcast([P, PIECE, PACK]))
        w2_last = at("w2_last", PASSES2 * H, U8).rearrange("p (b n) -> p b n", b=PASSES2)
        for b in range(PASSES2):
            reorder_w2(nc.scalar.copy, "m t", 1, b, w2_last[:, b, :])
        quantise_z(1, z1, keep.tile([P, M], U8, name="z_sc1", align_bytes=64), HALF)
        pick2(keep.tile([P, M], F32, name="picked_last", tag="tab1", align_bytes=64), [(1, 0)])

        results = keep.tile([P, PASSES2 * PACK, M], F32, name="results", tag="tab0", align_bytes=64)
        out_rows = out.rearrange("(b p t) m -> b t p m", p=P, t=PACK)
        early = list(picked)
        by_gpsimd, by_vector = early[:1], early[1:]
        fused = [(1, t) for t in range(PACK) if (1, t) not in picked]

        def second_pass(b, t, a, first):
            if first:
                y[b, t] = psum.tile([P, BANK], F32, name="bank%d" % (PACK * b + t))
            c0 = b * K_PASS + t * P
            nc.tensor.matmul_mx(
                out=y[b, t][:],
                lhsT=w2_w[a, b][:, 2 * t * P : 2 * (t + 1) * P].bitcast(FP4X4),
                lhsT_scale=w2_sc[:, a, c0 : c0 + P],
                rhs=z_codes[a][:].bitcast(FP8X4),
                rhs_scale=z_sc[a][:],
                start=first,
                stop=not first,
            )

        ahead = [by_vector[0]] + by_gpsimd + by_vector[1:] + fused[:1]
        for a in range(PASSES2):
            for b, t in ahead:
                second_pass(b, t, a, a == 0)
        for b, t in fused[1:]:
            for a in (1, 0):
                second_pass(b, t, a, a == 1)
        factors = keep.tile([P, len(by_gpsimd + fused), M], F32, name="factors", tag="tab2", align_bytes=64)
        factor = {}
        for i, (b, t) in enumerate(by_gpsimd + fused):
            factor[b, t] = factors[:, i, :]
            nc.scalar.activation(out=factor[b, t], in_=y[b, t][:], func=ACT.Identity, bias=1.0)
        for b, t in by_gpsimd:
            result = results[:, PACK * b + t, :]
            nc.gpsimd.tensor_tensor(out=result, in0=picked[b, t], in1=factor[b, t], op=ALU.mult)
            nc.scalar.dma_start(out=out_rows[b, t], in_=result)
        for b, t in by_vector:
            result = results[:, PACK * b + t, :]
            nc.vector.scalar_tensor_tensor(out=result, in0=y[b, t][:], scalar=1.0, in1=picked[b, t], op0=ALU.add, op1=ALU.mult)
            nc.sync.dma_start(out=out_rows[b, t], in_=result)
        for b, t in fused:
            result = results[:, PACK * b + t, :]
            for cols in halves if (b, t) == fused[-1] else [slice(0, M)]:
                nc.vector.tensor_tensor(out=result[:, cols], in0=h[b, t].indirect(pos2_t[:, cols.start // 16 : cols.stop // 16]), in1=factor[b, t][:, cols], op=ALU.mult)
                nc.sync.dma_start(out=out_rows[b, t][:, cols], in_=result[:, cols])
